import numpy as np
import ml_dtypes


def mxq(x, axis, fmt="e4m3"):
    dtype, down = {"e4m3": (ml_dtypes.float8_e4m3fn, 7), "e5m2": (ml_dtypes.float8_e5m2, 14)}[fmt]
    v = np.moveaxis(np.asarray(x, np.float32).astype(ml_dtypes.bfloat16).astype(np.float64), axis, -1)
    blocks = v.reshape(v.shape[:-1] + (-1, 32))
    amax = np.abs(blocks).max(-1, keepdims=True)
    byte = np.maximum(np.where(amax > 0, np.frexp(amax)[1] - 1 + 127, 0) - down, 1)
    scale = np.exp2(byte - 127.0)
    codes = (blocks / scale).astype(np.float32).astype(dtype).astype(np.float64)
    return np.moveaxis((codes * scale).reshape(v.shape), -1, axis)


WIDE = False


def mx_kscale(k):
    if not WIDE:
        return np.ones(k)
    levels = np.array([10, -10, 5, -5, 0])
    if k % 512:
        return np.exp2(np.random.permutation(np.resize(levels, k // 32))).repeat(32)
    a = np.empty((k // 512, 16))
    for p in range(k // 512):
        a[p, :8] = np.random.permutation(np.resize(levels, 8))
        for g in range(8):
            far = levels[np.abs(levels - a[p, g]) >= 10]
            a[p, g + 8] = far[np.random.randint(len(far))]
    return np.exp2(a.ravel()).repeat(32)


BF16 = ml_dtypes.bfloat16


def bf(x):
    return np.asarray(x, np.float32).astype(BF16)


def f64(x):
    return np.asarray(x).astype(np.float64)


E2M1 = np.array([0.0, 0.5, 1.0, 1.5, 2.0, 3.0, 4.0, 6.0, -0.0, -0.5, -1.0, -1.5, -2.0, -3.0, -4.0, -6.0])


def pack_weight(w, fmt):
    k, n = w.shape
    w = f64(bf(w)).reshape(k // 32, 32, n)
    amax = np.abs(w).max(1)
    if fmt == "e4m3":
        byte = np.frexp(amax)[1] - 1 + 127 - 7
    else:
        mant, ex = np.frexp(amax / 6.0)
        byte = np.where(mant > 0.5, ex, ex - 1) + 127
    byte = np.clip(np.where(amax > 0, byte, 1), 1, 254)
    scaled = (w * np.exp2(127.0 - byte)[:, None, :]).reshape(k, n).astype(np.float32)
    by_word = np.ascontiguousarray(scaled.reshape(k // 512, 128, 4, n).transpose(0, 1, 3, 2))
    if fmt == "e4m3":
        words = by_word.astype(ml_dtypes.float8_e4m3fn).view(np.uint8)
    else:
        c = by_word.astype(ml_dtypes.float4_e2m1fn).view(np.uint8) & 0xF
        words = c[..., 0::2] | (c[..., 1::2] << 4)
    return np.ascontiguousarray(words), np.ascontiguousarray(byte.astype(np.uint8).reshape(k // 512, 16, n))


def unpack_weight(words, scales, fmt):
    g, p, n, _ = words.shape
    if fmt == "e4m3":
        vals = np.ascontiguousarray(words).view(ml_dtypes.float8_e4m3fn).astype(np.float64)
    else:
        nib = np.empty((g, p, n, 4), np.uint8)
        nib[..., 0::2] = words & 0xF
        nib[..., 1::2] = words >> 4
        vals = E2M1[nib]
    vals = vals * np.repeat(np.exp2(scales.astype(np.float64) - 127.0), 8, axis=1)[..., None]
    return vals.transpose(0, 1, 3, 2).reshape(g * 512, n)
def pack4(w):
    words, scales = pack_weight(w, "e2m1")
    return words.reshape(words.shape[0], 128, -1), scales


def unpack4(words, scales):
    return unpack_weight(words.reshape(words.shape[0], 128, -1, 2), scales, "e2m1")


def planes(Y):
    n, m = Y.shape
    b = f64(bf(Y)).reshape(n // 32, 32, m)
    amax = np.abs(b).max(1)
    byte = np.clip(np.where(amax > 0, np.frexp(amax)[1] - 1 + 127 - 7, 1), 1, 254)
    codes = (b * np.exp2(127.0 - byte)[:, None, :]).reshape(n, m).astype(np.float32).astype(ml_dtypes.float8_e4m3fn).view(np.uint8)
    words = codes.reshape(n // 512, 128, 4, m).transpose(0, 1, 3, 2)
    return np.ascontiguousarray(words), np.ascontiguousarray(byte.astype(np.uint8).reshape(n // 512, 16, m))


N, D, A = 2048, 1024, 512


def softmax_rows(z):
    q = np.exp(z - z.max(axis=-1, keepdims=True))
    return q / q.sum(axis=-1, keepdims=True)


def softmax_fisher_apply(p, u):
    ubar = np.sum(p * u, axis=-1, keepdims=True)
    return p, u - ubar


def setup_inputs():
    s = mx_kscale(D)
    t = mx_kscale(N)
    h = bf(np.random.standard_normal((N, D)))
    g = bf((1.0 + 0.1 * np.random.standard_normal(D)) * s)
    w_words, w_scales = pack4(1.5 * np.random.standard_normal((D, A)) / np.sqrt(D) / s[:, None])
    return {"h": h,
            "g": g,
            "w_words": w_words,
            "w_scales": w_scales,
            "v": bf(np.random.standard_normal((D, A)) / np.sqrt(D) / s[:, None]),
            "e": bf(np.random.uniform(0.5, 1.5, N) * t),
            "rho": bf(np.random.uniform(0.5, 1.5, N) / t),
            "lam": bf(np.random.uniform(5.0, 15.0, D) * s)}


def core(h, g, w_words, w_scales, v, e, rho, lam):
    h, g, v, e, rho, lam = f64(h), f64(g), f64(v), f64(e), f64(rho), f64(lam)
    w = unpack4(w_words, w_scales)
    n_samples = h.shape[0]
    n_actions = w.shape[1]

    f = mxq(h * g[None, :], 1, "e4m3")
    p = softmax_rows(f @ w)
    u = f @ mxq(v, 0, "e4m3")
    p, centered = softmax_fisher_apply(p, u)
    y = float(n_actions) * p * centered * rho[:, None]
    scale = 1.0 / np.sqrt(n_samples)
    k = scale * (mxq(h * e[:, None], 0, "e4m3").T @ mxq(y, 0, "e4m3"))
    return k + lam[:, None] * v


def reference(h, g, w_words, w_scales, v, e, rho, lam):
    R_out = core(h, g, w_words, w_scales, v, e, rho, lam)
    words, scales = planes(R_out)
    return R_out, words, scales

@@ -1,0 +1,419 @@
+import math
+from contextlib import ExitStack
+
+import concourse.mybir as mybir
+from concourse.masks import make_identity
+
+N, D, A = 2048, 1024, 512
+FLOPS = 3 * 2 * N * D * A
+
+F32 = mybir.dt.float32
+BF16 = mybir.dt.bfloat16
+I32 = mybir.dt.int32
+U32 = mybir.dt.uint32
+U8 = mybir.dt.uint8
+FP8X4 = mybir.dt.float8_e4m3fn_x4
+FP4X4 = mybir.dt.float4_e2m1fn_x4
+ALU = mybir.AluOpType
+ACT = mybir.ActivationFunctionType
+
+P = 128
+PACK = 4
+K_PASS = P * PACK
+GROUPS = N // K_PASS
+HALVES = D // K_PASS
+TILES = GROUPS * PACK
+
+
+def tile_dampedsoftmaxfisherproduct_kernel(tc, h, g, w_words, w_scales, v, e, rho, lam, out_0, out_1, out_2):
+    nc = tc.nc
+    with ExitStack() as ctx:
+        sb = ctx.enter_context(tc.tile_pool(name="sb", bufs=1))
+        ps = ctx.enter_context(tc.psum_pool(name="ps", bufs=1))
+
+        def tile(name, shape, dtype):
+            return sb.tile(shape, dtype, name=name, align_bytes=64)
+
+        banks = [ps.tile([P, 512], F32, name="bank%d" % b) for b in range(8)]
+        ring = banks[0:4]
+        z_banks = banks[4:6]
+        u_banks = banks[6:8]
+        k_banks = banks
+
+        ident = tile("ident", [P, P], F32)
+        warm = tile("warm", [P, 1], F32)
+        g_sb = tile("g_sb", [P, HALVES, PACK], BF16)
+        lam_sb = tile("lam_sb", [P, HALVES, PACK], BF16)
+        e_sb = tile("e_sb", [P, GROUPS, PACK], BF16)
+        rho_sb = tile("rho_sb", [P, GROUPS, PACK], BF16)
+        lam32 = tile("lam32", [P, HALVES * PACK], F32)
+        rho_neg = tile("rho_neg", [P, TILES], F32)
+        diag = tile("diag", [P, TILES, P], BF16)
+        h_sb = [tile("h%d" % G, [P, PACK, D], BF16) for G in range(GROUPS)]
+        v_sb = tile("v_sb", [P, HALVES, PACK, A], BF16)
+        w_codes = tile("w_codes", [P, HALVES, 2 * A], U8)
+        w_plane = tile("w_plane", [P, HALVES, A], U8)
+        v_codes = tile("v_codes", [P, HALVES, A], U32)
+        v_plane = tile("v_plane", [P, HALVES, A], U8)
+        f_bf = [tile("f_bf%d" % b, [P, HALVES, 2 * P, PACK], BF16) for b in range(2)]
+        f_codes = tile("f_codes", [P, TILES // 2, HALVES, 2 * P], U32)
+        f_plane = tile("f_plane", [P, TILES // 2, HALVES, 2 * P], U8)
+        he_bf = [tile("he_bf%d" % b, [P, PACK, P, PACK], BF16) for b in range(3)]
+        he_codes = tile("he_codes", [P, GROUPS, HALVES, K_PASS], U32)
+        he_plane = tile("he_plane", [P, GROUPS, HALVES, K_PASS], U8)
+        ex = [tile("ex%d" % b, [P, PACK, A], F32) for b in range(2)]
+        eu = [tile("eu%d" % b, [P, PACK, A], F32) for b in range(2)]
+        y_bf = [tile("y_bf%d" % b, [P, A, PACK], BF16) for b in range(2)]
+        y_rows = tile("y_rows", [P, PACK, A], BF16)
+        y_codes = tile("y_codes", [P, GROUPS, A], U32)
+        y_plane = tile("y_plane", [P, GROUPS, A], U8)
+        res = tile("res", [P, HALVES, PACK, A], F32)
+        wide_bf = [tile("wide_bf%d" % b, [P, A, PACK], BF16) for b in range(2)]
+        o_codes = tile("o_codes", [P, HALVES, A], U32)
+        o_plane = tile("o_plane", [P, HALVES, A], U8)
+        neg_max = tile("neg_max", [P, TILES], F32)
+        total = tile("total", [P, TILES], F32)
+        inv = tile("inv", [P, TILES], F32)
+        coef = tile("coef", [P, TILES], F32)
+        acc = tile("acc", [P, TILES], F32)
+        shift = tile("shift", [P, TILES], F32)
+
+        def col(t, i):
+            return t[:, i : i + 1]
+
+        def flat(ap):
+            return ap.rearrange("p a t -> p (a t)")
+
+        held = {}
+
+        def take_bank(key):
+            if key[0] == "D":
+                held[key] = ring[key[2] % 2]
+            else:
+                held[key] = ring[(0 if key[1] == 0 else 2) + key[2]]
+            return held[key]
+
+        def load_h(G, t0, t1):
+            rows = h[G * K_PASS : (G + 1) * K_PASS, :].rearrange("(p t) d -> p t d", t=PACK)
+            nc.sync.dma_start(out=h_sb[G][:, t0:t1, :], in_=rows[:, t0:t1, :])
+
+        def load_v(gh):
+            rows = v[gh * K_PASS : (gh + 1) * K_PASS, :].rearrange("(p t) a -> p t a", t=PACK)
+            nc.sync.dma_start(out=v_sb[:, gh, :, :], in_=rows)
+
+        def load_vec(dst, src):
+            nc.scalar.dma_start(out=dst[:], in_=src.rearrange("(c p t) -> p c t", p=P, t=PACK))
+
+        def T(pair, gh):
+            G, tp = divmod(pair, 2)
+            bank = take_bank(("T", pair, gh))
+            for u in range(2):
+                for tt in range(2):
+                    words = h_sb[G][:, 2 * tp + tt, :].bitcast(F32)
+                    c0 = (2 * u + tt) * P
+                    nc.tensor.transpose(bank[:, c0 : c0 + P], words[:, 256 * gh + u : 256 * (gh + 1) : 2], ident[:])
+
+        def F(pair, gh):
+            bank = held[("T", pair, gh)]
+            nc.vector.tensor_tensor(
+                out=f_bf[pair % 2][:, gh, :, :].rearrange("p r (u e) -> p r u e", u=2),
+                in0=bank[:].bitcast(BF16).rearrange("p (u r e) -> p r u e", u=2, e=2),
+                in1=g_sb[:, gh : gh + 1, :].rearrange("p o (u e) -> p o u e", u=2).to_broadcast([P, 2 * P, 2, 2]),
+                op=ALU.mult,
+            )
+
+        def QF(pair):
+            nc.vector.quantize_mx(
+                out=f_codes[:, pair, :, :].rearrange("p g r -> p (g r)").bitcast(FP8X4),
+                scales=f_plane[:, pair, :, :].rearrange("p g r -> p (g r)"),
+                in_=f_bf[pair % 2][:].rearrange("p g r t -> p (g r t)"),
+            )
+
+        def stage1(i, bank, codes, plane):
+            pair, tt = divmod(i, 2)
+            for gh in range(HALVES):
+                nc.tensor.matmul_mx(
+                    out=bank[:],
+                    lhsT=f_codes[:, pair, gh, tt * P : (tt + 1) * P].bitcast(FP8X4),
+                    lhsT_scale=f_plane[:, pair, gh, tt * P : (tt + 1) * P],
+                    rhs=codes(gh),
+                    rhs_scale=plane[:, gh, :],
+                    start=(gh == 0),
+                    stop=(gh == HALVES - 1),
+                )
+
+        def Z(i):
+            stage1(i, z_banks[i % 2], lambda gh: w_codes[:, gh, :].bitcast(FP4X4), w_plane)
+
+        def U(i):
+            stage1(i, u_banks[i % 2], lambda gh: v_codes[:, gh, :].bitcast(FP8X4), v_plane)
+
+        def DG(G, j):
+            bank = take_bank(("D", G, j))
+            for t in range(PACK):
+                nc.tensor.matmul(
+                    out=bank[:, t * P : (t + 1) * P],
+                    lhsT=diag[:, PACK * G + t, :],
+                    rhs=h_sb[G][:, t, j * P : (j + 1) * P],
+                    start=True,
+                    stop=True,
+                )
+
+        def HE(G, j):
+            gh, jj = divmod(j, PACK)
+            bank = held[("D", G, j)]
+            nc.scalar.copy(
+                out=he_bf[(2 * G + gh) % 3][:, :, 32 * jj : 32 * (jj + 1), :],
+                in_=bank[:].rearrange("p (t m s) -> p s m t", t=PACK, s=PACK),
+            )
+
+        def QH(G, gh):
+            nc.vector.quantize_mx(
+                out=he_codes[:, G, gh, :].bitcast(FP8X4),
+                scales=he_plane[:, G, gh, :],
+                in_=he_bf[(2 * G + gh) % 3][:].rearrange("p s m t -> p (s m t)"),
+            )
+
+        def VI(gh):
+            nc.scalar.copy(out=wide_bf[gh][:], in_=v_sb[:, gh, :, :].rearrange("p t a -> p a t"))
+
+        def QV(gh):
+            nc.vector.quantize_mx(out=v_codes[:, gh, :].bitcast(FP8X4), scales=v_plane[:, gh, :], in_=flat(wide_bf[gh][:]))
+
+        def LV(c):
+            gh, s = divmod(c, PACK)
+            nc.gpsimd.tensor_scalar(out=res[:, gh, s, :], in0=v_sb[:, gh, s, :], scalar1=col(lam32, c), scalar2=0.0, op0=ALU.mult, op1=ALU.add)
+
+        def MAX(i):
+            nc.vector.tensor_reduce(out=col(neg_max, i), in_=z_banks[i % 2][:], axis=mybir.AxisListType.X, op=ALU.max, negate=True)
+
+        def row(tiles, i):
+            return tiles[(i // PACK) % 2][:, i % PACK, :]
+
+        def EXP(i):
+            nc.scalar.activation(out=row(ex, i), in_=z_banks[i % 2][:], func=ACT.Exp, bias=col(neg_max, i), accum_out=col(total, i))
+
+        def R(i):
+            nc.vector.reciprocal(out=col(inv, i), in_=col(total, i))
+
+        def small_mul(out, a, b):
+            nc.scalar.activation(out=out, in_=a, func=ACT.Copy, scale=b)
+
+        def C(i):
+            small_mul(col(coef, i), col(inv, i), col(rho_neg, i))
+
+        def W(i):
+            nc.vector.scalar_tensor_tensor(
+                out=row(eu, i), in0=u_banks[i % 2][:], scalar=col(coef, i), in1=row(ex, i),
+                op0=ALU.mult, op1=ALU.mult, accum_out=col(acc, i),
+            )
+
+        def B(i):
+            if i < 12:
+                small_mul(col(shift, i), col(acc, i), col(inv, i))
+            else:
+                nc.vector.tensor_scalar(out=col(shift, i), in0=col(acc, i), scalar1=col(inv, i), scalar2=None, op0=ALU.mult)
+
+        def E2(i):
+            nc.scalar.activation(out=row(ex, i), in_=row(ex, i), func=ACT.Copy, scale=col(shift, i))
+
+        def FIN(G, eng, a0, a1):
+            cols = slice(a0, a1)
+            eng.tensor_tensor(
+                out=y_bf[G % 2][:, cols, :],
+                in0=ex[G % 2][:, :, cols].rearrange("p t a -> p a t"),
+                in1=eu[G % 2][:, :, cols].rearrange("p t a -> p a t"),
+                op=ALU.subtract,
+            )
+
+        def Y(i):
+            nc.vector.scalar_tensor_tensor(
+                out=y_rows[:, i % PACK, :], in0=row(ex, i), scalar=col(shift, i), in1=row(eu, i),
+                op0=ALU.mult, op1=ALU.subtract,
+            )
+
+        def interleave(dst, src, split):
+            nc.scalar.copy(out=dst[:, split:, :], in_=src[:, :, split:].rearrange("p t a -> p a t"))
+            nc.vector.tensor_copy(out=dst[:, :split, :], in_=src[:, :, :split].rearrange("p t a -> p a t"))
+
+        def QY(G):
+            nc.vector.quantize_mx(out=y_codes[:, G, :].bitcast(FP8X4), scales=y_plane[:, G, :], in_=flat(y_bf[G % 2][:]))
+
+        def K(c, G):
+            gh, s = divmod(c, PACK)
+            nc.tensor.matmul_mx(
+                out=k_banks[c][:],
+                lhsT=he_codes[:, G, gh, s * P : (s + 1) * P].bitcast(FP8X4),
+                lhsT_scale=he_plane[:, G, gh, s * P : (s + 1) * P],
+                rhs=y_codes[:, G, :].bitcast(FP8X4),
+                rhs_scale=y_plane[:, G, :],
+                start=(G == 0),
+                stop=(G == GROUPS - 1),
+            )
+
+        def EP(c):
+            gh, s = divmod(c, PACK)
+            nc.vector.scalar_tensor_tensor(
+                out=res[:, gh, s, :], in0=k_banks[c][:], scalar=1.0 / math.sqrt(N), in1=res[:, gh, s, :],
+                op0=ALU.mult, op1=ALU.add,
+            )
+            if s % 2 == 1:
+                rows = out_0[gh * K_PASS : (gh + 1) * K_PASS, :].rearrange("(p t) a -> p t a", t=PACK)
+                nc.sync.dma_start(out=rows[:, s - 1 : s + 1, :], in_=res[:, gh, s - 1 : s + 1, :])
+
+        def QO(gh):
+            nc.vector.quantize_mx(out=o_codes[:, gh, :].bitcast(FP8X4), scales=o_plane[:, gh, :], in_=flat(wide_bf[gh][:]))
+            nc.sync.dma_start(out=out_1[gh].rearrange("p m t -> p (m t)").bitcast(I32), in_=o_codes[:, gh, :].bitcast(I32))
+            if gh == HALVES - 1:
+                for Q in range(4):
+                    eng = nc.sync if Q < 2 else nc.scalar
+                    eng.dma_start(
+                        out=out_2[:, 4 * Q : 4 * Q + 4, :].rearrange("g q a -> q g a").bitcast(I32),
+                        in_=o_plane[32 * Q : 32 * Q + 4, :, :].bitcast(I32),
+                    )
+
+        ctx.enter_context(tc.manual_schedule())
+
+        load_vec(g_sb, g)
+        load_vec(e_sb, e)
+        load_h(0, 0, 2)
+        make_identity(nc, ident[:])
+        nc.vector.memset(w_plane[:].rearrange("p g a -> p (g a)").bitcast(U32), 0)
+        nc.vector.memset(warm[:], 0.0)
+        load_v(0)
+        for Q in range(4):
+            nc.scalar.dma_start(
+                out=w_plane[32 * Q : 32 * Q + 4, :, :].bitcast(I32),
+                in_=w_scales[:, 4 * Q : 4 * Q + 4, :].rearrange("g q a -> q g a").bitcast(I32),
+            )
+        nc.scalar.activation(out=warm[:], in_=warm[:], func=ACT.Exp)
+        nc.sync.dma_start(out=w_codes[:].bitcast(I32), in_=w_words.rearrange("g p n -> p g n").bitcast(I32))
+        load_v(1)
+        load_h(0, 2, 4)
+        nc.sync.dma_start(out=rho_sb[:], in_=rho.rearrange("(c p t) -> p c t", p=P, t=PACK))
+        nc.sync.dma_start(out=lam_sb[:], in_=lam.rearrange("(c p t) -> p c t", p=P, t=PACK))
+        for G in range(1, GROUPS):
+            load_h(G, 0, PACK)
+        for i in range(TILES):
+            nc.vector.tensor_scalar(out=diag[:, i, :], in0=ident[:], scalar1=col(e_sb[:].rearrange("p c t -> p (c t)"), i), scalar2=None, op0=ALU.mult)
+
+        T(0, 0)
+        T(0, 1)
+        F(0, 0)
+        F(0, 1)
+        VI(0)
+        QF(0)
+        Z(0)
+        Z(1)
+        T(1, 0)
+        T(1, 1)
+        interleave(wide_bf[1], v_sb[:, 1, :, :], 448)
+        MAX(0)
+        EXP(0)
+        QV(0)
+        QV(1)
+        U(0)
+        DG(0, 0)
+        DG(0, 1)
+        nc.vector.tensor_scalar(out=rho_neg[:], in0=rho_sb[:].rearrange("p c t -> p (c t)"), scalar1=-float(A), scalar2=None, op0=ALU.mult)
+        nc.vector.tensor_copy(out=lam32[:], in_=lam_sb[:].rearrange("p c t -> p (c t)"))
+        F(1, 0)
+        F(1, 1)
+        T(2, 0)
+        T(2, 1)
+        he_jobs = [(G, j) for G in range(GROUPS) for j in range(2 * PACK)]
+        fill = {}
+        for G in range(GROUPS):
+            s0 = PACK * G
+            nxt = 2 * (G + 1)
+            if G + 1 < GROUPS:
+                fill[s0] = ([lambda: QF(1)] if G == 0 else [lambda nxt=nxt: F(nxt, 0)], ([lambda: F(2, 0)] if G == 0 else []) + [lambda nxt=nxt: F(nxt, 1)])
+                fill[s0 + 1] = ([lambda nxt=nxt: F(nxt + 1, 0)], [lambda nxt=nxt: F(nxt + 1, 1)])
+                fill[s0 + 2] = ([lambda nxt=nxt: QF(nxt)], [lambda G=G: QY(G - 1)] if G else [lambda: QH(0, 0)])
+                fill[s0 + 3] = ([lambda nxt=nxt: QF(nxt + 1)], ([lambda G=G: QH(G, 0)] if G else []) + [lambda G=G: QH(G, 1)])
+            else:
+                fill[s0] = ([lambda: FIN(2, nc.vector, 0, 256), lambda: pool_fin(2, 256)], [])
+                fill[s0 + 1] = ([], [lambda: QY(2), lambda: QH(3, 0)])
+                fill[s0 + 2] = ([lambda: Y(12)], [lambda: Y(13), lambda: QH(3, 1)])
+                fill[s0 + 3] = ([lambda: Y(14)], [])
+
+        def pool_fin(G, a0):
+            for a in range(a0, A, 128):
+                FIN(G, nc.gpsimd, a, min(A, a + 128))
+
+        HE(0, 0)
+        DG(0, 2)
+        HE(0, 1)
+        DG(0, 3)
+        he_count = [2,2,2,2, 2,2,2,2, 2,2,2,2, 3,3,0,0]
+        done = 2
+        made = 4
+        for i in range(TILES):
+            G, t = divmod(i, PACK)
+            now = he_jobs[done : done + he_count[i]]
+            done += he_count[i]
+            R(i)
+            if i < 14:
+                C(i)
+            if i + 1 < TILES:
+                MAX(i + 1)
+                EXP(i + 1)
+                U(i + 1)
+            if i >= 14:
+                nc.vector.tensor_scalar(out=col(coef, i), in0=col(inv, i), scalar1=col(rho_neg, i), scalar2=None, op0=ALU.mult)
+            if t == 1 and G + 1 < GROUPS:
+                T(2 * G + 3, 1)
+            for job in fill[i][0]:
+                job()
+            if i == 0:
+                for c in range(8):
+                    LV(c)
+            if i + 2 < TILES:
+                Z(i + 2)
+            W(i)
+            if t == 0 and 0 < G < GROUPS - 1:
+                T(2 * G + 3, 0)
+            if t == 3 and G + 2 < GROUPS:
+                T(2 * G + 4, 0)
+                T(2 * G + 4, 1)
+            for n, job in enumerate(now):
+                if n == len(now) - 1 and i < 12:
+                    B(i)
+                HE(*job)
+                if made < len(he_jobs):
+                    DG(*he_jobs[made])
+                    made += 1
+            for job in fill[i][1]:
+                job()
+            if i == 0:
+                T(3, 0)
+            if i >= 12:
+                B(i)
+            if G + 1 < GROUPS:
+                E2(i)
+                if t == 3 and G < 2:
+                    pool_fin(G, 0)
+            if i == 13:
+                for Gk in range(3):
+                    for c in range(4):
+                        K(c, Gk)
+            if i == 14:
+                for c in (4, 6):
+                    for Gk in range(3):
+                        K(c, Gk)
+        for c in (5, 7):
+            for Gk in range(3):
+                K(c, Gk)
+        Y(15)
+        interleave(y_bf[1], y_rows, 336)
+        QY(3)
+        for c in range(8):
+            K(c, 3)
+        for c in range(4):
+            EP(c)
+        nc.scalar.copy(out=wide_bf[0][:], in_=res[:, 0, :, :].rearrange("p t a -> p a t"))
+        for c in range(4, 8):
+            EP(c)
+        interleave(wide_bf[1], res[:, 1, :, :], 336)
+        QO(0)
+        QO(1)

@@ -61,7 +61,7 @@ def tile_dampedsoftmaxfisherproduct_kernel(tc, h, g, w_words, w_scales, v, e, rh
         he_bf = [tile("he_bf%d" % b, [P, PACK, P, PACK], BF16) for b in range(3)]
         he_codes = tile("he_codes", [P, GROUPS, HALVES, K_PASS], U32)
         he_plane = tile("he_plane", [P, GROUPS, HALVES, K_PASS], U8)
-        ex = [tile("ex%d" % b, [P, PACK, A], F32) for b in range(2)]
+        ex = [tile("ex%d" % b, [P, PACK, A], F32) for b in range(3)]
         eu = [tile("eu%d" % b, [P, PACK, A], F32) for b in range(2)]
         y_bf = [tile("y_bf%d" % b, [P, A, PACK], BF16) for b in range(2)]
         y_rows = tile("y_rows", [P, PACK, A], BF16)
@@ -174,21 +174,18 @@ def tile_dampedsoftmaxfisherproduct_kernel(tc, h, g, w_words, w_scales, v, e, rh
                 in_=he_bf[(2 * G + gh) % 3][:].rearrange("p s m t -> p (s m t)"),
             )
 
-        def VI(gh):
-            nc.scalar.copy(out=wide_bf[gh][:], in_=v_sb[:, gh, :, :].rearrange("p t a -> p a t"))
-
         def QV(gh):
             nc.vector.quantize_mx(out=v_codes[:, gh, :].bitcast(FP8X4), scales=v_plane[:, gh, :], in_=flat(wide_bf[gh][:]))
 
         def LV(c):
             gh, s = divmod(c, PACK)
-            nc.gpsimd.tensor_scalar(out=res[:, gh, s, :], in0=v_sb[:, gh, s, :], scalar1=col(lam32, c), scalar2=0.0, op0=ALU.mult, op1=ALU.add)
+            nc.scalar.activation(out=res[:, gh, s, :], in_=v_sb[:, gh, s, :], func=ACT.Copy, scale=col(lam32, c))
 
         def MAX(i):
             nc.vector.tensor_reduce(out=col(neg_max, i), in_=z_banks[i % 2][:], axis=mybir.AxisListType.X, op=ALU.max, negate=True)
 
         def row(tiles, i):
-            return tiles[(i // PACK) % 2][:, i % PACK, :]
+            return tiles[(i // PACK) % len(tiles)][:, i % PACK, :]
 
         def EXP(i):
             nc.scalar.activation(out=row(ex, i), in_=z_banks[i % 2][:], func=ACT.Exp, bias=col(neg_max, i), accum_out=col(total, i))
@@ -217,12 +214,13 @@ def tile_dampedsoftmaxfisherproduct_kernel(tc, h, g, w_words, w_scales, v, e, rh
         def E2(i):
             nc.scalar.activation(out=row(ex, i), in_=row(ex, i), func=ACT.Copy, scale=col(shift, i))
 
-        def FIN(G, eng, a0, a1):
+        def FIN(G, pool, a0, a1):
             cols = slice(a0, a1)
+            eng = nc.gpsimd if pool else nc.vector
             eng.tensor_tensor(
-                out=y_bf[G % 2][:, cols, :],
-                in0=ex[G % 2][:, :, cols].rearrange("p t a -> p a t"),
-                in1=eu[G % 2][:, :, cols].rearrange("p t a -> p a t"),
+                out=y_bf[G % 2][:, cols, :].rearrange("p (c i) t -> p c t i", i=2),
+                in0=ex[G % 3][:, :, cols].rearrange("p t (c i) -> p c t i", i=2),
+                in1=eu[G % 2][:, :, cols].rearrange("p t (c i) -> p c t i", i=2),
                 op=ALU.subtract,
             )
 
@@ -232,9 +230,31 @@ def tile_dampedsoftmaxfisherproduct_kernel(tc, h, g, w_words, w_scales, v, e, rh
                 op0=ALU.mult, op1=ALU.subtract,
             )
 
-        def interleave(dst, src, split):
-            nc.scalar.copy(out=dst[:, split:, :], in_=src[:, :, split:].rearrange("p t a -> p a t"))
-            nc.vector.tensor_copy(out=dst[:, :split, :], in_=src[:, :, :split].rearrange("p t a -> p a t"))
+        def il(eng, dst, src, a0, a1, run):
+            out = dst[:, a0:a1, :].rearrange("p (c i) t -> p c t i", i=run)
+            in_ = src[:, :, a0:a1].rearrange("p t (c i) -> p c t i", i=run)
+            if eng == "A":
+                nc.scalar.copy(out=out, in_=in_)
+            else:
+                nc.vector.tensor_copy(out=out, in_=in_)
+
+        def VI(gh, vec, a0, a1):
+            il("V" if vec else "A", wide_bf[gh], v_sb[:, gh, :, :], a0, a1, 4)
+
+        def YI(vec, a0, a1):
+            il("V" if vec else "A", y_bf[1], y_rows, a0, a1, 4)
+
+        def OI(gh, vec, a0, a1):
+            il("V" if vec else "A", wide_bf[gh], res[:, gh, :, :], a0, a1, 2)
+
+        def DIAG(i):
+            nc.vector.tensor_scalar(out=diag[:, i, :], in0=ident[:], scalar1=col(e_sb[:].rearrange("p c t -> p (c t)"), i), scalar2=None, op0=ALU.mult)
+
+        def RHO():
+            nc.vector.tensor_scalar(out=rho_neg[:], in0=rho_sb[:].rearrange("p c t -> p (c t)"), scalar1=-float(A), scalar2=None, op0=ALU.mult)
+
+        def LAM():
+            nc.vector.tensor_copy(out=lam32[:], in_=lam_sb[:].rearrange("p c t -> p (c t)"))
 
         def QY(G):
             nc.vector.quantize_mx(out=y_codes[:, G, :].bitcast(FP8X4), scales=y_plane[:, G, :], in_=flat(y_bf[G % 2][:]))
@@ -294,126 +314,349 @@ def tile_dampedsoftmaxfisherproduct_kernel(tc, h, g, w_words, w_scales, v, e, rh
         nc.sync.dma_start(out=lam_sb[:], in_=lam.rearrange("(c p t) -> p c t", p=P, t=PACK))
         for G in range(1, GROUPS):
             load_h(G, 0, PACK)
-        for i in range(TILES):
-            nc.vector.tensor_scalar(out=diag[:, i, :], in0=ident[:], scalar1=col(e_sb[:].rearrange("p c t -> p (c t)"), i), scalar2=None, op0=ALU.mult)
 
+        DIAG(3)
+        DIAG(4)
+        DIAG(1)
         T(0, 0)
-        T(0, 1)
+        DIAG(2)
+        DIAG(10)
         F(0, 0)
+        T(0, 1)
         F(0, 1)
-        VI(0)
+        VI(0, 0, 0, 256)
+        DIAG(13)
         QF(0)
         Z(0)
+        VI(0, 0, 256, 512)
+        DIAG(7)
+        VI(1, 0, 0, 256)
+        VI(1, 0, 256, 512)
         Z(1)
-        T(1, 0)
-        T(1, 1)
-        interleave(wide_bf[1], v_sb[:, 1, :, :], 448)
-        MAX(0)
-        EXP(0)
+        DIAG(0)
+        DIAG(9)
         QV(0)
-        QV(1)
-        U(0)
         DG(0, 0)
-        DG(0, 1)
-        nc.vector.tensor_scalar(out=rho_neg[:], in0=rho_sb[:].rearrange("p c t -> p (c t)"), scalar1=-float(A), scalar2=None, op0=ALU.mult)
-        nc.vector.tensor_copy(out=lam32[:], in_=lam_sb[:].rearrange("p c t -> p (c t)"))
-        F(1, 0)
-        F(1, 1)
-        T(2, 0)
-        T(2, 1)
-        he_jobs = [(G, j) for G in range(GROUPS) for j in range(2 * PACK)]
-        fill = {}
-        for G in range(GROUPS):
-            s0 = PACK * G
-            nxt = 2 * (G + 1)
-            if G + 1 < GROUPS:
-                fill[s0] = ([lambda: QF(1)] if G == 0 else [lambda nxt=nxt: F(nxt, 0)], ([lambda: F(2, 0)] if G == 0 else []) + [lambda nxt=nxt: F(nxt, 1)])
-                fill[s0 + 1] = ([lambda nxt=nxt: F(nxt + 1, 0)], [lambda nxt=nxt: F(nxt + 1, 1)])
-                fill[s0 + 2] = ([lambda nxt=nxt: QF(nxt)], [lambda G=G: QY(G - 1)] if G else [lambda: QH(0, 0)])
-                fill[s0 + 3] = ([lambda nxt=nxt: QF(nxt + 1)], ([lambda G=G: QH(G, 0)] if G else []) + [lambda G=G: QH(G, 1)])
-            else:
-                fill[s0] = ([lambda: FIN(2, nc.vector, 0, 256), lambda: pool_fin(2, 256)], [])
-                fill[s0 + 1] = ([], [lambda: QY(2), lambda: QH(3, 0)])
-                fill[s0 + 2] = ([lambda: Y(12)], [lambda: Y(13), lambda: QH(3, 1)])
-                fill[s0 + 3] = ([lambda: Y(14)], [])
-
-        def pool_fin(G, a0):
-            for a in range(a0, A, 128):
-                FIN(G, nc.gpsimd, a, min(A, a + 128))
-
         HE(0, 0)
+        MAX(0)
+        T(1, 0)
+        MAX(1)
+        EXP(1)
+        T(1, 1)
+        RHO()
+        DG(0, 1)
         DG(0, 2)
+        F(1, 0)
+        T(2, 0)
         HE(0, 1)
+        F(1, 1)
+        T(2, 1)
+        QV(1)
+        EXP(0)
         DG(0, 3)
-        he_count = [2,2,2,2, 2,2,2,2, 2,2,2,2, 3,3,0,0]
-        done = 2
-        made = 4
-        for i in range(TILES):
-            G, t = divmod(i, PACK)
-            now = he_jobs[done : done + he_count[i]]
-            done += he_count[i]
-            R(i)
-            if i < 14:
-                C(i)
-            if i + 1 < TILES:
-                MAX(i + 1)
-                EXP(i + 1)
-                U(i + 1)
-            if i >= 14:
-                nc.vector.tensor_scalar(out=col(coef, i), in0=col(inv, i), scalar1=col(rho_neg, i), scalar2=None, op0=ALU.mult)
-            if t == 1 and G + 1 < GROUPS:
-                T(2 * G + 3, 1)
-            for job in fill[i][0]:
-                job()
-            if i == 0:
-                for c in range(8):
-                    LV(c)
-            if i + 2 < TILES:
-                Z(i + 2)
-            W(i)
-            if t == 0 and 0 < G < GROUPS - 1:
-                T(2 * G + 3, 0)
-            if t == 3 and G + 2 < GROUPS:
-                T(2 * G + 4, 0)
-                T(2 * G + 4, 1)
-            for n, job in enumerate(now):
-                if n == len(now) - 1 and i < 12:
-                    B(i)
-                HE(*job)
-                if made < len(he_jobs):
-                    DG(*he_jobs[made])
-                    made += 1
-            for job in fill[i][1]:
-                job()
-            if i == 0:
-                T(3, 0)
-            if i >= 12:
-                B(i)
-            if G + 1 < GROUPS:
-                E2(i)
-                if t == 3 and G < 2:
-                    pool_fin(G, 0)
-            if i == 13:
-                for Gk in range(3):
-                    for c in range(4):
-                        K(c, Gk)
-            if i == 14:
-                for c in (4, 6):
-                    for Gk in range(3):
-                        K(c, Gk)
-        for c in (5, 7):
-            for Gk in range(3):
-                K(c, Gk)
+        R(1)
+        QF(1)
+        DIAG(5)
+        F(2, 0)
+        Z(2)
+        HE(0, 2)
+        F(2, 1)
+        DIAG(8)
+        QF(2)
+        Z(3)
+        MAX(2)
+        MAX(3)
+        T(3, 0)
+        R(0)
+        DIAG(6)
+        EXP(2)
+        F(3, 0)
+        T(3, 1)
+        C(0)
+        U(0)
+        DG(0, 4)
+        Z(4)
+        U(1)
+        R(2)
+        C(1)
+        C(2)
+        T(4, 0)
+        DIAG(15)
+        F(3, 1)
+        HE(0, 3)
+        W(0)
+        HE(0, 4)
+        DG(0, 5)
+        EXP(3)
+        DG(0, 6)
+        HE(0, 5)
+        MAX(4)
+        W(1)
+        U(2)
+        B(0)
+        EXP(4)
+        QF(3)
+        Z(5)
+        F(4, 0)
+        HE(0, 6)
+        DG(0, 7)
+        R(3)
+        W(2)
+        MAX(5)
+        T(4, 1)
+        R(4)
+        Z(6)
+        DG(1, 0)
+        HE(0, 7)
+        QH(0, 0)
+        DG(1, 1)
+        EXP(5)
+        DIAG(11)
+        Z(7)
+        U(3)
+        F(4, 1)
+        QH(0, 1)
+        MAX(6)
+        T(5, 0)
+        HE(1, 0)
+        T(5, 1)
+        C(4)
+        HE(1, 1)
+        B(1)
+        C(3)
+        DG(1, 2)
+        MAX(7)
+        W(3)
+        F(5, 0)
+        EXP(6)
+        EXP(7)
+        F(5, 1)
+        HE(1, 2)
+        DG(1, 3)
+        QF(4)
+        B(3)
+        QF(5)
+        HE(1, 3)
+        U(4)
+        R(7)
+        U(5)
+        E2(1)
+        R(6)
+        R(5)
+        DG(1, 4)
+        W(4)
+        Z(8)
+        DG(1, 5)
+        T(6, 0)
+        HE(1, 4)
+        T(6, 1)
+        QH(1, 0)
+        E2(0)
+        MAX(8)
+        C(5)
+        HE(1, 5)
+        Z(9)
+        W(5)
+        F(6, 0)
+        DIAG(12)
+        C(6)
+        DG(1, 6)
+        F(6, 1)
+        EXP(8)
+        U(7)
+        MAX(9)
+        QF(6)
+        R(8)
+        C(7)
+        Z(10)
+        B(2)
+        MAX(10)
+        E2(2)
+        DG(1, 7)
+        B(4)
+        U(6)
+        HE(1, 6)
+        DG(2, 0)
+        E2(3)
+        HE(1, 7)
+        EXP(9)
+        DG(2, 1)
+        T(7, 1)
+        HE(2, 0)
+        HE(2, 1)
+        EXP(10)
+        B(5)
+        FIN(0, 0, 0, 256)
+        W(7)
+        DG(2, 2)
+        DIAG(14)
+        DG(2, 3)
+        HE(2, 2)
+        C(8)
+        W(6)
+        R(9)
+        LAM()
+        Z(11)
+        E2(4)
+        DG(2, 4)
+        FIN(0, 0, 256, 512)
+        MAX(11)
+        F(7, 1)
+        QH(1, 1)
+        T(7, 0)
+        E2(5)
+        Z(12)
+        HE(2, 3)
+        B(7)
+        DG(2, 5)
+        HE(2, 4)
+        R(10)
+        F(7, 0)
+        MAX(12)
+        EXP(11)
+        HE(2, 5)
+        U(9)
+        DG(2, 6)
+        C(9)
+        E2(7)
+        B(6)
+        U(8)
+        QF(7)
+        R(11)
+        W(9)
+        W(8)
+        EXP(12)
+        HE(2, 6)
+        E2(6)
+        Z(13)
+        MAX(13)
+        QY(0)
+        DG(2, 7)
+        R(12)
+        B(8)
+        HE(2, 7)
+        FIN(1, 0, 256, 512)
+        U(10)
+        DG(3, 0)
+        E2(8)
+        B(9)
+        EXP(13)
+        C(10)
+        U(11)
+        Z(14)
+        HE(3, 0)
+        DG(3, 1)
+        K(2, 0)
+        C(11)
+        FIN(1, 0, 0, 256)
+        C(12)
+        W(11)
+        K(3, 0)
+        LV(5)
+        HE(3, 1)
+        W(10)
+        R(13)
+        E2(9)
+        MAX(14)
+        Z(15)
+        DG(3, 2)
+        B(11)
+        MAX(15)
+        HE(3, 2)
+        DG(3, 3)
+        QY(1)
+        C(13)
+        U(12)
+        E2(11)
+        EXP(14)
+        DG(3, 4)
+        LV(1)
+        B(10)
+        EXP(15)
+        E2(10)
+        QH(2, 1)
+        W(12)
+        LV(3)
+        U(13)
+        R(14)
+        W(13)
+        B(12)
+        HE(3, 3)
+        U(15)
+        QH(2, 0)
+        C(14)
+        LV(2)
+        HE(3, 4)
+        K(4, 0)
+        DG(3, 5)
+        U(14)
+        R(15)
+        K(2, 1)
+        K(4, 1)
+        HE(3, 5)
+        B(13)
+        FIN(2, 0, 256, 512)
+        K(5, 0)
+        C(15)
+        FIN(2, 0, 0, 256)
+        DG(3, 6)
+        DG(3, 7)
+        W(14)
+        W(15)
+        HE(3, 6)
+        K(3, 1)
+        K(0, 0)
+        QY(2)
+        B(14)
+        B(15)
+        Y(13)
+        LV(0)
+        Y(14)
+        HE(3, 7)
+        K(0, 1)
+        K(3, 2)
+        K(4, 2)
+        K(1, 0)
+        K(5, 1)
+        Y(12)
         Y(15)
-        interleave(y_bf[1], y_rows, 336)
+        K(1, 1)
+        K(7, 0)
+        K(5, 2)
+        QH(3, 0)
+        YI(0, 336, 512)
+        YI(1, 0, 336)
+        K(1, 2)
+        K(6, 0)
+        K(0, 2)
+        K(6, 1)
         QY(3)
-        for c in range(8):
-            K(c, 3)
-        for c in range(4):
-            EP(c)
-        nc.scalar.copy(out=wide_bf[0][:], in_=res[:, 0, :, :].rearrange("p t a -> p a t"))
-        for c in range(4, 8):
-            EP(c)
-        interleave(wide_bf[1], res[:, 1, :, :], 336)
+        K(2, 2)
+        QH(3, 1)
+        K(0, 3)
+        EP(0)
+        K(2, 3)
+        EP(2)
+        K(3, 3)
+        K(6, 2)
+        EP(3)
+        K(1, 3)
+        LV(4)
+        EP(1)
+        K(4, 3)
+        LV(6)
+        EP(4)
+        LV(7)
+        K(6, 3)
+        EP(6)
+        K(7, 1)
+        K(5, 3)
+        K(7, 2)
+        K(7, 3)
+        OI(0, 0, 0, 512)
+        EP(7)
+        EP(5)
+        OI(1, 1, 0, 352)
+        OI(1, 0, 352, 512)
         QO(0)
         QO(1)

@@ -55,16 +55,18 @@ def tile_dampedsoftmaxfisherproduct_kernel(tc, h, g, w_words, w_scales, v, e, rh
         w_plane = tile("w_plane", [P, HALVES, A], U8)
         v_codes = tile("v_codes", [P, HALVES, A], U32)
         v_plane = tile("v_plane", [P, HALVES, A], U8)
-        f_bf = [tile("f_bf%d" % b, [P, HALVES, 2 * P, PACK], BF16) for b in range(2)]
-        f_codes = tile("f_codes", [P, TILES // 2, HALVES, 2 * P], U32)
-        f_plane = tile("f_plane", [P, TILES // 2, HALVES, 2 * P], U8)
+        f_bf = [tile("f_bf%d" % b, [P, 2, HALVES, P, PACK], BF16) for b in range(2)]
+        f_codes = tile("f_codes", [P, TILES, HALVES, P], U32)
+        f_plane = tile("f_plane", [P, TILES, HALVES, P], U8)
         he_bf = [tile("he_bf%d" % b, [P, PACK, P, PACK], BF16) for b in range(3)]
         he_codes = tile("he_codes", [P, GROUPS, HALVES, K_PASS], U32)
         he_plane = tile("he_plane", [P, GROUPS, HALVES, K_PASS], U8)
-        ex = [tile("ex%d" % b, [P, PACK, A], F32) for b in range(3)]
+        ex = [tile("ex%d" % b, [P, PACK, A], F32) for b in range(2)]
         eu = [tile("eu%d" % b, [P, PACK, A], F32) for b in range(2)]
         y_bf = [tile("y_bf%d" % b, [P, A, PACK], BF16) for b in range(2)]
-        y_rows = tile("y_rows", [P, PACK, A], BF16)
+        y_rows = [tile("y_rows%d" % b, [P, PACK, A], BF16) for b in range(2)]
+        e32 = tile("e32", [P, TILES], F32)
+        ks = [tile("ks%d" % b, [P, A], F32) for b in range(2)]
         y_codes = tile("y_codes", [P, GROUPS, A], U32)
         y_plane = tile("y_plane", [P, GROUPS, A], U8)
         res = tile("res", [P, HALVES, PACK, A], F32)
@@ -84,58 +86,50 @@ def tile_dampedsoftmaxfisherproduct_kernel(tc, h, g, w_words, w_scales, v, e, rh
         def flat(ap):
             return ap.rearrange("p a t -> p (a t)")
 
-        held = {}
+        def t_bank(i):
+            return ring[(0 if i < 2 else 2) + i % 2]
 
-        def take_bank(key):
-            if key[0] == "D":
-                held[key] = ring[key[2] % 2]
-            else:
-                held[key] = ring[(0 if key[1] == 0 else 2) + key[2]]
-            return held[key]
-
-        def load_h(G, t0, t1):
+        def load_h(G, t0, t1, d0=0, d1=D):
             rows = h[G * K_PASS : (G + 1) * K_PASS, :].rearrange("(p t) d -> p t d", t=PACK)
-            nc.sync.dma_start(out=h_sb[G][:, t0:t1, :], in_=rows[:, t0:t1, :])
+            nc.sync.dma_start(out=h_sb[G][:, t0:t1, d0:d1], in_=rows[:, t0:t1, d0:d1])
 
         def load_v(gh):
             rows = v[gh * K_PASS : (gh + 1) * K_PASS, :].rearrange("(p t) a -> p t a", t=PACK)
             nc.sync.dma_start(out=v_sb[:, gh, :, :], in_=rows)
 
-        def load_vec(dst, src):
-            nc.scalar.dma_start(out=dst[:], in_=src.rearrange("(c p t) -> p c t", p=P, t=PACK))
+        def load_vec(eng, dst, src):
+            eng.dma_start(out=dst[:], in_=src.rearrange("(c p t) -> p c t", p=P, t=PACK))
 
-        def T(pair, gh):
-            G, tp = divmod(pair, 2)
-            bank = take_bank(("T", pair, gh))
+        def T(i):
+            G, t = divmod(i, PACK)
+            bank = t_bank(i)
+            words = h_sb[G][:, t, :].bitcast(F32)
             for u in range(2):
-                for tt in range(2):
-                    words = h_sb[G][:, 2 * tp + tt, :].bitcast(F32)
-                    c0 = (2 * u + tt) * P
+                for gh in range(HALVES):
+                    c0 = (2 * u + gh) * P
                     nc.tensor.transpose(bank[:, c0 : c0 + P], words[:, 256 * gh + u : 256 * (gh + 1) : 2], ident[:])
 
-        def F(pair, gh):
-            bank = held[("T", pair, gh)]
+        def F(i):
             nc.vector.tensor_tensor(
-                out=f_bf[pair % 2][:, gh, :, :].rearrange("p r (u e) -> p r u e", u=2),
-                in0=bank[:].bitcast(BF16).rearrange("p (u r e) -> p r u e", u=2, e=2),
-                in1=g_sb[:, gh : gh + 1, :].rearrange("p o (u e) -> p o u e", u=2).to_broadcast([P, 2 * P, 2, 2]),
+                out=f_bf[(i // 2) % 2][:, i % 2, :, :, :].rearrange("p g r (u e) -> p g r u e", u=2),
+                in0=t_bank(i)[:].bitcast(BF16).rearrange("p (u g r e) -> p g r u e", u=2, g=HALVES, e=2),
+                in1=g_sb[:].rearrange("p g (o u e) -> p g o u e", o=1, u=2).to_broadcast([P, HALVES, P, 2, 2]),
                 op=ALU.mult,
             )
 
-        def QF(pair):
+        def QF(i, n):
             nc.vector.quantize_mx(
-                out=f_codes[:, pair, :, :].rearrange("p g r -> p (g r)").bitcast(FP8X4),
-                scales=f_plane[:, pair, :, :].rearrange("p g r -> p (g r)"),
-                in_=f_bf[pair % 2][:].rearrange("p g r t -> p (g r t)"),
+                out=f_codes[:, i : i + n, :, :].rearrange("p i g r -> p (i g r)").bitcast(FP8X4),
+                scales=f_plane[:, i : i + n, :, :].rearrange("p i g r -> p (i g r)"),
+                in_=f_bf[(i // 2) % 2][:, i % 2 : i % 2 + n, :, :, :].rearrange("p i g r t -> p (i g r t)"),
             )
 
         def stage1(i, bank, codes, plane):
-            pair, tt = divmod(i, 2)
             for gh in range(HALVES):
                 nc.tensor.matmul_mx(
                     out=bank[:],
-                    lhsT=f_codes[:, pair, gh, tt * P : (tt + 1) * P].bitcast(FP8X4),
-                    lhsT_scale=f_plane[:, pair, gh, tt * P : (tt + 1) * P],
+                    lhsT=f_codes[:, i, gh, :].bitcast(FP8X4),
+                    lhsT_scale=f_plane[:, i, gh, :],
                     rhs=codes(gh),
                     rhs_scale=plane[:, gh, :],
                     start=(gh == 0),
@@ -149,7 +143,7 @@ def tile_dampedsoftmaxfisherproduct_kernel(tc, h, g, w_words, w_scales, v, e, rh
             stage1(i, u_banks[i % 2], lambda gh: v_codes[:, gh, :].bitcast(FP8X4), v_plane)
 
         def DG(G, j):
-            bank = take_bank(("D", G, j))
+            bank = ring[j % 2]
             for t in range(PACK):
                 nc.tensor.matmul(
                     out=bank[:, t * P : (t + 1) * P],
@@ -161,7 +155,7 @@ def tile_dampedsoftmaxfisherproduct_kernel(tc, h, g, w_words, w_scales, v, e, rh
 
         def HE(G, j):
             gh, jj = divmod(j, PACK)
-            bank = held[("D", G, j)]
+            bank = ring[j % 2]
             nc.scalar.copy(
                 out=he_bf[(2 * G + gh) % 3][:, :, 32 * jj : 32 * (jj + 1), :],
                 in_=bank[:].rearrange("p (t m s) -> p s m t", t=PACK, s=PACK),
@@ -190,8 +184,8 @@ def tile_dampedsoftmaxfisherproduct_kernel(tc, h, g, w_words, w_scales, v, e, rh
         def EXP(i):
             nc.scalar.activation(out=row(ex, i), in_=z_banks[i % 2][:], func=ACT.Exp, bias=col(neg_max, i), accum_out=col(total, i))
 
-        def R(i):
-            nc.vector.reciprocal(out=col(inv, i), in_=col(total, i))
+        def R(i, n):
+            nc.vector.reciprocal(out=inv[:, i : i + n], in_=total[:, i : i + n])
 
         def small_mul(out, a, b):
             nc.scalar.activation(out=out, in_=a, func=ACT.Copy, scale=b)
@@ -206,7 +200,7 @@ def tile_dampedsoftmaxfisherproduct_kernel(tc, h, g, w_words, w_scales, v, e, rh
             )
 
         def B(i):
-            if i < 12:
+            if i < 15:
                 small_mul(col(shift, i), col(acc, i), col(inv, i))
             else:
                 nc.vector.tensor_scalar(out=col(shift, i), in0=col(acc, i), scalar1=col(inv, i), scalar2=None, op0=ALU.mult)
@@ -226,7 +220,7 @@ def tile_dampedsoftmaxfisherproduct_kernel(tc, h, g, w_words, w_scales, v, e, rh
 
         def Y(i):
             nc.vector.scalar_tensor_tensor(
-                out=y_rows[:, i % PACK, :], in0=row(ex, i), scalar=col(shift, i), in1=row(eu, i),
+                out=row(y_rows, i), in0=row(ex, i), scalar=col(shift, i), in1=row(eu, i),
                 op0=ALU.mult, op1=ALU.subtract,
             )
 
@@ -241,20 +235,23 @@ def tile_dampedsoftmaxfisherproduct_kernel(tc, h, g, w_words, w_scales, v, e, rh
         def VI(gh, vec, a0, a1):
             il("V" if vec else "A", wide_bf[gh], v_sb[:, gh, :, :], a0, a1, 4)
 
-        def YI(vec, a0, a1):
-            il("V" if vec else "A", y_bf[1], y_rows, a0, a1, 4)
+        def YI(G, vec, a0, a1):
+            il("V" if vec else "A", y_bf[G % 2], y_rows[G % 2], a0, a1, 4)
 
         def OI(gh, vec, a0, a1):
             il("V" if vec else "A", wide_bf[gh], res[:, gh, :, :], a0, a1, 2)
 
         def DIAG(i):
-            nc.vector.tensor_scalar(out=diag[:, i, :], in0=ident[:], scalar1=col(e_sb[:].rearrange("p c t -> p (c t)"), i), scalar2=None, op0=ALU.mult)
+            nc.scalar.activation(out=diag[:, i, :], in_=ident[:], func=ACT.Copy, scale=col(e32, i))
+
+        def E32():
+            nc.gpsimd.tensor_copy(out=e32[:], in_=e_sb[:].rearrange("p c t -> p (c t)"))
 
         def RHO():
-            nc.vector.tensor_scalar(out=rho_neg[:], in0=rho_sb[:].rearrange("p c t -> p (c t)"), scalar1=-float(A), scalar2=None, op0=ALU.mult)
+            nc.gpsimd.tensor_scalar(out=rho_neg[:], in0=rho_sb[:].rearrange("p c t -> p (c t)"), scalar1=-float(A), scalar2=0.0, op0=ALU.mult, op1=ALU.add)
 
         def LAM():
-            nc.vector.tensor_copy(out=lam32[:], in_=lam_sb[:].rearrange("p c t -> p (c t)"))
+            nc.gpsimd.tensor_copy(out=lam32[:], in_=lam_sb[:].rearrange("p c t -> p (c t)"))
 
         def QY(G):
             nc.vector.quantize_mx(out=y_codes[:, G, :].bitcast(FP8X4), scales=y_plane[:, G, :], in_=flat(y_bf[G % 2][:]))
@@ -271,15 +268,23 @@ def tile_dampedsoftmaxfisherproduct_kernel(tc, h, g, w_words, w_scales, v, e, rh
                 stop=(G == GROUPS - 1),
             )
 
-        def EP(c):
+        def EP(c, a0, a1):
             gh, s = divmod(c, PACK)
             nc.vector.scalar_tensor_tensor(
-                out=res[:, gh, s, :], in0=k_banks[c][:], scalar=1.0 / math.sqrt(N), in1=res[:, gh, s, :],
+                out=res[:, gh, s, a0:a1], in0=k_banks[c][:, a0:a1], scalar=1.0 / math.sqrt(N), in1=res[:, gh, s, a0:a1],
                 op0=ALU.mult, op1=ALU.add,
             )
-            if s % 2 == 1:
-                rows = out_0[gh * K_PASS : (gh + 1) * K_PASS, :].rearrange("(p t) a -> p t a", t=PACK)
-                nc.sync.dma_start(out=rows[:, s - 1 : s + 1, :], in_=res[:, gh, s - 1 : s + 1, :])
+
+        def EA(c):
+            nc.scalar.activation(out=ks[c % 2][:], in_=k_banks[c][:], func=ACT.Copy, scale=1.0 / math.sqrt(N))
+
+        def EG(c):
+            gh, s = divmod(c, PACK)
+            nc.gpsimd.tensor_tensor(out=res[:, gh, s, :], in0=ks[c % 2][:], in1=res[:, gh, s, :], op=ALU.add)
+
+        def ST(gh, s):
+            rows = out_0[gh * K_PASS : (gh + 1) * K_PASS, :].rearrange("(p t) a -> p t a", t=PACK)
+            nc.sync.dma_start(out=rows[:, s : s + 2, :], in_=res[:, gh, s : s + 2, :])
 
         def QO(gh):
             nc.vector.quantize_mx(out=o_codes[:, gh, :].bitcast(FP8X4), scales=o_plane[:, gh, :], in_=flat(wide_bf[gh][:]))
@@ -294,369 +299,374 @@ def tile_dampedsoftmaxfisherproduct_kernel(tc, h, g, w_words, w_scales, v, e, rh
 
         ctx.enter_context(tc.manual_schedule())
 
-        load_vec(g_sb, g)
-        load_vec(e_sb, e)
-        load_h(0, 0, 2)
+        load_vec(nc.scalar, g_sb, g)
+        load_vec(nc.scalar, e_sb, e)
+        load_h(0, 0, 1)
+        load_h(0, 1, 2)
         make_identity(nc, ident[:])
         nc.vector.memset(w_plane[:].rearrange("p g a -> p (g a)").bitcast(U32), 0)
         nc.vector.memset(warm[:], 0.0)
-        load_v(0)
+        nc.sync.dma_start(out=w_codes[:].bitcast(I32), in_=w_words.rearrange("g p n -> p g n").bitcast(I32))
+        load_h(0, 2, 4)
         for Q in range(4):
-            nc.scalar.dma_start(
+            nc.gpsimd.dma_start(
                 out=w_plane[32 * Q : 32 * Q + 4, :, :].bitcast(I32),
                 in_=w_scales[:, 4 * Q : 4 * Q + 4, :].rearrange("g q a -> q g a").bitcast(I32),
             )
         nc.scalar.activation(out=warm[:], in_=warm[:], func=ACT.Exp)
-        nc.sync.dma_start(out=w_codes[:].bitcast(I32), in_=w_words.rearrange("g p n -> p g n").bitcast(I32))
+        load_v(0)
+        load_h(1, 0, 2)
         load_v(1)
-        load_h(0, 2, 4)
-        nc.sync.dma_start(out=rho_sb[:], in_=rho.rearrange("(c p t) -> p c t", p=P, t=PACK))
-        nc.sync.dma_start(out=lam_sb[:], in_=lam.rearrange("(c p t) -> p c t", p=P, t=PACK))
-        for G in range(1, GROUPS):
-            load_h(G, 0, PACK)
+        load_vec(nc.sync, rho_sb, rho)
+        load_h(1, 2, 4)
+        load_h(2, 0, PACK)
+        load_h(3, 0, PACK)
+        load_vec(nc.sync, lam_sb, lam)
 
-        DIAG(3)
-        DIAG(4)
-        DIAG(1)
-        T(0, 0)
+        E32()
         DIAG(2)
-        DIAG(10)
-        F(0, 0)
-        T(0, 1)
-        F(0, 1)
-        VI(0, 0, 0, 256)
-        DIAG(13)
-        QF(0)
-        Z(0)
-        VI(0, 0, 256, 512)
-        DIAG(7)
-        VI(1, 0, 0, 256)
-        VI(1, 0, 256, 512)
-        Z(1)
+        T(0)
+        T(1)
+        DIAG(3)
         DIAG(0)
-        DIAG(9)
+        T(2)
+        F(0)
+        T(3)
+        F(1)
+        QF(1, 1)
+        LAM()
+        DIAG(1)
+        F(2)
+        F(3)
+        T(4)
+        QF(0, 1)
+        QF(2, 2)
+        Z(1)
+        DIAG(11)
+        Z(0)
+        T(5)
+        VI(0, 0, 0, 512)
+        F(4)
+        T(6)
         QV(0)
-        DG(0, 0)
-        HE(0, 0)
-        MAX(0)
-        T(1, 0)
+        VI(1, 0, 256, 512)
         MAX(1)
-        EXP(1)
-        T(1, 1)
-        RHO()
+        MAX(0)
         DG(0, 1)
-        DG(0, 2)
-        F(1, 0)
-        T(2, 0)
-        HE(0, 1)
-        F(1, 1)
-        T(2, 1)
-        QV(1)
+        DG(0, 0)
+        VI(1, 0, 0, 256)
+        EXP(1)
+        F(5)
         EXP(0)
-        DG(0, 3)
-        R(1)
-        QF(1)
-        DIAG(5)
-        F(2, 0)
-        Z(2)
-        HE(0, 2)
-        F(2, 1)
-        DIAG(8)
-        QF(2)
         Z(3)
-        MAX(2)
-        MAX(3)
-        T(3, 0)
-        R(0)
-        DIAG(6)
-        EXP(2)
-        F(3, 0)
-        T(3, 1)
-        C(0)
-        U(0)
-        DG(0, 4)
-        Z(4)
-        U(1)
-        R(2)
+        Z(2)
+        HE(0, 0)
+        DG(0, 2)
+        QV(1)
+        R(1, 1)
+        T(7)
+        F(6)
+        RHO()
+        DIAG(5)
+        R(0, 1)
         C(1)
-        C(2)
-        T(4, 0)
-        DIAG(15)
-        F(3, 1)
-        HE(0, 3)
-        W(0)
-        HE(0, 4)
-        DG(0, 5)
+        LV(1)
+        C(0)
+        QF(4, 2)
+        U(0)
+        HE(0, 1)
+        HE(0, 2)
+        DIAG(12)
+        U(1)
+        DG(0, 3)
+        MAX(3)
+        DG(0, 4)
+        MAX(2)
+        F(7)
+        EXP(2)
         EXP(3)
+        Z(4)
+        W(0)
+        HE(0, 3)
+        DIAG(8)
+        DIAG(7)
+        Z(5)
+        HE(0, 4)
+        W(1)
+        DIAG(14)
+        DG(0, 5)
+        DIAG(9)
+        DIAG(4)
+        QF(6, 2)
+        T(9)
+        R(2, 2)
+        B(0)
+        T(8)
+        C(2)
+        QH(0, 0)
+        MAX(4)
+        MAX(5)
+        U(2)
+        U(3)
+        Y(0)
         DG(0, 6)
         HE(0, 5)
-        MAX(4)
-        W(1)
-        U(2)
-        B(0)
-        EXP(4)
-        QF(3)
-        Z(5)
-        F(4, 0)
-        HE(0, 6)
+        DIAG(10)
         DG(0, 7)
-        R(3)
-        W(2)
-        MAX(5)
-        T(4, 1)
-        R(4)
-        Z(6)
-        DG(1, 0)
-        HE(0, 7)
-        QH(0, 0)
-        DG(1, 1)
-        EXP(5)
-        DIAG(11)
-        Z(7)
-        U(3)
-        F(4, 1)
-        QH(0, 1)
-        MAX(6)
-        T(5, 0)
-        HE(1, 0)
-        T(5, 1)
-        C(4)
-        HE(1, 1)
         B(1)
+        F(9)
+        EXP(4)
+        F(8)
+        Y(1)
         C(3)
-        DG(1, 2)
-        MAX(7)
+        DIAG(6)
+        EXP(5)
+        LV(6)
+        R(4, 2)
+        HE(0, 6)
+        Z(6)
+        HE(0, 7)
+        QF(8, 2)
+        W(2)
+        Z(7)
+        DG(1, 0)
+        MAX(6)
+        HE(1, 0)
+        DG(1, 1)
+        T(11)
+        C(5)
         W(3)
-        F(5, 0)
+        HE(1, 1)
+        MAX(7)
+        QH(0, 1)
+        T(10)
+        DG(1, 2)
+        F(10)
         EXP(6)
         EXP(7)
-        F(5, 1)
-        HE(1, 2)
-        DG(1, 3)
-        QF(4)
-        B(3)
-        QF(5)
-        HE(1, 3)
-        U(4)
-        R(7)
         U(5)
-        E2(1)
-        R(6)
-        R(5)
-        DG(1, 4)
-        W(4)
+        F(11)
+        DG(1, 3)
         Z(8)
-        DG(1, 5)
-        T(6, 0)
-        HE(1, 4)
-        T(6, 1)
-        QH(1, 0)
-        E2(0)
-        MAX(8)
-        C(5)
-        HE(1, 5)
-        Z(9)
         W(5)
-        F(6, 0)
-        DIAG(12)
-        C(6)
-        DG(1, 6)
-        F(6, 1)
-        EXP(8)
-        U(7)
-        MAX(9)
-        QF(6)
-        R(8)
-        C(7)
-        Z(10)
+        HE(1, 2)
         B(2)
-        MAX(10)
-        E2(2)
-        DG(1, 7)
-        B(4)
-        U(6)
+        LV(0)
+        DG(1, 4)
+        HE(1, 3)
+        C(4)
+        B(3)
+        Z(9)
+        MAX(8)
+        U(7)
+        R(6, 2)
+        QF(10, 2)
+        HE(1, 4)
+        QH(1, 0)
+        DG(1, 5)
+        C(6)
+        EXP(8)
+        DIAG(15)
+        HE(1, 5)
+        Y(2)
+        C(7)
+        MAX(9)
+        U(4)
+        DG(1, 6)
+        T(13)
         HE(1, 6)
-        DG(2, 0)
-        E2(3)
-        HE(1, 7)
-        EXP(9)
-        DG(2, 1)
-        T(7, 1)
-        HE(2, 0)
-        HE(2, 1)
-        EXP(10)
+        DIAG(13)
+        T(12)
+        DG(1, 7)
+        Y(3)
         B(5)
-        FIN(0, 0, 0, 256)
+        W(4)
+        F(12)
+        YI(0, 0, 0, 128)
+        EXP(9)
+        HE(1, 7)
+        Z(10)
+        DG(2, 0)
+        F(13)
+        HE(2, 0)
+        U(6)
+        MAX(10)
+        R(8, 2)
+        C(9)
+        T(15)
         W(7)
+        W(6)
+        Y(5)
+        DG(2, 1)
+        EXP(10)
+        Z(11)
+        B(7)
         DG(2, 2)
-        DIAG(14)
+        B(4)
+        Y(4)
+        MAX(11)
+        QF(12, 2)
+        U(9)
+        HE(2, 1)
+        YI(0, 0, 384, 512)
+        T(14)
+        B(6)
+        Y(6)
         DG(2, 3)
         HE(2, 2)
-        C(8)
-        W(6)
-        R(9)
-        LAM()
-        Z(11)
-        E2(4)
         DG(2, 4)
-        FIN(0, 0, 256, 512)
-        MAX(11)
-        F(7, 1)
-        QH(1, 1)
-        T(7, 0)
-        E2(5)
+        EXP(11)
         Z(12)
         HE(2, 3)
-        B(7)
-        DG(2, 5)
-        HE(2, 4)
-        R(10)
-        F(7, 0)
-        MAX(12)
-        EXP(11)
-        HE(2, 5)
-        U(9)
-        DG(2, 6)
-        C(9)
-        E2(7)
-        B(6)
+        Z(13)
         U(8)
-        QF(7)
-        R(11)
+        DG(2, 5)
         W(9)
+        Y(7)
+        YI(0, 0, 256, 384)
+        C(8)
+        U(11)
+        B(9)
+        R(10, 2)
+        YI(0, 0, 128, 256)
+        C(11)
+        F(15)
+        HE(2, 4)
+        DG(2, 6)
+        F(14)
+        HE(2, 5)
+        MAX(12)
         W(8)
+        YI(1, 0, 384, 512)
+        U(10)
+        MAX(13)
+        QH(1, 1)
+        LV(2)
+        QF(14, 2)
         EXP(12)
         HE(2, 6)
-        E2(6)
-        Z(13)
-        MAX(13)
-        QY(0)
-        DG(2, 7)
-        R(12)
-        B(8)
-        HE(2, 7)
-        FIN(1, 0, 256, 512)
-        U(10)
-        DG(3, 0)
-        E2(8)
-        B(9)
-        EXP(13)
         C(10)
-        U(11)
-        Z(14)
-        HE(3, 0)
-        DG(3, 1)
-        K(2, 0)
-        C(11)
-        FIN(1, 0, 0, 256)
-        C(12)
+        QY(0)
         W(11)
-        K(3, 0)
-        LV(5)
-        HE(3, 1)
-        W(10)
-        R(13)
-        E2(9)
-        MAX(14)
+        EXP(13)
+        DG(2, 7)
+        DG(3, 0)
+        HE(2, 7)
+        R(12, 2)
+        Z(14)
+        DG(3, 1)
+        YI(1, 0, 0, 128)
         Z(15)
-        DG(3, 2)
-        B(11)
-        MAX(15)
-        HE(3, 2)
-        DG(3, 3)
-        QY(1)
-        C(13)
-        U(12)
-        E2(11)
-        EXP(14)
-        DG(3, 4)
-        LV(1)
-        B(10)
-        EXP(15)
-        E2(10)
-        QH(2, 1)
-        W(12)
-        LV(3)
         U(13)
-        R(14)
-        W(13)
-        B(12)
-        HE(3, 3)
-        U(15)
+        W(10)
+        MAX(14)
+        HE(3, 0)
+        HE(3, 1)
         QH(2, 0)
-        C(14)
-        LV(2)
-        HE(3, 4)
-        K(4, 0)
+        Y(9)
+        DG(3, 2)
+        DG(3, 3)
+        C(13)
+        B(8)
+        YI(1, 0, 128, 256)
+        B(11)
+        W(13)
+        B(10)
+        U(15)
+        MAX(15)
+        C(12)
+        U(12)
+        Y(11)
+        HE(3, 2)
+        YI(1, 0, 256, 384)
+        HE(3, 3)
+        EXP(15)
+        DG(3, 4)
+        Y(10)
+        Y(8)
         DG(3, 5)
-        U(14)
-        R(15)
-        K(2, 1)
-        K(4, 1)
-        HE(3, 5)
-        B(13)
-        FIN(2, 0, 256, 512)
+        K(2, 0)
+        EXP(14)
+        W(12)
+        K(3, 0)
+        R(14, 2)
+        HE(3, 4)
         K(5, 0)
+        HE(3, 5)
+        QY(1)
+        K(4, 0)
         C(15)
-        FIN(2, 0, 0, 256)
-        DG(3, 6)
-        DG(3, 7)
-        W(14)
+        QH(2, 1)
         W(15)
-        HE(3, 6)
-        K(3, 1)
-        K(0, 0)
-        QY(2)
-        B(14)
-        B(15)
-        Y(13)
-        LV(0)
-        Y(14)
-        HE(3, 7)
-        K(0, 1)
-        K(3, 2)
-        K(4, 2)
-        K(1, 0)
+        U(14)
+        C(14)
+        DG(3, 6)
+        K(2, 1)
+        B(13)
+        B(12)
+        W(14)
+        YI(2, 0, 0, 256)
         K(5, 1)
-        Y(12)
-        Y(15)
-        K(1, 1)
+        K(4, 1)
         K(7, 0)
-        K(5, 2)
-        QH(3, 0)
-        YI(0, 336, 512)
-        YI(1, 0, 336)
-        K(1, 2)
-        K(6, 0)
-        K(0, 2)
-        K(6, 1)
-        QY(3)
-        K(2, 2)
-        QH(3, 1)
-        K(0, 3)
-        EP(0)
-        K(2, 3)
-        EP(2)
-        K(3, 3)
-        K(6, 2)
-        EP(3)
-        K(1, 3)
-        LV(4)
-        EP(1)
-        K(4, 3)
-        LV(6)
-        EP(4)
+        HE(3, 6)
+        K(0, 0)
+        YI(2, 0, 256, 512)
+        B(14)
+        DG(3, 7)
+        LV(3)
+        K(0, 1)
+        K(3, 1)
+        B(15)
+        HE(3, 7)
+        Y(12)
+        K(1, 0)
+        Y(15)
         LV(7)
-        K(6, 3)
-        EP(6)
-        K(7, 1)
+        Y(13)
+        Y(14)
+        K(1, 1)
+        YI(3, 0, 336, 512)
+        K(6, 0)
+        QY(2)
+        YI(3, 1, 0, 336)
+        K(3, 2)
+        QH(3, 0)
+        K(2, 2)
+        QY(3)
+        K(4, 2)
+        K(0, 2)
+        K(1, 2)
+        K(0, 3)
+        QH(3, 1)
+        K(1, 3)
+        K(2, 3)
+        K(3, 3)
+        K(5, 2)
         K(5, 3)
+        LV(5)
+        K(6, 1)
+        EP(0, 0, 512)
+        EP(1, 0, 512)
+        K(4, 3)
+        K(7, 1)
+        ST(0, 0)
+        EP(3, 0, 512)
+        K(6, 2)
+        EP(2, 0, 512)
+        EP(5, 0, 512)
+        LV(4)
+        EP(4, 0, 512)
         K(7, 2)
         K(7, 3)
+        K(6, 3)
+        EP(7, 0, 512)
+        EP(6, 0, 512)
+        ST(0, 2)
         OI(0, 0, 0, 512)
-        EP(7)
-        EP(5)
-        OI(1, 1, 0, 352)
         OI(1, 0, 352, 512)
+        ST(1, 0)
+        ST(1, 2)
+        OI(1, 1, 0, 352)
         QO(0)
         QO(1)

@@ -43,10 +43,8 @@ def tile_dampedsoftmaxfisherproduct_kernel(tc, h, g, w_words, w_scales, v, e, rh
         ident = tile("ident", [P, P], F32)
         warm = tile("warm", [P, 1], F32)
         g_sb = tile("g_sb", [P, HALVES, PACK], BF16)
-        lam_sb = tile("lam_sb", [P, HALVES, PACK], BF16)
-        e_sb = tile("e_sb", [P, GROUPS, PACK], BF16)
-        rho_sb = tile("rho_sb", [P, GROUPS, PACK], BF16)
-        lam32 = tile("lam32", [P, HALVES * PACK], F32)
+        vec_rows = tile("vec_rows", [P, K_PASS], BF16)
+        lam_e = tile("lam_e", [P, HALVES + GROUPS, PACK], F32)
         rho_neg = tile("rho_neg", [P, TILES], F32)
         diag = tile("diag", [P, TILES, P], BF16)
         h_sb = [tile("h%d" % G, [P, PACK, D], BF16) for G in range(GROUPS)]
@@ -65,7 +63,6 @@ def tile_dampedsoftmaxfisherproduct_kernel(tc, h, g, w_words, w_scales, v, e, rh
         eu = [tile("eu%d" % b, [P, PACK, A], F32) for b in range(2)]
         y_bf = [tile("y_bf%d" % b, [P, A, PACK], BF16) for b in range(2)]
         y_rows = [tile("y_rows%d" % b, [P, PACK, A], BF16) for b in range(2)]
-        e32 = tile("e32", [P, TILES], F32)
         ks = [tile("ks%d" % b, [P, A], F32) for b in range(2)]
         y_codes = tile("y_codes", [P, GROUPS, A], U32)
         y_plane = tile("y_plane", [P, GROUPS, A], U8)
@@ -79,6 +76,9 @@ def tile_dampedsoftmaxfisherproduct_kernel(tc, h, g, w_words, w_scales, v, e, rh
         coef = tile("coef", [P, TILES], F32)
         acc = tile("acc", [P, TILES], F32)
         shift = tile("shift", [P, TILES], F32)
+
+        lam32 = lam_e[:, :HALVES, :].rearrange("p c t -> p (c t)")
+        e32 = lam_e[:, HALVES:, :].rearrange("p c t -> p (c t)")
 
         def col(t, i):
             return t[:, i : i + 1]
@@ -97,8 +97,23 @@ def tile_dampedsoftmaxfisherproduct_kernel(tc, h, g, w_words, w_scales, v, e, rh
             rows = v[gh * K_PASS : (gh + 1) * K_PASS, :].rearrange("(p t) a -> p t a", t=PACK)
             nc.sync.dma_start(out=v_sb[:, gh, :, :], in_=rows)
 
-        def load_vec(eng, dst, src):
-            eng.dma_start(out=dst[:], in_=src.rearrange("(c p t) -> p c t", p=P, t=PACK))
+        def load_vec(row0, src):
+            rows = src.rearrange("(c k) -> c k", k=K_PASS)
+            nc.sync.dma_start(out=vec_rows[row0 : row0 + rows.shape[0], :], in_=rows)
+
+        def vec_cols(row0, row1):
+            return u_banks[0][:, : 2 * P].bitcast(BF16).rearrange("p (u r e) -> p r u e", u=2, e=2)[:, row0:row1, :, :]
+
+        def VT():
+            words = vec_rows[:].bitcast(F32)
+            for u in range(2):
+                nc.tensor.transpose(u_banks[0][:, u * P : (u + 1) * P], words[:, u::2], ident[:])
+
+        def VG():
+            nc.vector.tensor_copy(out=g_sb[:].rearrange("p c (u e) -> p c u e", u=2), in_=vec_cols(0, 2))
+
+        def VL():
+            nc.vector.tensor_copy(out=lam_e[:].rearrange("p c (u e) -> p c u e", u=2), in_=vec_cols(2, 8))
 
         def T(i):
             G, t = divmod(i, PACK)
@@ -224,6 +239,10 @@ def tile_dampedsoftmaxfisherproduct_kernel(tc, h, g, w_words, w_scales, v, e, rh
                 op0=ALU.mult, op1=ALU.subtract,
             )
 
+        def YP(i):
+            nc.gpsimd.tensor_scalar(out=row(ex, i), in0=row(ex, i), scalar1=col(shift, i), scalar2=0.0, op0=ALU.mult, op1=ALU.add)
+            nc.gpsimd.tensor_tensor(out=row(y_rows, i), in0=row(ex, i), in1=row(eu, i), op=ALU.subtract)
+
         def il(eng, dst, src, a0, a1, run):
             out = dst[:, a0:a1, :].rearrange("p (c i) t -> p c t i", i=run)
             in_ = src[:, :, a0:a1].rearrange("p t (c i) -> p c t i", i=run)
@@ -244,14 +263,10 @@ def tile_dampedsoftmaxfisherproduct_kernel(tc, h, g, w_words, w_scales, v, e, rh
         def DIAG(i):
             nc.scalar.activation(out=diag[:, i, :], in_=ident[:], func=ACT.Copy, scale=col(e32, i))
 
-        def E32():
-            nc.gpsimd.tensor_copy(out=e32[:], in_=e_sb[:].rearrange("p c t -> p (c t)"))
 
         def RHO():
-            nc.gpsimd.tensor_scalar(out=rho_neg[:], in0=rho_sb[:].rearrange("p c t -> p (c t)"), scalar1=-float(A), scalar2=0.0, op0=ALU.mult, op1=ALU.add)
+            nc.vector.tensor_scalar(out=rho_neg[:].rearrange("p (c u e) -> p c u e", u=2, e=2), in0=vec_cols(8, 12), scalar1=-float(A), scalar2=None, op0=ALU.mult)
 
-        def LAM():
-            nc.gpsimd.tensor_copy(out=lam32[:], in_=lam_sb[:].rearrange("p c t -> p (c t)"))
 
         def QY(G):
             nc.vector.quantize_mx(out=y_codes[:, G, :].bitcast(FP8X4), scales=y_plane[:, G, :], in_=flat(y_bf[G % 2][:]))
@@ -288,7 +303,12 @@ def tile_dampedsoftmaxfisherproduct_kernel(tc, h, g, w_words, w_scales, v, e, rh
 
         def QO(gh):
             nc.vector.quantize_mx(out=o_codes[:, gh, :].bitcast(FP8X4), scales=o_plane[:, gh, :], in_=flat(wide_bf[gh][:]))
-            nc.sync.dma_start(out=out_1[gh].rearrange("p m t -> p (m t)").bitcast(I32), in_=o_codes[:, gh, :].bitcast(I32))
+            words = out_1[gh].rearrange("p m t -> p (m t)").bitcast(I32)
+            if gh == 0:
+                nc.sync.dma_start(out=words, in_=o_codes[:, gh, :].bitcast(I32))
+            else:
+                nc.sync.dma_start(out=words[:, : A // 2], in_=o_codes[:, gh, : A // 2].bitcast(I32))
+                nc.scalar.dma_start(out=words[:, A // 2 :], in_=o_codes[:, gh, A // 2 :].bitcast(I32))
             if gh == HALVES - 1:
                 for Q in range(4):
                     eng = nc.sync if Q < 2 else nc.scalar
@@ -299,374 +319,376 @@ def tile_dampedsoftmaxfisherproduct_kernel(tc, h, g, w_words, w_scales, v, e, rh
 
         ctx.enter_context(tc.manual_schedule())
 
-        load_vec(nc.scalar, g_sb, g)
-        load_vec(nc.scalar, e_sb, e)
+        nc.gpsimd.memset(vec_rows[:].bitcast(U32), 0)
+        nc.vector.memset(warm[:], 0.0)
+        nc.vector.memset(w_plane[:].rearrange("p g a -> p (g a)").bitcast(U32), 0)
+        make_identity(nc, ident[:])
+        load_vec(0, g)
+        load_vec(2, lam)
+        load_vec(4, e)
+        load_vec(8, rho)
         load_h(0, 0, 1)
         load_h(0, 1, 2)
-        make_identity(nc, ident[:])
-        nc.vector.memset(w_plane[:].rearrange("p g a -> p (g a)").bitcast(U32), 0)
-        nc.vector.memset(warm[:], 0.0)
-        nc.sync.dma_start(out=w_codes[:].bitcast(I32), in_=w_words.rearrange("g p n -> p g n").bitcast(I32))
         load_h(0, 2, 4)
+        nc.sync.dma_start(out=w_codes[:].bitcast(I32), in_=w_words.rearrange("g p n -> p g n").bitcast(I32))
+        nc.scalar.activation(out=warm[:], in_=warm[:], func=ACT.Exp)
+        load_v(0)
         for Q in range(4):
-            nc.gpsimd.dma_start(
+            nc.scalar.dma_start(
                 out=w_plane[32 * Q : 32 * Q + 4, :, :].bitcast(I32),
                 in_=w_scales[:, 4 * Q : 4 * Q + 4, :].rearrange("g q a -> q g a").bitcast(I32),
             )
-        nc.scalar.activation(out=warm[:], in_=warm[:], func=ACT.Exp)
-        load_v(0)
         load_h(1, 0, 2)
         load_v(1)
-        load_vec(nc.sync, rho_sb, rho)
         load_h(1, 2, 4)
         load_h(2, 0, PACK)
         load_h(3, 0, PACK)
-        load_vec(nc.sync, lam_sb, lam)
 
-        E32()
-        DIAG(2)
+        VT()
+        RHO()
+        VL()
+        VG()
         T(0)
         T(1)
-        DIAG(3)
-        DIAG(0)
-        T(2)
         F(0)
-        T(3)
+        DIAG(0)
         F(1)
+        T(2)
         QF(1, 1)
-        LAM()
-        DIAG(1)
         F(2)
+        T(3)
+        DIAG(2)
+        DIAG(1)
         F(3)
-        T(4)
+        DIAG(14)
+        DIAG(3)
         QF(0, 1)
-        QF(2, 2)
+        DIAG(4)
+        DG(0, 0)
         Z(1)
-        DIAG(11)
-        Z(0)
+        QF(2, 2)
         T(5)
         VI(0, 0, 0, 512)
-        F(4)
-        T(6)
-        QV(0)
         VI(1, 0, 256, 512)
         MAX(1)
-        MAX(0)
-        DG(0, 1)
-        DG(0, 0)
-        VI(1, 0, 0, 256)
-        EXP(1)
         F(5)
-        EXP(0)
+        T(4)
+        EXP(1)
+        Z(0)
+        T(7)
+        F(4)
+        VI(1, 0, 0, 256)
+        QV(0)
+        T(6)
+        MAX(0)
+        F(7)
+        F(6)
+        R(1, 1)
+        QF(4, 2)
         Z(3)
-        Z(2)
+        DG(0, 1)
+        T(9)
+        LV(6)
         HE(0, 0)
+        EXP(0)
+        T(8)
+        DIAG(15)
+        HE(0, 1)
+        MAX(3)
         DG(0, 2)
         QV(1)
-        R(1, 1)
-        T(7)
-        F(6)
-        RHO()
-        DIAG(5)
-        R(0, 1)
-        C(1)
-        LV(1)
-        C(0)
-        QF(4, 2)
-        U(0)
-        HE(0, 1)
-        HE(0, 2)
-        DIAG(12)
-        U(1)
-        DG(0, 3)
-        MAX(3)
-        DG(0, 4)
-        MAX(2)
-        F(7)
-        EXP(2)
         EXP(3)
-        Z(4)
-        W(0)
-        HE(0, 3)
-        DIAG(8)
-        DIAG(7)
-        Z(5)
-        HE(0, 4)
-        W(1)
-        DIAG(14)
-        DG(0, 5)
-        DIAG(9)
-        DIAG(4)
-        QF(6, 2)
-        T(9)
-        R(2, 2)
-        B(0)
-        T(8)
-        C(2)
-        QH(0, 0)
-        MAX(4)
-        MAX(5)
-        U(2)
-        U(3)
-        Y(0)
-        DG(0, 6)
-        HE(0, 5)
-        DIAG(10)
-        DG(0, 7)
-        B(1)
-        F(9)
-        EXP(4)
-        F(8)
-        Y(1)
-        C(3)
+        C(1)
+        HE(0, 2)
+        Z(2)
         DIAG(6)
-        EXP(5)
-        LV(6)
-        R(4, 2)
-        HE(0, 6)
-        Z(6)
-        HE(0, 7)
-        QF(8, 2)
-        W(2)
-        Z(7)
-        DG(1, 0)
-        MAX(6)
-        HE(1, 0)
-        DG(1, 1)
-        T(11)
-        C(5)
-        W(3)
-        HE(1, 1)
-        MAX(7)
-        QH(0, 1)
+        QF(6, 2)
+        R(0, 1)
+        F(9)
+        C(0)
+        U(0)
+        MAX(2)
+        F(8)
+        U(1)
+        LV(3)
+        EXP(2)
+        W(0)
+        W(1)
+        DG(0, 3)
+        Z(5)
+        MAX(5)
+        DG(0, 4)
+        Z(4)
         T(10)
-        DG(1, 2)
+        R(2, 2)
+        HE(0, 3)
+        B(0)
+        HE(0, 4)
+        T(11)
+        MAX(4)
+        QH(0, 0)
+        Y(0)
         F(10)
-        EXP(6)
-        EXP(7)
-        U(5)
+        DIAG(5)
+        C(3)
+        C(2)
+        DG(0, 5)
+        QF(8, 2)
+        U(2)
+        EXP(5)
+        DIAG(13)
+        DG(0, 6)
+        Z(7)
+        DIAG(7)
+        U(3)
         F(11)
-        DG(1, 3)
-        Z(8)
-        W(5)
-        HE(1, 2)
-        B(2)
+        EXP(4)
+        DIAG(8)
+        R(4, 2)
+        HE(0, 5)
+        MAX(7)
+        W(2)
+        HE(0, 6)
+        DG(0, 7)
+        QF(10, 2)
+        B(1)
         LV(0)
+        Z(6)
+        T(13)
+        MAX(6)
+        EXP(7)
+        DG(1, 0)
+        Y(1)
+        HE(0, 7)
+        Z(9)
+        U(4)
+        W(3)
+        DG(1, 1)
+        HE(1, 0)
+        C(5)
+        DG(1, 2)
+        EXP(6)
+        C(4)
+        MAX(9)
+        F(13)
+        W(4)
+        Z(8)
+        HE(1, 1)
+        T(12)
+        DG(1, 3)
+        B(2)
+        B(3)
+        EXP(9)
+        Y(2)
+        MAX(8)
+        DIAG(11)
+        U(5)
+        HE(1, 2)
+        Y(3)
         DG(1, 4)
         HE(1, 3)
-        C(4)
-        B(3)
-        Z(9)
-        MAX(8)
-        U(7)
-        R(6, 2)
-        QF(10, 2)
-        HE(1, 4)
-        QH(1, 0)
-        DG(1, 5)
-        C(6)
-        EXP(8)
-        DIAG(15)
-        HE(1, 5)
-        Y(2)
-        C(7)
-        MAX(9)
-        U(4)
-        DG(1, 6)
-        T(13)
-        HE(1, 6)
-        DIAG(13)
-        T(12)
-        DG(1, 7)
-        Y(3)
-        B(5)
-        W(4)
-        F(12)
-        YI(0, 0, 0, 128)
-        EXP(9)
-        HE(1, 7)
-        Z(10)
-        DG(2, 0)
-        F(13)
-        HE(2, 0)
-        U(6)
-        MAX(10)
-        R(8, 2)
-        C(9)
-        T(15)
-        W(7)
-        W(6)
-        Y(5)
-        DG(2, 1)
-        EXP(10)
-        Z(11)
-        B(7)
-        DG(2, 2)
         B(4)
-        Y(4)
+        Z(11)
+        R(6, 2)
+        W(5)
+        EXP(8)
+        DIAG(10)
+        U(6)
+        DG(1, 5)
+        QH(1, 0)
+        HE(1, 4)
+        F(12)
+        Z(10)
+        LV(1)
+        DG(1, 6)
         MAX(11)
-        QF(12, 2)
-        U(9)
-        HE(2, 1)
-        YI(0, 0, 384, 512)
+        C(6)
+        HE(1, 5)
+        YI(0, 0, 0, 128)
+        MAX(10)
+        C(7)
+        W(6)
+        HE(1, 6)
+        U(7)
         T(14)
-        B(6)
-        Y(6)
-        DG(2, 3)
-        HE(2, 2)
-        DG(2, 4)
         EXP(11)
-        Z(12)
-        HE(2, 3)
-        Z(13)
+        DG(1, 7)
+        T(15)
+        R(8, 2)
+        DIAG(9)
+        B(5)
+        DIAG(12)
+        W(7)
+        DG(2, 0)
+        YI(0, 0, 256, 384)
+        QH(0, 1)
+        C(8)
+        HE(1, 7)
+        U(9)
+        DG(2, 1)
+        QF(12, 2)
+        B(6)
+        Y(4)
+        C(9)
+        B(7)
+        EXP(10)
+        HE(2, 0)
+        F(15)
+        HE(2, 1)
         U(8)
-        DG(2, 5)
+        Z(13)
+        DG(2, 2)
+        YI(0, 0, 128, 256)
+        HE(2, 2)
+        F(14)
         W(9)
         Y(7)
-        YI(0, 0, 256, 384)
-        C(8)
-        U(11)
-        B(9)
-        R(10, 2)
-        YI(0, 0, 128, 256)
-        C(11)
-        F(15)
-        HE(2, 4)
-        DG(2, 6)
-        F(14)
-        HE(2, 5)
-        MAX(12)
+        DG(2, 3)
         W(8)
-        YI(1, 0, 384, 512)
-        U(10)
+        Z(12)
+        HE(2, 3)
+        DG(2, 4)
         MAX(13)
-        QH(1, 1)
-        LV(2)
-        QF(14, 2)
+        YI(0, 0, 384, 512)
+        HE(2, 4)
+        MAX(12)
+        DG(2, 5)
+        DG(2, 6)
+        U(10)
+        HE(2, 5)
+        Y(5)
+        R(10, 2)
         EXP(12)
-        HE(2, 6)
-        C(10)
+        QH(1, 1)
+        Y(6)
         QY(0)
-        W(11)
+        QF(14, 2)
         EXP(13)
-        DG(2, 7)
-        DG(3, 0)
-        HE(2, 7)
+        C(10)
+        U(11)
+        HE(2, 6)
         R(12, 2)
-        Z(14)
-        DG(3, 1)
-        YI(1, 0, 0, 128)
-        Z(15)
-        U(13)
+        B(9)
         W(10)
+        DG(2, 7)
+        Z(14)
+        DG(3, 0)
+        Z(15)
+        C(11)
+        B(8)
+        YI(1, 0, 256, 384)
+        U(12)
+        YI(1, 0, 128, 256)
+        C(12)
+        W(11)
+        HE(2, 7)
+        DG(3, 1)
+        YI(1, 0, 384, 512)
+        K(3, 0)
+        U(13)
+        B(11)
+        QH(2, 0)
         MAX(14)
         HE(3, 0)
-        HE(3, 1)
-        QH(2, 0)
-        Y(9)
-        DG(3, 2)
-        DG(3, 3)
-        C(13)
-        B(8)
-        YI(1, 0, 128, 256)
-        B(11)
-        W(13)
-        B(10)
-        U(15)
-        MAX(15)
-        C(12)
-        U(12)
-        Y(11)
-        HE(3, 2)
-        YI(1, 0, 256, 384)
-        HE(3, 3)
-        EXP(15)
-        DG(3, 4)
-        Y(10)
-        Y(8)
-        DG(3, 5)
-        K(2, 0)
         EXP(14)
+        MAX(15)
+        DG(3, 2)
+        EXP(15)
+        C(13)
+        B(10)
         W(12)
-        K(3, 0)
+        HE(3, 1)
+        HE(3, 2)
+        K(4, 0)
+        Y(11)
+        B(12)
+        U(14)
+        Y(9)
         R(14, 2)
+        C(14)
+        C(15)
+        W(13)
+        YI(1, 0, 0, 128)
+        Y(8)
+        DG(3, 3)
+        DG(3, 4)
+        HE(3, 3)
+        Y(10)
+        W(14)
+        QY(1)
+        B(13)
         HE(3, 4)
+        U(15)
+        Y(12)
+        DG(3, 5)
+        DG(3, 6)
+        YI(2, 0, 0, 256)
         K(5, 0)
         HE(3, 5)
-        QY(1)
-        K(4, 0)
-        C(15)
-        QH(2, 1)
-        W(15)
-        U(14)
-        C(14)
-        DG(3, 6)
-        K(2, 1)
-        B(13)
-        B(12)
-        W(14)
-        YI(2, 0, 0, 256)
-        K(5, 1)
-        K(4, 1)
-        K(7, 0)
-        HE(3, 6)
-        K(0, 0)
-        YI(2, 0, 256, 512)
         B(14)
+        K(2, 0)
+        K(2, 1)
+        W(15)
         DG(3, 7)
-        LV(3)
-        K(0, 1)
-        K(3, 1)
-        B(15)
-        HE(3, 7)
-        Y(12)
-        K(1, 0)
-        Y(15)
-        LV(7)
-        Y(13)
-        Y(14)
-        K(1, 1)
-        YI(3, 0, 336, 512)
+        K(5, 1)
+        HE(3, 6)
+        YI(2, 0, 256, 512)
         K(6, 0)
+        Y(13)
+        K(7, 0)
+        B(15)
+        K(6, 1)
+        Y(14)
+        Y(15)
+        QH(2, 1)
+        HE(3, 7)
+        K(4, 1)
+        K(0, 0)
+        YI(3, 0, 160, 512)
+        K(0, 1)
         QY(2)
-        YI(3, 1, 0, 336)
-        K(3, 2)
+        K(7, 1)
+        K(1, 0)
+        K(1, 1)
+        K(3, 1)
+        LV(7)
+        YI(3, 1, 0, 160)
         QH(3, 0)
-        K(2, 2)
         QY(3)
-        K(4, 2)
+        LV(5)
+        K(3, 2)
+        K(7, 2)
         K(0, 2)
+        QH(3, 1)
         K(1, 2)
         K(0, 3)
-        QH(3, 1)
-        K(1, 3)
-        K(2, 3)
-        K(3, 3)
-        K(5, 2)
-        K(5, 3)
-        LV(5)
-        K(6, 1)
         EP(0, 0, 512)
+        K(1, 3)
+        LV(2)
+        K(2, 2)
         EP(1, 0, 512)
-        K(4, 3)
-        K(7, 1)
-        ST(0, 0)
-        EP(3, 0, 512)
+        K(3, 3)
         K(6, 2)
+        K(2, 3)
+        K(4, 2)
+        EP(3, 0, 512)
         EP(2, 0, 512)
-        EP(5, 0, 512)
-        LV(4)
-        EP(4, 0, 512)
-        K(7, 2)
-        K(7, 3)
         K(6, 3)
-        EP(7, 0, 512)
         EP(6, 0, 512)
-        ST(0, 2)
+        LV(4)
+        K(7, 3)
+        K(5, 2)
         OI(0, 0, 0, 512)
-        OI(1, 0, 352, 512)
-        ST(1, 0)
+        K(5, 3)
+        ST(0, 0)
+        K(4, 3)
+        EP(7, 0, 512)
+        EP(5, 0, 512)
+        EP(4, 0, 512)
+        ST(0, 2)
         ST(1, 2)
+        ST(1, 0)
         OI(1, 1, 0, 352)
+        OI(1, 0, 352, 512)
         QO(0)
         QO(1)

@@ -345,350 +345,350 @@ def tile_dampedsoftmaxfisherproduct_kernel(tc, h, g, w_words, w_scales, v, e, rh
         load_h(3, 0, PACK)
 
         VT()
-        RHO()
         VL()
-        VG()
-        T(0)
-        T(1)
-        F(0)
-        DIAG(0)
-        F(1)
-        T(2)
-        QF(1, 1)
-        F(2)
-        T(3)
-        DIAG(2)
-        DIAG(1)
-        F(3)
-        DIAG(14)
         DIAG(3)
-        QF(0, 1)
-        DIAG(4)
-        DG(0, 0)
-        Z(1)
-        QF(2, 2)
-        T(5)
-        VI(0, 0, 0, 512)
-        VI(1, 0, 256, 512)
-        MAX(1)
-        F(5)
-        T(4)
-        EXP(1)
-        Z(0)
-        T(7)
-        F(4)
-        VI(1, 0, 0, 256)
-        QV(0)
-        T(6)
-        MAX(0)
-        F(7)
-        F(6)
-        R(1, 1)
-        QF(4, 2)
-        Z(3)
-        DG(0, 1)
-        T(9)
-        LV(6)
-        HE(0, 0)
-        EXP(0)
-        T(8)
-        DIAG(15)
-        HE(0, 1)
-        MAX(3)
-        DG(0, 2)
-        QV(1)
-        EXP(3)
-        C(1)
-        HE(0, 2)
-        Z(2)
-        DIAG(6)
-        QF(6, 2)
-        R(0, 1)
-        F(9)
-        C(0)
-        U(0)
-        MAX(2)
-        F(8)
-        U(1)
-        LV(3)
-        EXP(2)
-        W(0)
-        W(1)
-        DG(0, 3)
-        Z(5)
-        MAX(5)
-        DG(0, 4)
-        Z(4)
-        T(10)
-        R(2, 2)
-        HE(0, 3)
-        B(0)
-        HE(0, 4)
-        T(11)
-        MAX(4)
-        QH(0, 0)
-        Y(0)
-        F(10)
+        DIAG(1)
+        RHO()
+        DIAG(0)
+        T(0)
+        DIAG(11)
+        VG()
+        T(1)
+        T(3)
+        T(2)
         DIAG(5)
-        C(3)
-        C(2)
-        DG(0, 5)
-        QF(8, 2)
-        U(2)
-        EXP(5)
-        DIAG(13)
-        DG(0, 6)
-        Z(7)
+        F(0)
+        F(1)
         DIAG(7)
-        U(3)
-        F(11)
-        EXP(4)
-        DIAG(8)
-        R(4, 2)
+        QF(0, 1)
+        DIAG(2)
+        DG(0, 0)
+        QF(1, 1)
+        VI(0, 0, 0, 512)
+        F(3)
+        DG(0, 1)
+        Z(1)
+        F(2)
+        QF(2, 2)
+        Z(0)
+        T(5)
+        MAX(1)
+        MAX(0)
+        T(4)
+        F(5)
+        F(4)
+        HE(0, 0)
+        QV(0)
+        DG(0, 2)
+        HE(0, 1)
+        EXP(1)
+        QF(4, 2)
+        T(7)
+        T(6)
+        F(7)
+        Z(3)
+        EXP(0)
+        Z(2)
+        T(9)
+        VI(1, 0, 256, 512)
+        F(6)
+        T(8)
+        MAX(3)
+        VI(1, 0, 0, 256)
+        MAX(2)
+        DIAG(12)
+        R(0, 1)
+        EXP(3)
+        F(9)
+        EXP(2)
+        DG(0, 3)
+        DIAG(13)
+        F(8)
+        HE(0, 2)
+        Z(5)
+        DIAG(14)
+        C(0)
+        Z(4)
+        QV(1)
+        R(1, 1)
+        MAX(5)
+        HE(0, 3)
+        C(1)
+        U(1)
+        QF(8, 2)
+        DG(0, 4)
+        DIAG(10)
+        MAX(4)
+        DIAG(6)
+        DG(0, 5)
+        R(2, 2)
+        W(1)
+        DIAG(15)
+        DIAG(4)
+        QF(6, 2)
+        HE(0, 4)
         HE(0, 5)
-        MAX(7)
-        W(2)
-        HE(0, 6)
-        DG(0, 7)
-        QF(10, 2)
+        U(0)
+        T(11)
+        EXP(5)
+        T(10)
+        W(0)
+        DG(0, 6)
         B(1)
-        LV(0)
+        Z(7)
+        EXP(4)
         Z(6)
-        T(13)
-        MAX(6)
-        EXP(7)
-        DG(1, 0)
         Y(1)
+        C(2)
+        B(0)
+        U(3)
+        F(10)
+        LV(4)
+        LV(5)
+        YP(0)
+        DG(0, 7)
+        MAX(7)
+        HE(0, 6)
+        U(2)
+        DG(1, 0)
+        QH(0, 0)
+        F(11)
+        EXP(7)
         HE(0, 7)
         Z(9)
-        U(4)
-        W(3)
-        DG(1, 1)
         HE(1, 0)
-        C(5)
-        DG(1, 2)
-        EXP(6)
-        C(4)
-        MAX(9)
-        F(13)
-        W(4)
-        Z(8)
-        HE(1, 1)
+        R(4, 2)
+        DG(1, 1)
+        DIAG(8)
+        W(2)
         T(12)
-        DG(1, 3)
+        C(5)
+        T(13)
+        DG(1, 2)
+        C(4)
+        HE(1, 1)
+        C(3)
+        MAX(6)
         B(2)
+        EXP(6)
+        QH(0, 1)
+        DIAG(9)
+        YP(2)
+        QF(10, 2)
+        HE(1, 2)
+        W(3)
+        DG(1, 3)
+        Z(8)
+        HE(1, 3)
+        MAX(9)
+        U(4)
+        DG(1, 4)
         B(3)
         EXP(9)
-        Y(2)
-        MAX(8)
-        DIAG(11)
-        U(5)
-        HE(1, 2)
-        Y(3)
-        DG(1, 4)
-        HE(1, 3)
-        B(4)
-        Z(11)
-        R(6, 2)
-        W(5)
-        EXP(8)
-        DIAG(10)
-        U(6)
         DG(1, 5)
-        QH(1, 0)
         HE(1, 4)
-        F(12)
-        Z(10)
-        LV(1)
-        DG(1, 6)
-        MAX(11)
-        C(6)
+        F(13)
         HE(1, 5)
-        YI(0, 0, 0, 128)
-        MAX(10)
-        C(7)
-        W(6)
-        HE(1, 6)
-        U(7)
-        T(14)
-        EXP(11)
+        U(5)
+        MAX(8)
+        Z(11)
+        DG(1, 6)
+        W(4)
+        F(12)
+        Y(3)
+        B(4)
+        R(6, 2)
+        EXP(8)
         DG(1, 7)
-        T(15)
+        W(5)
+        HE(1, 6)
+        U(6)
         R(8, 2)
-        DIAG(9)
-        B(5)
-        DIAG(12)
-        W(7)
+        Z(10)
+        YI(0, 0, 128, 256)
+        C(6)
         DG(2, 0)
-        YI(0, 0, 256, 384)
-        QH(0, 1)
-        C(8)
+        B(5)
         HE(1, 7)
-        U(9)
-        DG(2, 1)
+        YI(0, 0, 256, 384)
+        C(8)
+        T(15)
         QF(12, 2)
-        B(6)
-        Y(4)
-        C(9)
-        B(7)
-        EXP(10)
+        MAX(11)
+        MAX(10)
+        U(7)
         HE(2, 0)
+        W(6)
+        C(7)
+        EXP(10)
+        DG(2, 1)
+        QH(1, 0)
+        Y(5)
+        B(6)
         F(15)
+        EXP(11)
+        YP(4)
+        T(14)
+        DG(2, 2)
         HE(2, 1)
         U(8)
-        Z(13)
-        DG(2, 2)
-        YI(0, 0, 128, 256)
-        HE(2, 2)
-        F(14)
-        W(9)
-        Y(7)
+        C(9)
         DG(2, 3)
-        W(8)
+        W(7)
+        HE(2, 2)
         Z(12)
+        W(8)
+        YI(0, 0, 0, 128)
+        B(7)
         HE(2, 3)
         DG(2, 4)
-        MAX(13)
+        U(9)
+        F(14)
+        YP(6)
+        DG(2, 5)
+        R(10, 2)
         YI(0, 0, 384, 512)
         HE(2, 4)
+        Z(13)
         MAX(12)
-        DG(2, 5)
-        DG(2, 6)
-        U(10)
-        HE(2, 5)
-        Y(5)
-        R(10, 2)
-        EXP(12)
-        QH(1, 1)
-        Y(6)
-        QY(0)
-        QF(14, 2)
-        EXP(13)
+        Y(7)
         C(10)
-        U(11)
-        HE(2, 6)
-        R(12, 2)
-        B(9)
-        W(10)
-        DG(2, 7)
-        Z(14)
-        DG(3, 0)
-        Z(15)
-        C(11)
+        QF(14, 2)
+        DG(2, 6)
+        MAX(13)
+        U(10)
+        EXP(12)
+        W(9)
         B(8)
+        QH(1, 1)
+        HE(2, 5)
+        HE(2, 6)
+        YP(8)
+        Z(14)
+        DG(2, 7)
+        C(11)
+        W(10)
+        EXP(13)
+        YI(1, 0, 0, 128)
+        YI(1, 0, 128, 256)
+        HE(2, 7)
+        DG(3, 0)
+        U(11)
+        MAX(14)
+        W(11)
+        B(10)
+        Z(15)
+        DG(3, 1)
+        HE(3, 0)
+        QH(2, 0)
+        MAX(15)
+        R(12, 2)
+        QY(0)
+        EXP(14)
+        HE(3, 1)
         YI(1, 0, 256, 384)
         U(12)
-        YI(1, 0, 128, 256)
         C(12)
-        W(11)
-        HE(2, 7)
-        DG(3, 1)
-        YI(1, 0, 384, 512)
-        K(3, 0)
         U(13)
-        B(11)
-        QH(2, 0)
-        MAX(14)
-        HE(3, 0)
-        EXP(14)
-        MAX(15)
+        DG(3, 3)
         DG(3, 2)
         EXP(15)
         C(13)
-        B(10)
         W(12)
-        HE(3, 1)
+        YI(1, 0, 384, 512)
+        B(9)
+        K(2, 0)
+        B(11)
         HE(3, 2)
-        K(4, 0)
-        Y(11)
-        B(12)
         U(14)
-        Y(9)
-        R(14, 2)
-        C(14)
-        C(15)
-        W(13)
-        YI(1, 0, 0, 128)
-        Y(8)
-        DG(3, 3)
         DG(3, 4)
         HE(3, 3)
-        Y(10)
-        W(14)
+        R(14, 2)
+        W(13)
         QY(1)
+        C(15)
+        C(14)
+        LV(2)
+        B(12)
+        DG(3, 5)
+        Y(9)
+        Y(11)
+        U(15)
         B(13)
         HE(3, 4)
-        U(15)
-        Y(12)
-        DG(3, 5)
-        DG(3, 6)
-        YI(2, 0, 0, 256)
-        K(5, 0)
-        HE(3, 5)
-        B(14)
-        K(2, 0)
-        K(2, 1)
+        W(14)
+        K(3, 0)
         W(15)
-        DG(3, 7)
-        K(5, 1)
-        HE(3, 6)
-        YI(2, 0, 256, 512)
+        DG(3, 6)
         K(6, 0)
+        HE(3, 5)
+        YP(10)
+        YI(2, 0, 0, 256)
         Y(13)
-        K(7, 0)
+        B(14)
+        Y(12)
+        K(5, 0)
         B(15)
-        K(6, 1)
         Y(14)
-        Y(15)
-        QH(2, 1)
-        HE(3, 7)
+        K(7, 0)
+        YI(2, 0, 256, 512)
+        K(4, 0)
         K(4, 1)
-        K(0, 0)
-        YI(3, 0, 160, 512)
-        K(0, 1)
-        QY(2)
-        K(7, 1)
-        K(1, 0)
-        K(1, 1)
+        HE(3, 6)
+        DG(3, 7)
+        K(6, 1)
+        K(2, 1)
+        HE(3, 7)
+        Y(15)
         K(3, 1)
-        LV(7)
+        YI(3, 0, 160, 512)
+        K(5, 1)
+        K(0, 0)
+        QY(2)
+        K(1, 0)
         YI(3, 1, 0, 160)
-        QH(3, 0)
-        QY(3)
-        LV(5)
-        K(3, 2)
-        K(7, 2)
+        LV(1)
+        K(0, 1)
+        K(1, 1)
         K(0, 2)
+        K(3, 2)
+        QH(3, 0)
+        K(7, 1)
+        LV(3)
         QH(3, 1)
-        K(1, 2)
-        K(0, 3)
-        EP(0, 0, 512)
-        K(1, 3)
-        LV(2)
         K(2, 2)
-        EP(1, 0, 512)
-        K(3, 3)
-        K(6, 2)
+        K(1, 2)
+        QY(3)
+        K(1, 3)
+        QH(2, 1)
+        K(0, 3)
         K(2, 3)
-        K(4, 2)
-        EP(3, 0, 512)
+        K(6, 2)
+        K(7, 2)
+        EP(1, 0, 512)
+        LV(0)
+        LV(7)
+        EP(0, 0, 512)
+        K(3, 3)
+        ST(0, 0)
+        LV(6)
         EP(2, 0, 512)
         K(6, 3)
-        EP(6, 0, 512)
-        LV(4)
+        EP(3, 0, 512)
         K(7, 3)
-        K(5, 2)
-        OI(0, 0, 0, 512)
-        K(5, 3)
-        ST(0, 0)
-        K(4, 3)
         EP(7, 0, 512)
-        EP(5, 0, 512)
-        EP(4, 0, 512)
+        EP(6, 0, 512)
         ST(0, 2)
+        K(4, 2)
+        K(4, 3)
+        K(5, 2)
+        K(5, 3)
         ST(1, 2)
+        EP(4, 0, 512)
+        EP(5, 0, 512)
+        OI(0, 0, 0, 512)
         ST(1, 0)
-        OI(1, 1, 0, 352)
         OI(1, 0, 352, 512)
+        OI(1, 1, 0, 352)
         QO(0)
         QO(1)

@@ -23,6 +23,12 @@ K_PASS = P * PACK
 GROUPS = N // K_PASS
 HALVES = D // K_PASS
 TILES = GROUPS * PACK
+PAIRS = TILES // 2
+LAST = PAIRS - 1
+HE_COLS = 256
+HE_ITEMS = GROUPS * HALVES
+EX_BUFS = 3
+HE_BUFS = 4
 
 
 def tile_dampedsoftmaxfisherproduct_kernel(tc, h, g, w_words, w_scales, v, e, rho, lam, out_0, out_1, out_2):
@@ -35,20 +41,20 @@ def tile_dampedsoftmaxfisherproduct_kernel(tc, h, g, w_words, w_scales, v, e, rh
             return sb.tile(shape, dtype, name=name, align_bytes=64)
 
         banks = [ps.tile([P, 512], F32, name="bank%d" % b) for b in range(8)]
-        ring = banks[0:4]
-        z_banks = banks[4:6]
-        u_banks = banks[6:8]
-        k_banks = banks
+        t_banks = banks[0:2]
+        z_banks = banks[2:4]
+        u_banks = banks[4:6]
+        d_banks = banks[6:8]
 
         ident = tile("ident", [P, P], F32)
-        warm = tile("warm", [P, 1], F32)
         g_sb = tile("g_sb", [P, HALVES, PACK], BF16)
         vec_rows = tile("vec_rows", [P, K_PASS], BF16)
-        lam_e = tile("lam_e", [P, HALVES + GROUPS, PACK], F32)
+        lam32 = tile("lam32", [P, HALVES * PACK], F32)
+        e32 = tile("e32", [P, TILES], F32)
         rho_neg = tile("rho_neg", [P, TILES], F32)
-        diag = tile("diag", [P, TILES, P], BF16)
-        h_sb = [tile("h%d" % G, [P, PACK, D], BF16) for G in range(GROUPS)]
-        v_sb = tile("v_sb", [P, HALVES, PACK, A], BF16)
+        diag = [tile("diag%d" % G, [P, PACK, P], BF16) for G in range(GROUPS)]
+        h_sb = [tile("h%d" % j, [P, 2, D], BF16) for j in range(PAIRS)]
+        v_sb = [tile("v%d" % gh, [P, PACK, A], BF16) for gh in range(HALVES)]
         w_codes = tile("w_codes", [P, HALVES, 2 * A], U8)
         w_plane = tile("w_plane", [P, HALVES, A], U8)
         v_codes = tile("v_codes", [P, HALVES, A], U32)
@@ -56,17 +62,15 @@ def tile_dampedsoftmaxfisherproduct_kernel(tc, h, g, w_words, w_scales, v, e, rh
         f_bf = [tile("f_bf%d" % b, [P, 2, HALVES, P, PACK], BF16) for b in range(2)]
         f_codes = tile("f_codes", [P, TILES, HALVES, P], U32)
         f_plane = tile("f_plane", [P, TILES, HALVES, P], U8)
-        he_bf = [tile("he_bf%d" % b, [P, PACK, P, PACK], BF16) for b in range(3)]
-        he_codes = tile("he_codes", [P, GROUPS, HALVES, K_PASS], U32)
-        he_plane = tile("he_plane", [P, GROUPS, HALVES, K_PASS], U8)
+        he_bf = [tile("he_bf%d" % b, [P, PACK, P, PACK], BF16) for b in range(HE_BUFS)]
+        he_codes = tile("he_codes", [P, HE_ITEMS, K_PASS], U32)
+        he_plane = tile("he_plane", [P, HE_ITEMS, K_PASS], U8)
         ex = [tile("ex%d" % b, [P, PACK, A], F32) for b in range(2)]
         eu = [tile("eu%d" % b, [P, PACK, A], F32) for b in range(2)]
         y_bf = [tile("y_bf%d" % b, [P, A, PACK], BF16) for b in range(2)]
-        y_rows = [tile("y_rows%d" % b, [P, PACK, A], BF16) for b in range(2)]
-        ks = [tile("ks%d" % b, [P, A], F32) for b in range(2)]
         y_codes = tile("y_codes", [P, GROUPS, A], U32)
         y_plane = tile("y_plane", [P, GROUPS, A], U8)
-        res = tile("res", [P, HALVES, PACK, A], F32)
+        res = [tile("res%d" % gh, [P, PACK, A], F32) for gh in range(HALVES)]
         wide_bf = [tile("wide_bf%d" % b, [P, A, PACK], BF16) for b in range(2)]
         o_codes = tile("o_codes", [P, HALVES, A], U32)
         o_plane = tile("o_plane", [P, HALVES, A], U8)
@@ -77,8 +81,13 @@ def tile_dampedsoftmaxfisherproduct_kernel(tc, h, g, w_words, w_scales, v, e, rh
         acc = tile("acc", [P, TILES], F32)
         shift = tile("shift", [P, TILES], F32)
 
-        lam32 = lam_e[:, :HALVES, :].rearrange("p c t -> p (c t)")
-        e32 = lam_e[:, HALVES:, :].rearrange("p c t -> p (c t)")
+        def as_words(t):
+            return t.rearrange("p s a -> p (s a)").bitcast(BF16).rearrange("p (a t) -> p a t", t=PACK)
+
+        v_bf = [as_words(res[0][:, 0:2, :]), f_bf[1][:].rearrange("p i g r t -> p (i g r) t")]
+
+        def res_row(c):
+            return res[c // PACK][:, c % PACK, :]
 
         def col(t, i):
             return t[:, i : i + 1]
@@ -86,39 +95,57 @@ def tile_dampedsoftmaxfisherproduct_kernel(tc, h, g, w_words, w_scales, v, e, rh
         def flat(ap):
             return ap.rearrange("p a t -> p (a t)")
 
-        def t_bank(i):
-            return ring[(0 if i < 2 else 2) + i % 2]
+        def h_row(i):
+            return h_sb[i // 2][:, i % 2, :]
 
-        def load_h(G, t0, t1, d0=0, d1=D):
+        def t_bank(i):
+            return (u_banks if i // 2 == 1 else t_banks)[i % 2]
+
+        def z_bank(i):
+            return {1: u_banks, LAST: t_banks}.get(i // 2, z_banks)[i % 2]
+
+        def u_bank(i):
+            return (z_banks if i // 2 == LAST else u_banks)[i % 2]
+
+        def k_bank(c):
+            return (t_banks + u_banks + z_banks + d_banks)[c]
+
+        def load_h(i0, i1):
+            G, t0 = divmod(i0, PACK)
             rows = h[G * K_PASS : (G + 1) * K_PASS, :].rearrange("(p t) d -> p t d", t=PACK)
-            nc.sync.dma_start(out=h_sb[G][:, t0:t1, d0:d1], in_=rows[:, t0:t1, d0:d1])
+            nc.sync.dma_start(out=h_sb[i0 // 2][:, i0 % 2 : i0 % 2 + i1 - i0, :], in_=rows[:, t0 : t0 + i1 - i0, :])
 
         def load_v(gh):
             rows = v[gh * K_PASS : (gh + 1) * K_PASS, :].rearrange("(p t) a -> p t a", t=PACK)
-            nc.sync.dma_start(out=v_sb[:, gh, :, :], in_=rows)
+            nc.sync.dma_start(out=v_sb[gh][:], in_=rows)
 
-        def load_vec(row0, src):
+        def load_vec(eng, row0, src):
             rows = src.rearrange("(c k) -> c k", k=K_PASS)
-            nc.sync.dma_start(out=vec_rows[row0 : row0 + rows.shape[0], :], in_=rows)
+            eng.dma_start(out=vec_rows[row0 : row0 + rows.shape[0], :], in_=rows)
 
         def vec_cols(row0, row1):
-            return u_banks[0][:, : 2 * P].bitcast(BF16).rearrange("p (u r e) -> p r u e", u=2, e=2)[:, row0:row1, :, :]
+            return z_banks[0][:, : 2 * P].bitcast(BF16).rearrange("p (u r e) -> p r u e", u=2, e=2)[:, row0:row1, :, :]
 
         def VT():
             words = vec_rows[:].bitcast(F32)
             for u in range(2):
-                nc.tensor.transpose(u_banks[0][:, u * P : (u + 1) * P], words[:, u::2], ident[:])
+                nc.tensor.transpose(z_banks[0][:, u * P : (u + 1) * P], words[:, u::2], ident[:])
 
         def VG():
             nc.vector.tensor_copy(out=g_sb[:].rearrange("p c (u e) -> p c u e", u=2), in_=vec_cols(0, 2))
 
+        def VE():
+            nc.vector.tensor_copy(out=e32[:].rearrange("p (c u e) -> p c u e", u=2, e=2), in_=vec_cols(2, 6))
+
         def VL():
-            nc.vector.tensor_copy(out=lam_e[:].rearrange("p c (u e) -> p c u e", u=2), in_=vec_cols(2, 8))
+            nc.vector.tensor_copy(out=lam32[:].rearrange("p (c u e) -> p c u e", u=2, e=2), in_=vec_cols(6, 8))
+
+        def RHO():
+            nc.vector.tensor_scalar(out=rho_neg[:].rearrange("p (c u e) -> p c u e", u=2, e=2), in0=vec_cols(8, 12), scalar1=-float(A), scalar2=None, op0=ALU.mult)
 
         def T(i):
-            G, t = divmod(i, PACK)
             bank = t_bank(i)
-            words = h_sb[G][:, t, :].bitcast(F32)
+            words = h_row(i).bitcast(F32)
             for u in range(2):
                 for gh in range(HALVES):
                     c0 = (2 * u + gh) * P
@@ -152,154 +179,146 @@ def tile_dampedsoftmaxfisherproduct_kernel(tc, h, g, w_words, w_scales, v, e, rh
                 )
 
         def Z(i):
-            stage1(i, z_banks[i % 2], lambda gh: w_codes[:, gh, :].bitcast(FP4X4), w_plane)
+            stage1(i, z_bank(i), lambda gh: w_codes[:, gh, :].bitcast(FP4X4), w_plane)
 
         def U(i):
-            stage1(i, u_banks[i % 2], lambda gh: v_codes[:, gh, :].bitcast(FP8X4), v_plane)
+            stage1(i, u_bank(i), lambda gh: v_codes[:, gh, :].bitcast(FP8X4), v_plane)
 
-        def DG(G, j):
-            bank = ring[j % 2]
+        def DG(k, b):
+            gh, G = divmod(k, GROUPS)
+            d0 = gh * K_PASS + b * HE_COLS
+            bank = d_banks[b][:].bitcast(BF16)
             for t in range(PACK):
                 nc.tensor.matmul(
-                    out=bank[:, t * P : (t + 1) * P],
-                    lhsT=diag[:, PACK * G + t, :],
-                    rhs=h_sb[G][:, t, j * P : (j + 1) * P],
+                    out=bank[:, t * HE_COLS : (t + 1) * HE_COLS],
+                    lhsT=diag[G][:, t, :],
+                    rhs=h_row(PACK * G + t)[:, d0 : d0 + HE_COLS],
                     start=True,
                     stop=True,
                 )
 
-        def HE(G, j):
-            gh, jj = divmod(j, PACK)
-            bank = ring[j % 2]
+        def HE(k, b):
+            m = HE_COLS // PACK
             nc.scalar.copy(
-                out=he_bf[(2 * G + gh) % 3][:, :, 32 * jj : 32 * (jj + 1), :],
-                in_=bank[:].rearrange("p (t m s) -> p s m t", t=PACK, s=PACK),
+                out=he_bf[k % HE_BUFS][:, :, m * b : m * (b + 1), :],
+                in_=d_banks[b][:].bitcast(BF16).rearrange("p (t m s) -> p s m t", t=PACK, s=PACK),
             )
 
-        def QH(G, gh):
+        def QH(k):
             nc.vector.quantize_mx(
-                out=he_codes[:, G, gh, :].bitcast(FP8X4),
-                scales=he_plane[:, G, gh, :],
-                in_=he_bf[(2 * G + gh) % 3][:].rearrange("p s m t -> p (s m t)"),
+                out=he_codes[:, k, :].bitcast(FP8X4),
+                scales=he_plane[:, k, :],
+                in_=he_bf[k % HE_BUFS][:].rearrange("p s m t -> p (s m t)"),
             )
 
         def QV(gh):
-            nc.vector.quantize_mx(out=v_codes[:, gh, :].bitcast(FP8X4), scales=v_plane[:, gh, :], in_=flat(wide_bf[gh][:]))
+            nc.vector.quantize_mx(out=v_codes[:, gh, :].bitcast(FP8X4), scales=v_plane[:, gh, :], in_=flat(v_bf[gh]))
 
-        def LV(c):
+        def LV(c, pool):
             gh, s = divmod(c, PACK)
-            nc.scalar.activation(out=res[:, gh, s, :], in_=v_sb[:, gh, s, :], func=ACT.Copy, scale=col(lam32, c))
+            if pool:
+                nc.gpsimd.tensor_scalar(out=res_row(c), in0=v_sb[gh][:, s, :], scalar1=col(lam32, c), scalar2=0.0, op0=ALU.mult, op1=ALU.add)
+            else:
+                nc.scalar.activation(out=res_row(c), in_=v_sb[gh][:, s, :], func=ACT.Copy, scale=col(lam32, c))
 
         def MAX(i):
-            nc.vector.tensor_reduce(out=col(neg_max, i), in_=z_banks[i % 2][:], axis=mybir.AxisListType.X, op=ALU.max, negate=True)
+            nc.vector.tensor_reduce(out=col(neg_max, i), in_=z_bank(i)[:], axis=mybir.AxisListType.X, op=ALU.max, negate=True)
 
         def row(tiles, i):
-            return tiles[(i // PACK) % len(tiles)][:, i % PACK, :]
+            return tiles[(i // PACK) % 2][:, i % PACK, :]
 
         def EXP(i):
-            nc.scalar.activation(out=row(ex, i), in_=z_banks[i % 2][:], func=ACT.Exp, bias=col(neg_max, i), accum_out=col(total, i))
+            nc.scalar.activation(out=row(ex, i), in_=z_bank(i)[:], func=ACT.Exp, bias=col(neg_max, i), accum_out=col(total, i))
 
         def R(i, n):
             nc.vector.reciprocal(out=inv[:, i : i + n], in_=total[:, i : i + n])
 
-        def small_mul(out, a, b):
-            nc.scalar.activation(out=out, in_=a, func=ACT.Copy, scale=b)
-
         def C(i):
-            small_mul(col(coef, i), col(inv, i), col(rho_neg, i))
+            nc.scalar.activation(out=col(coef, i), in_=col(inv, i), func=ACT.Copy, scale=col(rho_neg, i))
 
         def W(i):
             nc.vector.scalar_tensor_tensor(
-                out=row(eu, i), in0=u_banks[i % 2][:], scalar=col(coef, i), in1=row(ex, i),
+                out=row(eu, i), in0=u_bank(i)[:], scalar=col(coef, i), in1=row(ex, i),
                 op0=ALU.mult, op1=ALU.mult, accum_out=col(acc, i),
             )
 
         def B(i):
-            if i < 15:
-                small_mul(col(shift, i), col(acc, i), col(inv, i))
-            else:
-                nc.vector.tensor_scalar(out=col(shift, i), in0=col(acc, i), scalar1=col(inv, i), scalar2=None, op0=ALU.mult)
+            nc.scalar.activation(out=col(shift, i), in_=col(acc, i), func=ACT.Copy, scale=col(inv, i))
 
         def E2(i):
             nc.scalar.activation(out=row(ex, i), in_=row(ex, i), func=ACT.Copy, scale=col(shift, i))
 
-        def FIN(G, pool, a0, a1):
-            cols = slice(a0, a1)
-            eng = nc.gpsimd if pool else nc.vector
-            eng.tensor_tensor(
-                out=y_bf[G % 2][:, cols, :].rearrange("p (c i) t -> p c t i", i=2),
-                in0=ex[G % 3][:, :, cols].rearrange("p t (c i) -> p c t i", i=2),
-                in1=eu[G % 2][:, :, cols].rearrange("p t (c i) -> p c t i", i=2),
+        def YP(j):
+            G, u = divmod(j, 2)
+            slots = slice(2 * u, 2 * u + 2)
+            nc.gpsimd.tensor_tensor(
+                out=y_bf[G % 2][:, :, slots],
+                in0=ex[G % 2][:, slots, :].rearrange("p t a -> p a t"),
+                in1=eu[G % 2][:, slots, :].rearrange("p t a -> p a t"),
                 op=ALU.subtract,
             )
 
-        def Y(i):
-            nc.vector.scalar_tensor_tensor(
-                out=row(y_rows, i), in0=row(ex, i), scalar=col(shift, i), in1=row(eu, i),
-                op0=ALU.mult, op1=ALU.subtract,
+        def YV(G, a0, a1):
+            nc.vector.tensor_tensor(
+                out=y_bf[G % 2][:, a0:a1, :].rearrange("p (c i) t -> p c t i", i=2),
+                in0=ex[G % 2][:, :, a0:a1].rearrange("p t (c i) -> p c t i", i=2),
+                in1=eu[G % 2][:, :, a0:a1].rearrange("p t (c i) -> p c t i", i=2),
+                op=ALU.subtract,
             )
 
-        def YP(i):
-            nc.gpsimd.tensor_scalar(out=row(ex, i), in0=row(ex, i), scalar1=col(shift, i), scalar2=0.0, op0=ALU.mult, op1=ALU.add)
-            nc.gpsimd.tensor_tensor(out=row(y_rows, i), in0=row(ex, i), in1=row(eu, i), op=ALU.subtract)
+        def runs(dst, src, a0, a1, run):
+            return (dst[:, a0:a1, :].rearrange("p (c i) t -> p c t i", i=run), src[:, :, a0:a1].rearrange("p t (c i) -> p c t i", i=run))
 
-        def il(eng, dst, src, a0, a1, run):
-            out = dst[:, a0:a1, :].rearrange("p (c i) t -> p c t i", i=run)
-            in_ = src[:, :, a0:a1].rearrange("p t (c i) -> p c t i", i=run)
-            if eng == "A":
-                nc.scalar.copy(out=out, in_=in_)
+        def VI(gh, pool):
+            if pool:
+                nc.gpsimd.tensor_scalar(out=v_bf[gh], in0=v_sb[gh][:].rearrange("p t a -> p a t"), scalar1=1.0, scalar2=0.0, op0=ALU.mult, op1=ALU.add)
             else:
-                nc.vector.tensor_copy(out=out, in_=in_)
-
-        def VI(gh, vec, a0, a1):
-            il("V" if vec else "A", wide_bf[gh], v_sb[:, gh, :, :], a0, a1, 4)
-
-        def YI(G, vec, a0, a1):
-            il("V" if vec else "A", y_bf[G % 2], y_rows[G % 2], a0, a1, 4)
+                out, in_ = runs(v_bf[gh], v_sb[gh], 0, A, 4)
+                nc.scalar.copy(out=out, in_=in_)
 
         def OI(gh, vec, a0, a1):
-            il("V" if vec else "A", wide_bf[gh], res[:, gh, :, :], a0, a1, 2)
+            out, in_ = runs(wide_bf[gh], res[gh], a0, a1, 2)
+            if vec:
+                nc.vector.tensor_copy(out=out, in_=in_)
+            else:
+                nc.scalar.copy(out=out, in_=in_)
 
-        def DIAG(i):
-            nc.scalar.activation(out=diag[:, i, :], in_=ident[:], func=ACT.Copy, scale=col(e32, i))
+        def OP(gh, a0, a1):
+            nc.gpsimd.tensor_scalar(out=wide_bf[gh][:, a0:a1, :], in0=res[gh][:, :, a0:a1].rearrange("p t a -> p a t"), scalar1=1.0, scalar2=0.0, op0=ALU.mult, op1=ALU.add)
 
+        def DIAG(i, scalar):
+            out = diag[i // PACK][:, i % PACK, :]
+            if scalar:
+                nc.scalar.activation(out=out, in_=ident[:], func=ACT.Copy, scale=col(e32, i))
+            else:
+                nc.vector.tensor_scalar(out=out, in0=ident[:], scalar1=col(e32, i), scalar2=None, op0=ALU.mult)
 
-        def RHO():
-            nc.vector.tensor_scalar(out=rho_neg[:].rearrange("p (c u e) -> p c u e", u=2, e=2), in0=vec_cols(8, 12), scalar1=-float(A), scalar2=None, op0=ALU.mult)
-
-
-        def QY(G):
-            nc.vector.quantize_mx(out=y_codes[:, G, :].bitcast(FP8X4), scales=y_plane[:, G, :], in_=flat(y_bf[G % 2][:]))
+        def QY(G, a0, a1):
+            nc.vector.quantize_mx(out=y_codes[:, G, a0:a1].bitcast(FP8X4), scales=y_plane[:, G, a0:a1], in_=flat(y_bf[G % 2][:, a0:a1, :]))
 
         def K(c, G):
             gh, s = divmod(c, PACK)
+            k = gh * GROUPS + G
             nc.tensor.matmul_mx(
-                out=k_banks[c][:],
-                lhsT=he_codes[:, G, gh, s * P : (s + 1) * P].bitcast(FP8X4),
-                lhsT_scale=he_plane[:, G, gh, s * P : (s + 1) * P],
+                out=k_bank(c)[:],
+                lhsT=he_codes[:, k, s * P : (s + 1) * P].bitcast(FP8X4),
+                lhsT_scale=he_plane[:, k, s * P : (s + 1) * P],
                 rhs=y_codes[:, G, :].bitcast(FP8X4),
                 rhs_scale=y_plane[:, G, :],
                 start=(G == 0),
                 stop=(G == GROUPS - 1),
             )
 
-        def EP(c, a0, a1):
+        def EP(c):
             gh, s = divmod(c, PACK)
             nc.vector.scalar_tensor_tensor(
-                out=res[:, gh, s, a0:a1], in0=k_banks[c][:, a0:a1], scalar=1.0 / math.sqrt(N), in1=res[:, gh, s, a0:a1],
+                out=res_row(c), in0=k_bank(c)[:], scalar=1.0 / math.sqrt(N), in1=res_row(c),
                 op0=ALU.mult, op1=ALU.add,
             )
 
-        def EA(c):
-            nc.scalar.activation(out=ks[c % 2][:], in_=k_banks[c][:], func=ACT.Copy, scale=1.0 / math.sqrt(N))
-
-        def EG(c):
-            gh, s = divmod(c, PACK)
-            nc.gpsimd.tensor_tensor(out=res[:, gh, s, :], in0=ks[c % 2][:], in1=res[:, gh, s, :], op=ALU.add)
-
         def ST(gh, s):
             rows = out_0[gh * K_PASS : (gh + 1) * K_PASS, :].rearrange("(p t) a -> p t a", t=PACK)
-            nc.sync.dma_start(out=rows[:, s : s + 2, :], in_=res[:, gh, s : s + 2, :])
+            nc.sync.dma_start(out=rows[:, s : s + 2, :], in_=res[gh][:, s : s + 2, :])
 
         def QO(gh):
             nc.vector.quantize_mx(out=o_codes[:, gh, :].bitcast(FP8X4), scales=o_plane[:, gh, :], in_=flat(wide_bf[gh][:]))
@@ -317,378 +336,190 @@ def tile_dampedsoftmaxfisherproduct_kernel(tc, h, g, w_words, w_scales, v, e, rh
                         in_=o_plane[32 * Q : 32 * Q + 4, :, :].bitcast(I32),
                     )
 
+        def both(step, j):
+            if 0 <= j < PAIRS:
+                step(2 * j)
+                step(2 * j + 1)
+
         ctx.enter_context(tc.manual_schedule())
 
-        nc.gpsimd.memset(vec_rows[:].bitcast(U32), 0)
-        nc.vector.memset(warm[:], 0.0)
+        nc.vector.memset(vec_rows[:].bitcast(U32), 0)
         nc.vector.memset(w_plane[:].rearrange("p g a -> p (g a)").bitcast(U32), 0)
         make_identity(nc, ident[:])
-        load_vec(0, g)
-        load_vec(2, lam)
-        load_vec(4, e)
-        load_vec(8, rho)
-        load_h(0, 0, 1)
-        load_h(0, 1, 2)
-        load_h(0, 2, 4)
+        load_h(0, 1)
+        load_h(1, 2)
+        load_vec(nc.scalar, 0, g)
+        load_vec(nc.scalar, 2, e)
+        load_h(2, 4)
         nc.sync.dma_start(out=w_codes[:].bitcast(I32), in_=w_words.rearrange("g p n -> p g n").bitcast(I32))
-        nc.scalar.activation(out=warm[:], in_=warm[:], func=ACT.Exp)
         load_v(0)
+        load_v(1)
         for Q in range(4):
             nc.scalar.dma_start(
                 out=w_plane[32 * Q : 32 * Q + 4, :, :].bitcast(I32),
                 in_=w_scales[:, 4 * Q : 4 * Q + 4, :].rearrange("g q a -> q g a").bitcast(I32),
             )
-        load_h(1, 0, 2)
-        load_v(1)
-        load_h(1, 2, 4)
-        load_h(2, 0, PACK)
-        load_h(3, 0, PACK)
-
-        VT()
-        VL()
-        DIAG(3)
-        DIAG(1)
-        RHO()
-        DIAG(0)
+        load_h(4, 6)
+        load_h(6, 8)
         T(0)
-        DIAG(11)
+        VT()
         VG()
+        VE()
+        load_vec(nc.sync, 6, lam)
+        load_vec(nc.sync, 8, rho)
+        for j in range(4, PAIRS):
+            load_h(2 * j, 2 * j + 2)
+
+        for i in range(2 * PACK, TILES):
+            DIAG(i, True)
         T(1)
-        T(3)
-        T(2)
-        DIAG(5)
-        F(0)
-        F(1)
-        DIAG(7)
-        QF(0, 1)
-        DIAG(2)
+        both(T, 1)
+        both(F, 0)
+        for i in range(PACK):
+            DIAG(i, False)
+        QF(0, 2)
         DG(0, 0)
-        QF(1, 1)
-        VI(0, 0, 0, 512)
-        F(3)
-        DG(0, 1)
-        Z(1)
-        F(2)
+        both(Z, 0)
+        both(F, 1)
+        for i in range(PACK, 2 * PACK):
+            DIAG(i, False)
         QF(2, 2)
-        Z(0)
-        T(5)
-        MAX(1)
-        MAX(0)
-        T(4)
-        F(5)
-        F(4)
-        HE(0, 0)
-        QV(0)
-        DG(0, 2)
-        HE(0, 1)
-        EXP(1)
-        QF(4, 2)
-        T(7)
-        T(6)
-        F(7)
-        Z(3)
-        EXP(0)
-        Z(2)
-        T(9)
-        VI(1, 0, 256, 512)
-        F(6)
-        T(8)
-        MAX(3)
-        VI(1, 0, 0, 256)
-        MAX(2)
-        DIAG(12)
-        R(0, 1)
-        EXP(3)
-        F(9)
-        EXP(2)
-        DG(0, 3)
-        DIAG(13)
-        F(8)
-        HE(0, 2)
-        Z(5)
-        DIAG(14)
-        C(0)
-        Z(4)
+        both(Z, 1)
+        VI(0, False)
+        VI(1, True)
+        both(T, 2)
+        DG(0, 1)
+
+        for j in range(2):
+            both(MAX, j)
+            both(EXP, j)
+        VT()
+        both(F, 2)
+        both(T, 3)
         QV(1)
-        R(1, 1)
-        MAX(5)
-        HE(0, 3)
-        C(1)
-        U(1)
-        QF(8, 2)
-        DG(0, 4)
-        DIAG(10)
-        MAX(4)
-        DIAG(6)
-        DG(0, 5)
-        R(2, 2)
-        W(1)
-        DIAG(15)
-        DIAG(4)
-        QF(6, 2)
-        HE(0, 4)
-        HE(0, 5)
-        U(0)
-        T(11)
-        EXP(5)
-        T(10)
-        W(0)
-        DG(0, 6)
-        B(1)
-        Z(7)
-        EXP(4)
-        Z(6)
-        Y(1)
-        C(2)
-        B(0)
-        U(3)
-        F(10)
-        LV(4)
-        LV(5)
-        YP(0)
-        DG(0, 7)
-        MAX(7)
-        HE(0, 6)
-        U(2)
+        RHO()
+        VL()
+        R(0, 4)
+        QF(4, 2)
+        QV(0)
+        HE(0, 0)
         DG(1, 0)
-        QH(0, 0)
-        F(11)
-        EXP(7)
-        HE(0, 7)
-        Z(9)
-        HE(1, 0)
-        R(4, 2)
+        both(U, 0)
+        for c in range(PACK - 1):
+            LV(c, True)
+        HE(0, 1)
+        both(C, 0)
+        LV(PACK - 1, False)
         DG(1, 1)
-        DIAG(8)
-        W(2)
-        T(12)
-        C(5)
-        T(13)
-        DG(1, 2)
-        C(4)
+        both(Z, 2)
+        both(F, 3)
+        both(W, 0)
+        both(U, 1)
+        HE(1, 0)
+        both(B, 0)
         HE(1, 1)
-        C(3)
-        MAX(6)
-        B(2)
-        EXP(6)
-        QH(0, 1)
-        DIAG(9)
-        YP(2)
-        QF(10, 2)
-        HE(1, 2)
-        W(3)
-        DG(1, 3)
-        Z(8)
-        HE(1, 3)
-        MAX(9)
-        U(4)
-        DG(1, 4)
-        B(3)
-        EXP(9)
-        DG(1, 5)
-        HE(1, 4)
-        F(13)
-        HE(1, 5)
-        U(5)
-        MAX(8)
-        Z(11)
-        DG(1, 6)
-        W(4)
-        F(12)
-        Y(3)
-        B(4)
-        R(6, 2)
-        EXP(8)
-        DG(1, 7)
-        W(5)
-        HE(1, 6)
-        U(6)
-        R(8, 2)
-        Z(10)
-        YI(0, 0, 128, 256)
-        C(6)
+        both(C, 1)
+        both(E2, 0)
+        QH(0)
+        QF(6, 2)
+        YP(0)
+        both(T, 4)
         DG(2, 0)
-        B(5)
-        HE(1, 7)
-        YI(0, 0, 256, 384)
-        C(8)
-        T(15)
-        QF(12, 2)
-        MAX(11)
-        MAX(10)
-        U(7)
-        HE(2, 0)
-        W(6)
-        C(7)
-        EXP(10)
         DG(2, 1)
-        QH(1, 0)
-        Y(5)
-        B(6)
-        F(15)
-        EXP(11)
-        YP(4)
-        T(14)
-        DG(2, 2)
-        HE(2, 1)
-        U(8)
-        C(9)
-        DG(2, 3)
-        W(7)
-        HE(2, 2)
-        Z(12)
-        W(8)
-        YI(0, 0, 0, 128)
-        B(7)
-        HE(2, 3)
-        DG(2, 4)
-        U(9)
-        F(14)
-        YP(6)
-        DG(2, 5)
-        R(10, 2)
-        YI(0, 0, 384, 512)
-        HE(2, 4)
-        Z(13)
-        MAX(12)
-        Y(7)
-        C(10)
-        QF(14, 2)
-        DG(2, 6)
-        MAX(13)
-        U(10)
-        EXP(12)
-        W(9)
-        B(8)
-        QH(1, 1)
-        HE(2, 5)
-        HE(2, 6)
-        YP(8)
-        Z(14)
-        DG(2, 7)
-        C(11)
-        W(10)
-        EXP(13)
-        YI(1, 0, 0, 128)
-        YI(1, 0, 128, 256)
-        HE(2, 7)
-        DG(3, 0)
-        U(11)
-        MAX(14)
-        W(11)
-        B(10)
-        Z(15)
-        DG(3, 1)
-        HE(3, 0)
-        QH(2, 0)
-        MAX(15)
-        R(12, 2)
-        QY(0)
-        EXP(14)
-        HE(3, 1)
-        YI(1, 0, 256, 384)
-        U(12)
-        C(12)
-        U(13)
-        DG(3, 3)
-        DG(3, 2)
-        EXP(15)
-        C(13)
-        W(12)
-        YI(1, 0, 384, 512)
-        B(9)
-        K(2, 0)
-        B(11)
-        HE(3, 2)
-        U(14)
-        DG(3, 4)
-        HE(3, 3)
-        R(14, 2)
-        W(13)
-        QY(1)
-        C(15)
-        C(14)
-        LV(2)
-        B(12)
-        DG(3, 5)
-        Y(9)
-        Y(11)
-        U(15)
-        B(13)
-        HE(3, 4)
-        W(14)
-        K(3, 0)
-        W(15)
-        DG(3, 6)
-        K(6, 0)
-        HE(3, 5)
-        YP(10)
-        YI(2, 0, 0, 256)
-        Y(13)
-        B(14)
-        Y(12)
-        K(5, 0)
-        B(15)
-        Y(14)
-        K(7, 0)
-        YI(2, 0, 256, 512)
-        K(4, 0)
-        K(4, 1)
-        HE(3, 6)
-        DG(3, 7)
-        K(6, 1)
-        K(2, 1)
-        HE(3, 7)
-        Y(15)
-        K(3, 1)
-        YI(3, 0, 160, 512)
-        K(5, 1)
-        K(0, 0)
-        QY(2)
-        K(1, 0)
-        YI(3, 1, 0, 160)
-        LV(1)
-        K(0, 1)
-        K(1, 1)
-        K(0, 2)
-        K(3, 2)
-        QH(3, 0)
-        K(7, 1)
-        LV(3)
-        QH(3, 1)
-        K(2, 2)
-        K(1, 2)
-        QY(3)
-        K(1, 3)
-        QH(2, 1)
-        K(0, 3)
-        K(2, 3)
-        K(6, 2)
-        K(7, 2)
-        EP(1, 0, 512)
-        LV(0)
-        LV(7)
-        EP(0, 0, 512)
-        K(3, 3)
-        ST(0, 0)
-        LV(6)
-        EP(2, 0, 512)
-        K(6, 3)
-        EP(3, 0, 512)
-        K(7, 3)
-        EP(7, 0, 512)
-        EP(6, 0, 512)
-        ST(0, 2)
-        K(4, 2)
-        K(4, 3)
-        K(5, 2)
-        K(5, 3)
-        ST(1, 2)
-        EP(4, 0, 512)
-        EP(5, 0, 512)
-        OI(0, 0, 0, 512)
-        ST(1, 0)
-        OI(1, 0, 352, 512)
-        OI(1, 1, 0, 352)
+
+        for j in range(2, PAIRS - 2):
+            both(MAX, j)
+            both(EXP, j)
+            both(Z, j + 1)
+            both(W, j - 1)
+            both(U, j)
+            R(2 * j, 2)
+            both(F, j + 2)
+            HE(j, 0)
+            both(B, j - 1)
+            HE(j, 1)
+            both(C, j)
+            both(E2, j - 1)
+            QH(j - 1)
+            QF(2 * (j + 2), 2)
+            if j >= 3:
+                G, half = divmod(j - 3, 2)
+                QY(G, half * A // 2, (half + 1) * A // 2)
+            YP(j - 1)
+            if j + 3 < PAIRS:
+                both(T, j + 3)
+            DG(j + 1, 0)
+            DG(j + 1, 1)
+
+        QY(1, A // 2, A)
+        j = LAST - 1
+        both(MAX, j)
+        both(EXP, j)
+        both(Z, LAST)
+        both(W, j - 1)
+        both(U, j)
+        both(U, LAST)
+        R(2 * j, 2)
+        both(MAX, LAST)
+        B(2 * j - 2)
+        E2(2 * j - 2)
+        B(2 * j - 1)
+        both(C, j)
+        E2(2 * j - 1)
+        YP(j - 1)
+        both(EXP, LAST)
+        both(W, j)
+        R(2 * LAST, 2)
+        both(B, j)
+        both(C, LAST)
+        both(E2, j)
+        both(W, LAST)
+        both(B, LAST)
+        both(E2, LAST)
+        for c in range(0, PACK, 2):
+            for G in range(2):
+                K(c, G)
+                K(c + 1, G)
+        QH(HE_ITEMS - 3)
+        K(PACK, 0)
+        K(PACK + 1, 0)
+        K(PACK, 1)
+        K(PACK + 1, 1)
+        QY(GROUPS - 2, 0, A)
+        for c in range(PACK):
+            K(c, GROUPS - 2)
+        YV(GROUPS - 1, 0, A)
+        for b in range(2):
+            HE(HE_ITEMS - 2, b)
+            DG(HE_ITEMS - 1, b)
+        QY(GROUPS - 1, 0, A)
+        QH(HE_ITEMS - 2)
+        for b in range(2):
+            HE(HE_ITEMS - 1, b)
+        for c in range(PACK, 2 * PACK):
+            LV(c, False)
+        for c in range(PACK):
+            K(c, GROUPS - 1)
+        K(PACK, 2)
+        K(PACK + 1, 2)
+        for c in range(PACK):
+            EP(c)
+            if c == 0:
+                QH(HE_ITEMS - 1)
+            if c % 2 == 1:
+                ST(0, c - 1)
+        OI(0, False, 0, A // 2)
+        OP(0, A // 2, A)
+        K(PACK, GROUPS - 1)
+        K(PACK + 1, GROUPS - 1)
+        for c in range(PACK + 2, 2 * PACK):
+            for G in range(GROUPS):
+                K(c, G)
+        for c in range(PACK, 2 * PACK):
+            EP(c)
+            if c % 2 == 1:
+                ST(1, c - 1 - PACK)
+        OI(1, False, A // 2, A)
         QO(0)
+        OI(1, True, 0, A // 2)
         QO(1)

@@ -27,8 +27,9 @@ PAIRS = TILES // 2
 LAST = PAIRS - 1
 HE_COLS = 256
 HE_ITEMS = GROUPS * HALVES
-EX_BUFS = 3
-HE_BUFS = 4
+STAGE_BUFS = 3
+F_LEAD = 3
+HALF_A = A // 2
 
 
 def tile_dampedsoftmaxfisherproduct_kernel(tc, h, g, w_words, w_scales, v, e, rho, lam, out_0, out_1, out_2):
@@ -59,18 +60,15 @@ def tile_dampedsoftmaxfisherproduct_kernel(tc, h, g, w_words, w_scales, v, e, rh
         w_plane = tile("w_plane", [P, HALVES, A], U8)
         v_codes = tile("v_codes", [P, HALVES, A], U32)
         v_plane = tile("v_plane", [P, HALVES, A], U8)
-        f_bf = [tile("f_bf%d" % b, [P, 2, HALVES, P, PACK], BF16) for b in range(2)]
-        f_codes = tile("f_codes", [P, TILES, HALVES, P], U32)
-        f_plane = tile("f_plane", [P, TILES, HALVES, P], U8)
-        he_bf = [tile("he_bf%d" % b, [P, PACK, P, PACK], BF16) for b in range(HE_BUFS)]
-        he_codes = tile("he_codes", [P, HE_ITEMS, K_PASS], U32)
-        he_plane = tile("he_plane", [P, HE_ITEMS, K_PASS], U8)
+        stage = [tile("stage%d" % b, [P, 2, K_PASS * PACK], BF16) for b in range(STAGE_BUFS)]
+        codes = tile("codes", [P, PAIRS, 2, K_PASS], U32)
+        plane = tile("plane", [P, PAIRS, 2, K_PASS], U8)
         ex = [tile("ex%d" % b, [P, PACK, A], F32) for b in range(2)]
         eu = [tile("eu%d" % b, [P, PACK, A], F32) for b in range(2)]
         y_bf = [tile("y_bf%d" % b, [P, A, PACK], BF16) for b in range(2)]
         y_codes = tile("y_codes", [P, GROUPS, A], U32)
         y_plane = tile("y_plane", [P, GROUPS, A], U8)
-        res = [tile("res%d" % gh, [P, PACK, A], F32) for gh in range(HALVES)]
+        res = [tile("res%d" % gh, [P, 2, PACK, HALF_A], F32) for gh in range(HALVES)]
         wide_bf = [tile("wide_bf%d" % b, [P, A, PACK], BF16) for b in range(2)]
         o_codes = tile("o_codes", [P, HALVES, A], U32)
         o_plane = tile("o_plane", [P, HALVES, A], U8)
@@ -81,13 +79,20 @@ def tile_dampedsoftmaxfisherproduct_kernel(tc, h, g, w_words, w_scales, v, e, rh
         acc = tile("acc", [P, TILES], F32)
         shift = tile("shift", [P, TILES], F32)
 
+        def f_unit(j):
+            return (j - F_LEAD) % PAIRS
+
+        def f_cols(t, i, gh):
+            c0 = (i % 2 * HALVES + gh) * P
+            return t[:, f_unit(i // 2), 1, c0 : c0 + P]
+
         def as_words(t):
             return t.rearrange("p s a -> p (s a)").bitcast(BF16).rearrange("p (a t) -> p a t", t=PACK)
 
-        v_bf = [as_words(res[0][:, 0:2, :]), f_bf[1][:].rearrange("p i g r t -> p (i g r) t")]
+        v_bf = [as_words(res[0][:, 0, :, :]), stage[f_unit(1) % STAGE_BUFS][:, 1, :].rearrange("p (a t) -> p a t", t=PACK)]
 
         def res_row(c):
-            return res[c // PACK][:, c % PACK, :]
+            return res[c // PACK][:, :, c % PACK, :]
 
         def col(t, i):
             return t[:, i : i + 1]
@@ -119,9 +124,9 @@ def tile_dampedsoftmaxfisherproduct_kernel(tc, h, g, w_words, w_scales, v, e, rh
             rows = v[gh * K_PASS : (gh + 1) * K_PASS, :].rearrange("(p t) a -> p t a", t=PACK)
             nc.sync.dma_start(out=v_sb[gh][:], in_=rows)
 
-        def load_vec(eng, row0, src):
+        def load_vec(row0, src):
             rows = src.rearrange("(c k) -> c k", k=K_PASS)
-            eng.dma_start(out=vec_rows[row0 : row0 + rows.shape[0], :], in_=rows)
+            nc.sync.dma_start(out=vec_rows[row0 : row0 + rows.shape[0], :], in_=rows)
 
         def vec_cols(row0, row1):
             return z_banks[0][:, : 2 * P].bitcast(BF16).rearrange("p (u r e) -> p r u e", u=2, e=2)[:, row0:row1, :, :]
@@ -153,27 +158,33 @@ def tile_dampedsoftmaxfisherproduct_kernel(tc, h, g, w_words, w_scales, v, e, rh
 
         def F(i):
             nc.vector.tensor_tensor(
-                out=f_bf[(i // 2) % 2][:, i % 2, :, :, :].rearrange("p g r (u e) -> p g r u e", u=2),
+                out=stage[f_unit(i // 2) % STAGE_BUFS][:, 1, i % 2 * D : (i % 2 + 1) * D].rearrange("p (g r u e) -> p g r u e", g=HALVES, u=2, e=2),
                 in0=t_bank(i)[:].bitcast(BF16).rearrange("p (u g r e) -> p g r u e", u=2, g=HALVES, e=2),
                 in1=g_sb[:].rearrange("p g (o u e) -> p g o u e", o=1, u=2).to_broadcast([P, HALVES, P, 2, 2]),
                 op=ALU.mult,
             )
 
-        def QF(i, n):
+        def Q(unit, part0, part1):
             nc.vector.quantize_mx(
-                out=f_codes[:, i : i + n, :, :].rearrange("p i g r -> p (i g r)").bitcast(FP8X4),
-                scales=f_plane[:, i : i + n, :, :].rearrange("p i g r -> p (i g r)"),
-                in_=f_bf[(i // 2) % 2][:, i % 2 : i % 2 + n, :, :, :].rearrange("p i g r t -> p (i g r t)"),
+                out=codes[:, unit, part0:part1, :].rearrange("p h c -> p (h c)").bitcast(FP8X4),
+                scales=plane[:, unit, part0:part1, :].rearrange("p h c -> p (h c)"),
+                in_=stage[unit % STAGE_BUFS][:, part0:part1, :].rearrange("p h c -> p (h c)"),
             )
 
-        def stage1(i, bank, codes, plane):
+        def QF(j):
+            Q(f_unit(j), 1, 2)
+
+        def QH(k):
+            Q(k, 0, 1)
+
+        def stage1(i, bank, rhs_codes, rhs_plane):
             for gh in range(HALVES):
                 nc.tensor.matmul_mx(
                     out=bank[:],
-                    lhsT=f_codes[:, i, gh, :].bitcast(FP8X4),
-                    lhsT_scale=f_plane[:, i, gh, :],
-                    rhs=codes(gh),
-                    rhs_scale=plane[:, gh, :],
+                    lhsT=f_cols(codes, i, gh).bitcast(FP8X4),
+                    lhsT_scale=f_cols(plane, i, gh),
+                    rhs=rhs_codes(gh),
+                    rhs_scale=rhs_plane[:, gh, :],
                     start=(gh == 0),
                     stop=(gh == HALVES - 1),
                 )
@@ -197,18 +208,11 @@ def tile_dampedsoftmaxfisherproduct_kernel(tc, h, g, w_words, w_scales, v, e, rh
                     stop=True,
                 )
 
-        def HE(k, b):
+        def HE(k, b, s0=0, s1=PACK):
             m = HE_COLS // PACK
             nc.scalar.copy(
-                out=he_bf[k % HE_BUFS][:, :, m * b : m * (b + 1), :],
-                in_=d_banks[b][:].bitcast(BF16).rearrange("p (t m s) -> p s m t", t=PACK, s=PACK),
-            )
-
-        def QH(k):
-            nc.vector.quantize_mx(
-                out=he_codes[:, k, :].bitcast(FP8X4),
-                scales=he_plane[:, k, :],
-                in_=he_bf[k % HE_BUFS][:].rearrange("p s m t -> p (s m t)"),
+                out=stage[k % STAGE_BUFS][:, 0, :].rearrange("p (s m t) -> p s m t", s=PACK, t=PACK)[:, s0:s1, m * b : m * (b + 1), :],
+                in_=d_banks[b][:].bitcast(BF16).rearrange("p (t m s) -> p s m t", t=PACK, s=PACK)[:, s0:s1, :, :],
             )
 
         def QV(gh):
@@ -217,9 +221,9 @@ def tile_dampedsoftmaxfisherproduct_kernel(tc, h, g, w_words, w_scales, v, e, rh
         def LV(c, pool):
             gh, s = divmod(c, PACK)
             if pool:
-                nc.gpsimd.tensor_scalar(out=res_row(c), in0=v_sb[gh][:, s, :], scalar1=col(lam32, c), scalar2=0.0, op0=ALU.mult, op1=ALU.add)
+                nc.gpsimd.tensor_scalar(out=res_row(c), in0=v_sb[gh][:, s, :].rearrange("p (h a) -> p h a", h=2), scalar1=col(lam32, c), scalar2=0.0, op0=ALU.mult, op1=ALU.add)
             else:
-                nc.scalar.activation(out=res_row(c), in_=v_sb[gh][:, s, :], func=ACT.Copy, scale=col(lam32, c))
+                nc.scalar.activation(out=res_row(c), in_=v_sb[gh][:, s, :].rearrange("p (h a) -> p h a", h=2), func=ACT.Copy, scale=col(lam32, c))
 
         def MAX(i):
             nc.vector.tensor_reduce(out=col(neg_max, i), in_=z_bank(i)[:], axis=mybir.AxisListType.X, op=ALU.max, negate=True)
@@ -244,6 +248,15 @@ def tile_dampedsoftmaxfisherproduct_kernel(tc, h, g, w_words, w_scales, v, e, rh
 
         def B(i):
             nc.scalar.activation(out=col(shift, i), in_=col(acc, i), func=ACT.Copy, scale=col(inv, i))
+
+        def BV(i):
+            nc.vector.tensor_tensor(out=col(shift, i), in0=col(acc, i), in1=col(inv, i), op=ALU.mult)
+
+        def E2P(i):
+            nc.gpsimd.tensor_scalar(out=row(ex, i), in0=row(ex, i), scalar1=col(acc, i), scalar2=col(inv, i), op0=ALU.mult, op1=ALU.mult)
+
+        def E2V(i):
+            nc.vector.tensor_scalar(out=row(ex, i), in0=row(ex, i), scalar1=col(acc, i), scalar2=col(inv, i), op0=ALU.mult, op1=ALU.mult)
 
         def E2(i):
             nc.scalar.activation(out=row(ex, i), in_=row(ex, i), func=ACT.Copy, scale=col(shift, i))
@@ -276,15 +289,15 @@ def tile_dampedsoftmaxfisherproduct_kernel(tc, h, g, w_words, w_scales, v, e, rh
                 out, in_ = runs(v_bf[gh], v_sb[gh], 0, A, 4)
                 nc.scalar.copy(out=out, in_=in_)
 
-        def OI(gh, vec, a0, a1):
-            out, in_ = runs(wide_bf[gh], res[gh], a0, a1, 2)
+        def OI(gh, half, vec, a0, a1):
+            out, in_ = runs(wide_bf[gh][:, half * HALF_A : (half + 1) * HALF_A, :], res[gh][:, half, :, :], a0, a1, 2)
             if vec:
                 nc.vector.tensor_copy(out=out, in_=in_)
             else:
                 nc.scalar.copy(out=out, in_=in_)
 
-        def OP(gh, a0, a1):
-            nc.gpsimd.tensor_scalar(out=wide_bf[gh][:, a0:a1, :], in0=res[gh][:, :, a0:a1].rearrange("p t a -> p a t"), scalar1=1.0, scalar2=0.0, op0=ALU.mult, op1=ALU.add)
+        def OP(gh, half):
+            nc.gpsimd.tensor_scalar(out=wide_bf[gh][:, half * HALF_A : (half + 1) * HALF_A, :], in0=res[gh][:, half, :, :].rearrange("p t a -> p a t"), scalar1=1.0, scalar2=0.0, op0=ALU.mult, op1=ALU.add)
 
         def DIAG(i, scalar):
             out = diag[i // PACK][:, i % PACK, :]
@@ -296,45 +309,49 @@ def tile_dampedsoftmaxfisherproduct_kernel(tc, h, g, w_words, w_scales, v, e, rh
         def QY(G, a0, a1):
             nc.vector.quantize_mx(out=y_codes[:, G, a0:a1].bitcast(FP8X4), scales=y_plane[:, G, a0:a1], in_=flat(y_bf[G % 2][:, a0:a1, :]))
 
-        def K(c, G):
-            gh, s = divmod(c, PACK)
+        def K(b, G):
+            gh, half, pair = b // 4, b // 2 % 2, b % 2
             k = gh * GROUPS + G
-            nc.tensor.matmul_mx(
-                out=k_bank(c)[:],
-                lhsT=he_codes[:, k, s * P : (s + 1) * P].bitcast(FP8X4),
-                lhsT_scale=he_plane[:, k, s * P : (s + 1) * P],
-                rhs=y_codes[:, G, :].bitcast(FP8X4),
-                rhs_scale=y_plane[:, G, :],
-                start=(G == 0),
-                stop=(G == GROUPS - 1),
-            )
+            cols = slice(half * HALF_A, (half + 1) * HALF_A)
+            for e in range(2):
+                s = 2 * pair + e
+                nc.tensor.matmul_mx(
+                    out=k_bank(b)[:, e * HALF_A : (e + 1) * HALF_A],
+                    lhsT=codes[:, k, 0, s * P : (s + 1) * P].bitcast(FP8X4),
+                    lhsT_scale=plane[:, k, 0, s * P : (s + 1) * P],
+                    rhs=y_codes[:, G, cols].bitcast(FP8X4),
+                    rhs_scale=y_plane[:, G, cols],
+                    start=(G == 0 and e == 0),
+                    stop=(G == GROUPS - 1 and e == 1),
+                )
 
-        def EP(c):
-            gh, s = divmod(c, PACK)
+        def EP(b):
+            gh, half, pair = b // 4, b // 2 % 2, b % 2
+            part = res[gh][:, half, 2 * pair : 2 * pair + 2, :].rearrange("p e a -> p (e a)")
             nc.vector.scalar_tensor_tensor(
-                out=res_row(c), in0=k_bank(c)[:], scalar=1.0 / math.sqrt(N), in1=res_row(c),
+                out=part, in0=k_bank(b)[:], scalar=1.0 / math.sqrt(N), in1=part,
                 op0=ALU.mult, op1=ALU.add,
             )
 
-        def ST(gh, s):
+        def ST(gh, half, s0=0, s1=PACK):
             rows = out_0[gh * K_PASS : (gh + 1) * K_PASS, :].rearrange("(p t) a -> p t a", t=PACK)
-            nc.sync.dma_start(out=rows[:, s : s + 2, :], in_=res[gh][:, s : s + 2, :])
+            cols = slice(half * HALF_A, (half + 1) * HALF_A)
+            nc.sync.dma_start(out=rows[:, s0:s1, cols], in_=res[gh][:, half, s0:s1, :])
 
-        def QO(gh):
-            nc.vector.quantize_mx(out=o_codes[:, gh, :].bitcast(FP8X4), scales=o_plane[:, gh, :], in_=flat(wide_bf[gh][:]))
+        def QO(gh, half):
+            cols = slice(half * HALF_A, (half + 1) * HALF_A)
+            nc.vector.quantize_mx(out=o_codes[:, gh, cols].bitcast(FP8X4), scales=o_plane[:, gh, cols], in_=flat(wide_bf[gh][:, cols, :]))
+
+        def store_words(gh, a0, a1):
             words = out_1[gh].rearrange("p m t -> p (m t)").bitcast(I32)
-            if gh == 0:
-                nc.sync.dma_start(out=words, in_=o_codes[:, gh, :].bitcast(I32))
-            else:
-                nc.sync.dma_start(out=words[:, : A // 2], in_=o_codes[:, gh, : A // 2].bitcast(I32))
-                nc.scalar.dma_start(out=words[:, A // 2 :], in_=o_codes[:, gh, A // 2 :].bitcast(I32))
-            if gh == HALVES - 1:
-                for Q in range(4):
-                    eng = nc.sync if Q < 2 else nc.scalar
-                    eng.dma_start(
-                        out=out_2[:, 4 * Q : 4 * Q + 4, :].rearrange("g q a -> q g a").bitcast(I32),
-                        in_=o_plane[32 * Q : 32 * Q + 4, :, :].bitcast(I32),
-                    )
+            nc.sync.dma_start(out=words[:, a0:a1], in_=o_codes[:, gh, a0:a1].bitcast(I32))
+
+        def store_scales():
+            for q in range(4):
+                nc.scalar.dma_start(
+                    out=out_2[:, 4 * q : 4 * q + 4, :].rearrange("g q a -> q g a").bitcast(I32),
+                    in_=o_plane[32 * q : 32 * q + 4, :, :].bitcast(I32),
+                )
 
         def both(step, j):
             if 0 <= j < PAIRS:
@@ -347,26 +364,26 @@ def tile_dampedsoftmaxfisherproduct_kernel(tc, h, g, w_words, w_scales, v, e, rh
         nc.vector.memset(w_plane[:].rearrange("p g a -> p (g a)").bitcast(U32), 0)
         make_identity(nc, ident[:])
         load_h(0, 1)
+        load_vec(0, g)
+        load_vec(2, e)
         load_h(1, 2)
-        load_vec(nc.scalar, 0, g)
-        load_vec(nc.scalar, 2, e)
         load_h(2, 4)
         nc.sync.dma_start(out=w_codes[:].bitcast(I32), in_=w_words.rearrange("g p n -> p g n").bitcast(I32))
+        for q in range(4):
+            nc.sync.dma_start(
+                out=w_plane[32 * q : 32 * q + 4, :, :].bitcast(I32),
+                in_=w_scales[:, 4 * q : 4 * q + 4, :].rearrange("g q a -> q g a").bitcast(I32),
+            )
         load_v(0)
         load_v(1)
-        for Q in range(4):
-            nc.scalar.dma_start(
-                out=w_plane[32 * Q : 32 * Q + 4, :, :].bitcast(I32),
-                in_=w_scales[:, 4 * Q : 4 * Q + 4, :].rearrange("g q a -> q g a").bitcast(I32),
-            )
         load_h(4, 6)
         load_h(6, 8)
         T(0)
         VT()
         VG()
         VE()
-        load_vec(nc.sync, 6, lam)
-        load_vec(nc.sync, 8, rho)
+        load_vec(6, lam)
+        load_vec(8, rho)
         for j in range(4, PAIRS):
             load_h(2 * j, 2 * j + 2)
 
@@ -377,13 +394,13 @@ def tile_dampedsoftmaxfisherproduct_kernel(tc, h, g, w_words, w_scales, v, e, rh
         both(F, 0)
         for i in range(PACK):
             DIAG(i, False)
-        QF(0, 2)
+        QF(0)
         DG(0, 0)
         both(Z, 0)
         both(F, 1)
         for i in range(PACK, 2 * PACK):
             DIAG(i, False)
-        QF(2, 2)
+        QF(1)
         both(Z, 1)
         VI(0, False)
         VI(1, True)
@@ -400,7 +417,7 @@ def tile_dampedsoftmaxfisherproduct_kernel(tc, h, g, w_words, w_scales, v, e, rh
         RHO()
         VL()
         R(0, 4)
-        QF(4, 2)
+        QF(2)
         QV(0)
         HE(0, 0)
         DG(1, 0)
@@ -416,12 +433,13 @@ def tile_dampedsoftmaxfisherproduct_kernel(tc, h, g, w_words, w_scales, v, e, rh
         both(W, 0)
         both(U, 1)
         HE(1, 0)
-        both(B, 0)
+        B(0)
         HE(1, 1)
+        B(1)
+        E2(0)
         both(C, 1)
-        both(E2, 0)
-        QH(0)
-        QF(6, 2)
+        E2(1)
+        Q(0, 0, 2)
         YP(0)
         both(T, 4)
         DG(2, 0)
@@ -435,24 +453,27 @@ def tile_dampedsoftmaxfisherproduct_kernel(tc, h, g, w_words, w_scales, v, e, rh
             both(U, j)
             R(2 * j, 2)
             both(F, j + 2)
+            B(2 * j - 2)
             HE(j, 0)
-            both(B, j - 1)
-            HE(j, 1)
+            E2(2 * j - 2)
+            HE(j, 1, 0, 2)
             both(C, j)
-            both(E2, j - 1)
-            QH(j - 1)
-            QF(2 * (j + 2), 2)
             if j >= 3:
                 G, half = divmod(j - 3, 2)
-                QY(G, half * A // 2, (half + 1) * A // 2)
+                QY(G, half * HALF_A, (half + 1) * HALF_A if j < PAIRS - 3 else A)
+            BV(2 * j - 1)
+            E2(2 * j - 1)
+            HE(j, 1, 2, PACK)
+            Q(j - 1, 0, 2)
             YP(j - 1)
             if j + 3 < PAIRS:
                 both(T, j + 3)
             DG(j + 1, 0)
-            DG(j + 1, 1)
+            if j < PAIRS - 3:
+                DG(j + 1, 1)
 
-        QY(1, A // 2, A)
         j = LAST - 1
+        HE(HE_ITEMS - 2, 0, 0, 2)
         both(MAX, j)
         both(EXP, j)
         both(Z, LAST)
@@ -461,65 +482,82 @@ def tile_dampedsoftmaxfisherproduct_kernel(tc, h, g, w_words, w_scales, v, e, rh
         both(U, LAST)
         R(2 * j, 2)
         both(MAX, LAST)
+        DG(HE_ITEMS - 2, 1)
         B(2 * j - 2)
+        E2P(2 * j - 1)
         E2(2 * j - 2)
-        B(2 * j - 1)
         both(C, j)
-        E2(2 * j - 1)
         YP(j - 1)
         both(EXP, LAST)
-        both(W, j)
-        R(2 * LAST, 2)
-        both(B, j)
-        both(C, LAST)
-        both(E2, j)
-        both(W, LAST)
-        both(B, LAST)
-        both(E2, LAST)
-        for c in range(0, PACK, 2):
+        for i in range(2 * j, TILES):
+            W(i)
+            if i + 2 < TILES:
+                R(i + 2, 1)
+                C(i + 2)
+            if i < TILES - 1:
+                B(i)
+            if i > 2 * j:
+                E2(i - 1)
+            else:
+                HE(HE_ITEMS - 2, 0, 2, PACK)
+        for b in range(0, 4, 2):
             for G in range(2):
-                K(c, G)
-                K(c + 1, G)
+                K(b, G)
+                K(b + 1, G)
+        DG(HE_ITEMS - 1, 0)
         QH(HE_ITEMS - 3)
-        K(PACK, 0)
-        K(PACK + 1, 0)
-        K(PACK, 1)
-        K(PACK + 1, 1)
+        E2V(TILES - 1)
         QY(GROUPS - 2, 0, A)
-        for c in range(PACK):
-            K(c, GROUPS - 2)
-        YV(GROUPS - 1, 0, A)
-        for b in range(2):
-            HE(HE_ITEMS - 2, b)
-            DG(HE_ITEMS - 1, b)
-        QY(GROUPS - 1, 0, A)
+        for G in range(2):
+            K(4, G)
+            K(5, G)
+        HE(HE_ITEMS - 2, 1)
+        DG(HE_ITEMS - 1, 1)
+        for b in range(4):
+            K(b, GROUPS - 2)
+        YV(GROUPS - 1, 0, HALF_A)
+        YV(GROUPS - 1, HALF_A, A)
+        QY(GROUPS - 1, 0, HALF_A)
+        QY(GROUPS - 1, HALF_A, A)
         QH(HE_ITEMS - 2)
         for b in range(2):
             HE(HE_ITEMS - 1, b)
         for c in range(PACK, 2 * PACK):
             LV(c, False)
-        for c in range(PACK):
-            K(c, GROUPS - 1)
-        K(PACK, 2)
-        K(PACK + 1, 2)
-        for c in range(PACK):
-            EP(c)
-            if c == 0:
-                QH(HE_ITEMS - 1)
-            if c % 2 == 1:
-                ST(0, c - 1)
-        OI(0, False, 0, A // 2)
-        OP(0, A // 2, A)
-        K(PACK, GROUPS - 1)
-        K(PACK + 1, GROUPS - 1)
-        for c in range(PACK + 2, 2 * PACK):
-            for G in range(GROUPS):
-                K(c, G)
-        for c in range(PACK, 2 * PACK):
-            EP(c)
-            if c % 2 == 1:
-                ST(1, c - 1 - PACK)
-        OI(1, False, A // 2, A)
-        QO(0)
-        OI(1, True, 0, A // 2)
-        QO(1)
+        for b in range(4):
+            K(b, GROUPS - 1)
+        K(4, 2)
+        K(5, 2)
+        EP(0)
+        ST(0, 0, 0, 2)
+        QH(HE_ITEMS - 1)
+        EP(1)
+        ST(0, 0, 2, PACK)
+        OP(0, 0)
+        for G in range(GROUPS - 1):
+            K(6, G)
+        for b in range(4, 7):
+            K(b, GROUPS - 1)
+        for G in range(GROUPS):
+            K(7, G)
+        EP(2)
+        EP(3)
+        ST(0, 1)
+        OI(0, 1, False, 0, HALF_A)
+        EP(4)
+        QO(0, 0)
+        EP(5)
+        ST(1, 0)
+        OI(1, 0, False, 0, HALF_A)
+        EP(6)
+        EP(7)
+        ST(1, 1)
+        QO(0, 1)
+        store_words(0, 0, A)
+        OI(1, 1, False, 160, HALF_A)
+        OI(1, 1, True, 0, 160)
+        QO(1, 0)
+        store_words(1, 0, HALF_A)
+        QO(1, 1)
+        store_words(1, HALF_A, A)
+        store_scales()

@@ -249,9 +249,6 @@ def tile_dampedsoftmaxfisherproduct_kernel(tc, h, g, w_words, w_scales, v, e, rh
         def B(i):
             nc.scalar.activation(out=col(shift, i), in_=col(acc, i), func=ACT.Copy, scale=col(inv, i))
 
-        def BV(i):
-            nc.vector.tensor_tensor(out=col(shift, i), in0=col(acc, i), in1=col(inv, i), op=ALU.mult)
-
         def E2P(i):
             nc.gpsimd.tensor_scalar(out=row(ex, i), in0=row(ex, i), scalar1=col(acc, i), scalar2=col(inv, i), op0=ALU.mult, op1=ALU.mult)
 
@@ -282,11 +279,11 @@ def tile_dampedsoftmaxfisherproduct_kernel(tc, h, g, w_words, w_scales, v, e, rh
         def runs(dst, src, a0, a1, run):
             return (dst[:, a0:a1, :].rearrange("p (c i) t -> p c t i", i=run), src[:, :, a0:a1].rearrange("p t (c i) -> p c t i", i=run))
 
-        def VI(gh, pool):
+        def VI(gh, pool, a0, a1):
             if pool:
-                nc.gpsimd.tensor_scalar(out=v_bf[gh], in0=v_sb[gh][:].rearrange("p t a -> p a t"), scalar1=1.0, scalar2=0.0, op0=ALU.mult, op1=ALU.add)
+                nc.gpsimd.tensor_scalar(out=v_bf[gh][:, a0:a1, :], in0=v_sb[gh][:, :, a0:a1].rearrange("p t a -> p a t"), scalar1=1.0, scalar2=0.0, op0=ALU.mult, op1=ALU.add)
             else:
-                out, in_ = runs(v_bf[gh], v_sb[gh], 0, A, 4)
+                out, in_ = runs(v_bf[gh], v_sb[gh], a0, a1, 4)
                 nc.scalar.copy(out=out, in_=in_)
 
         def OI(gh, half, vec, a0, a1):
@@ -295,9 +292,6 @@ def tile_dampedsoftmaxfisherproduct_kernel(tc, h, g, w_words, w_scales, v, e, rh
                 nc.vector.tensor_copy(out=out, in_=in_)
             else:
                 nc.scalar.copy(out=out, in_=in_)
-
-        def OP(gh, half):
-            nc.gpsimd.tensor_scalar(out=wide_bf[gh][:, half * HALF_A : (half + 1) * HALF_A, :], in0=res[gh][:, half, :, :].rearrange("p t a -> p a t"), scalar1=1.0, scalar2=0.0, op0=ALU.mult, op1=ALU.add)
 
         def DIAG(i, scalar):
             out = diag[i // PACK][:, i % PACK, :]
@@ -353,6 +347,20 @@ def tile_dampedsoftmaxfisherproduct_kernel(tc, h, g, w_words, w_scales, v, e, rh
                     in_=o_plane[32 * q : 32 * q + 4, :, :].bitcast(I32),
                 )
 
+        def first(j):
+            return 2 * j + j % 2
+
+        def second(j):
+            return 2 * j + 1 - j % 2
+
+        def use(step, j):
+            step(first(j))
+            step(second(j))
+
+        def fill(step, j):
+            step(second(j))
+            step(first(j))
+
         def both(step, j):
             if 0 <= j < PAIRS:
                 step(2 * j)
@@ -402,8 +410,9 @@ def tile_dampedsoftmaxfisherproduct_kernel(tc, h, g, w_words, w_scales, v, e, rh
             DIAG(i, False)
         QF(1)
         both(Z, 1)
-        VI(0, False)
-        VI(1, True)
+        VI(0, False, 0, A)
+        VI(1, False, 0, HALF_A)
+        VI(1, True, HALF_A, A)
         both(T, 2)
         DG(0, 1)
 
@@ -412,7 +421,7 @@ def tile_dampedsoftmaxfisherproduct_kernel(tc, h, g, w_words, w_scales, v, e, rh
             both(EXP, j)
         VT()
         both(F, 2)
-        both(T, 3)
+        fill(T, 3)
         QV(1)
         RHO()
         VL()
@@ -428,65 +437,65 @@ def tile_dampedsoftmaxfisherproduct_kernel(tc, h, g, w_words, w_scales, v, e, rh
         both(C, 0)
         LV(PACK - 1, False)
         DG(1, 1)
-        both(Z, 2)
-        both(F, 3)
+        fill(Z, 2)
+        use(F, 3)
         both(W, 0)
-        both(U, 1)
+        fill(U, 1)
         HE(1, 0)
         B(0)
         HE(1, 1)
         B(1)
         E2(0)
-        both(C, 1)
+        fill(C, 1)
         E2(1)
         Q(0, 0, 2)
         YP(0)
-        both(T, 4)
+        fill(T, 4)
         DG(2, 0)
         DG(2, 1)
 
         for j in range(2, PAIRS - 2):
-            both(MAX, j)
-            both(EXP, j)
-            both(Z, j + 1)
-            both(W, j - 1)
-            both(U, j)
+            use(MAX, j)
+            use(EXP, j)
+            fill(Z, j + 1)
+            use(W, j - 1)
+            fill(U, j)
             R(2 * j, 2)
-            both(F, j + 2)
-            B(2 * j - 2)
+            use(F, j + 2)
+            B(first(j - 1))
             HE(j, 0)
-            E2(2 * j - 2)
+            B(second(j - 1))
+            E2(first(j - 1))
             HE(j, 1, 0, 2)
-            both(C, j)
+            fill(C, j)
+            E2(second(j - 1))
+            HE(j, 1, 2, PACK)
             if j >= 3:
                 G, half = divmod(j - 3, 2)
                 QY(G, half * HALF_A, (half + 1) * HALF_A if j < PAIRS - 3 else A)
-            BV(2 * j - 1)
-            E2(2 * j - 1)
-            HE(j, 1, 2, PACK)
             Q(j - 1, 0, 2)
             YP(j - 1)
             if j + 3 < PAIRS:
-                both(T, j + 3)
+                fill(T, j + 3)
             DG(j + 1, 0)
             if j < PAIRS - 3:
                 DG(j + 1, 1)
 
         j = LAST - 1
         HE(HE_ITEMS - 2, 0, 0, 2)
-        both(MAX, j)
-        both(EXP, j)
+        use(MAX, j)
+        use(EXP, j)
         both(Z, LAST)
-        both(W, j - 1)
-        both(U, j)
+        DG(HE_ITEMS - 2, 1)
+        use(W, j - 1)
+        fill(U, j)
         both(U, LAST)
         R(2 * j, 2)
         both(MAX, LAST)
-        DG(HE_ITEMS - 2, 1)
-        B(2 * j - 2)
-        E2P(2 * j - 1)
-        E2(2 * j - 2)
-        both(C, j)
+        B(first(j - 1))
+        E2P(second(j - 1))
+        E2(first(j - 1))
+        fill(C, j)
         YP(j - 1)
         both(EXP, LAST)
         for i in range(2 * j, TILES):
@@ -533,7 +542,7 @@ def tile_dampedsoftmaxfisherproduct_kernel(tc, h, g, w_words, w_scales, v, e, rh
         QH(HE_ITEMS - 1)
         EP(1)
         ST(0, 0, 2, PACK)
-        OP(0, 0)
+        OI(0, 0, False, 0, HALF_A)
         for G in range(GROUPS - 1):
             K(6, G)
         for b in range(4, 7):

@@ -136,9 +136,6 @@ def tile_dampedsoftmaxfisherproduct_kernel(tc, h, g, w_words, w_scales, v, e, rh
             for u in range(2):
                 nc.tensor.transpose(z_banks[0][:, u * P : (u + 1) * P], words[:, u::2], ident[:])
 
-        def VG():
-            nc.vector.tensor_copy(out=g_sb[:].rearrange("p c (u e) -> p c u e", u=2), in_=vec_cols(0, 2))
-
         def VE():
             nc.vector.tensor_copy(out=e32[:].rearrange("p (c u e) -> p c u e", u=2, e=2), in_=vec_cols(2, 6))
 
@@ -293,6 +290,9 @@ def tile_dampedsoftmaxfisherproduct_kernel(tc, h, g, w_words, w_scales, v, e, rh
             else:
                 nc.scalar.copy(out=out, in_=in_)
 
+        def OP(gh, half):
+            nc.gpsimd.tensor_scalar(out=wide_bf[gh][:, half * HALF_A : (half + 1) * HALF_A, :], in0=res[gh][:, half, :, :].rearrange("p t a -> p a t"), scalar1=1.0, scalar2=0.0, op0=ALU.mult, op1=ALU.add)
+
         def DIAG(i, scalar):
             out = diag[i // PACK][:, i % PACK, :]
             if scalar:
@@ -326,11 +326,12 @@ def tile_dampedsoftmaxfisherproduct_kernel(tc, h, g, w_words, w_scales, v, e, rh
                 out=part, in0=k_bank(b)[:], scalar=1.0 / math.sqrt(N), in1=part,
                 op0=ALU.mult, op1=ALU.add,
             )
+            ST(b)
 
-        def ST(gh, half, s0=0, s1=PACK):
+        def ST(b):
+            gh, half, pair = b // 4, b // 2 % 2, b % 2
             rows = out_0[gh * K_PASS : (gh + 1) * K_PASS, :].rearrange("(p t) a -> p t a", t=PACK)
-            cols = slice(half * HALF_A, (half + 1) * HALF_A)
-            nc.sync.dma_start(out=rows[:, s0:s1, cols], in_=res[gh][:, half, s0:s1, :])
+            nc.sync.dma_start(out=rows[:, 2 * pair : 2 * pair + 2, half * HALF_A : (half + 1) * HALF_A], in_=res[gh][:, half, 2 * pair : 2 * pair + 2, :])
 
         def QO(gh, half):
             cols = slice(half * HALF_A, (half + 1) * HALF_A)
@@ -342,7 +343,8 @@ def tile_dampedsoftmaxfisherproduct_kernel(tc, h, g, w_words, w_scales, v, e, rh
 
         def store_scales():
             for q in range(4):
-                nc.scalar.dma_start(
+                eng = nc.scalar if q < 2 else nc.sync
+                eng.dma_start(
                     out=out_2[:, 4 * q : 4 * q + 4, :].rearrange("g q a -> q g a").bitcast(I32),
                     in_=o_plane[32 * q : 32 * q + 4, :, :].bitcast(I32),
                 )
@@ -372,7 +374,7 @@ def tile_dampedsoftmaxfisherproduct_kernel(tc, h, g, w_words, w_scales, v, e, rh
         nc.vector.memset(w_plane[:].rearrange("p g a -> p (g a)").bitcast(U32), 0)
         make_identity(nc, ident[:])
         load_h(0, 1)
-        load_vec(0, g)
+        nc.scalar.dma_start(out=g_sb[:], in_=g.rearrange("(c p t) -> p c t", p=P, t=PACK))
         load_vec(2, e)
         load_h(1, 2)
         load_h(2, 4)
@@ -386,20 +388,20 @@ def tile_dampedsoftmaxfisherproduct_kernel(tc, h, g, w_words, w_scales, v, e, rh
         load_v(1)
         load_h(4, 6)
         load_h(6, 8)
+
         T(0)
         VT()
-        VG()
-        VE()
         load_vec(6, lam)
         load_vec(8, rho)
         for j in range(4, PAIRS):
             load_h(2 * j, 2 * j + 2)
-
+        T(1)
+        F(0)
+        VE()
+        F(1)
         for i in range(2 * PACK, TILES):
             DIAG(i, True)
-        T(1)
         both(T, 1)
-        both(F, 0)
         for i in range(PACK):
             DIAG(i, False)
         QF(0)
@@ -411,8 +413,7 @@ def tile_dampedsoftmaxfisherproduct_kernel(tc, h, g, w_words, w_scales, v, e, rh
         QF(1)
         both(Z, 1)
         VI(0, False, 0, A)
-        VI(1, False, 0, HALF_A)
-        VI(1, True, HALF_A, A)
+        VI(1, True, 0, A)
         both(T, 2)
         DG(0, 1)
 
@@ -423,11 +424,11 @@ def tile_dampedsoftmaxfisherproduct_kernel(tc, h, g, w_words, w_scales, v, e, rh
         both(F, 2)
         fill(T, 3)
         QV(1)
+        QV(0)
+        QF(2)
         RHO()
         VL()
         R(0, 4)
-        QF(2)
-        QV(0)
         HE(0, 0)
         DG(1, 0)
         both(U, 0)
@@ -435,19 +436,20 @@ def tile_dampedsoftmaxfisherproduct_kernel(tc, h, g, w_words, w_scales, v, e, rh
             LV(c, True)
         HE(0, 1)
         both(C, 0)
-        LV(PACK - 1, False)
+        fill(C, 1)
         DG(1, 1)
         fill(Z, 2)
         use(F, 3)
         both(W, 0)
         fill(U, 1)
         HE(1, 0)
+        LV(PACK - 1, False)
         B(0)
-        HE(1, 1)
+        HE(1, 1, 0, 2)
         B(1)
         E2(0)
-        fill(C, 1)
         E2(1)
+        HE(1, 1, 2, PACK)
         Q(0, 0, 2)
         YP(0)
         fill(T, 4)
@@ -460,8 +462,8 @@ def tile_dampedsoftmaxfisherproduct_kernel(tc, h, g, w_words, w_scales, v, e, rh
             fill(Z, j + 1)
             use(W, j - 1)
             fill(U, j)
-            R(2 * j, 2)
             use(F, j + 2)
+            R(2 * j, 2)
             B(first(j - 1))
             HE(j, 0)
             B(second(j - 1))
@@ -538,10 +540,8 @@ def tile_dampedsoftmaxfisherproduct_kernel(tc, h, g, w_words, w_scales, v, e, rh
         K(4, 2)
         K(5, 2)
         EP(0)
-        ST(0, 0, 0, 2)
         QH(HE_ITEMS - 1)
         EP(1)
-        ST(0, 0, 2, PACK)
         OI(0, 0, False, 0, HALF_A)
         for G in range(GROUPS - 1):
             K(6, G)
@@ -551,16 +551,13 @@ def tile_dampedsoftmaxfisherproduct_kernel(tc, h, g, w_words, w_scales, v, e, rh
             K(7, G)
         EP(2)
         EP(3)
-        ST(0, 1)
-        OI(0, 1, False, 0, HALF_A)
+        OP(0, 1)
         EP(4)
-        QO(0, 0)
         EP(5)
-        ST(1, 0)
         OI(1, 0, False, 0, HALF_A)
         EP(6)
+        QO(0, 0)
         EP(7)
-        ST(1, 1)
         QO(0, 1)
         store_words(0, 0, A)
         OI(1, 1, False, 160, HALF_A)

@@ -49,7 +49,9 @@ def tile_dampedsoftmaxfisherproduct_kernel(tc, h, g, w_words, w_scales, v, e, rh
 
         ident = tile("ident", [P, P], F32)
         g_sb = tile("g_sb", [P, HALVES, PACK], BF16)
-        vec_rows = tile("vec_rows", [P, K_PASS], BF16)
+        e_sb = tile("e_sb", [P, GROUPS, PACK], BF16)
+        rho_sb = tile("rho_sb", [P, GROUPS, PACK], BF16)
+        lam_sb = tile("lam_sb", [P, HALVES, PACK], BF16)
         lam32 = tile("lam32", [P, HALVES * PACK], F32)
         e32 = tile("e32", [P, TILES], F32)
         rho_neg = tile("rho_neg", [P, TILES], F32)
@@ -124,26 +126,17 @@ def tile_dampedsoftmaxfisherproduct_kernel(tc, h, g, w_words, w_scales, v, e, rh
             rows = v[gh * K_PASS : (gh + 1) * K_PASS, :].rearrange("(p t) a -> p t a", t=PACK)
             nc.sync.dma_start(out=v_sb[gh][:], in_=rows)
 
-        def load_vec(row0, src):
-            rows = src.rearrange("(c k) -> c k", k=K_PASS)
-            nc.sync.dma_start(out=vec_rows[row0 : row0 + rows.shape[0], :], in_=rows)
-
-        def vec_cols(row0, row1):
-            return z_banks[0][:, : 2 * P].bitcast(BF16).rearrange("p (u r e) -> p r u e", u=2, e=2)[:, row0:row1, :, :]
-
-        def VT():
-            words = vec_rows[:].bitcast(F32)
-            for u in range(2):
-                nc.tensor.transpose(z_banks[0][:, u * P : (u + 1) * P], words[:, u::2], ident[:])
+        def load_vec(eng, dst, src):
+            eng.dma_start(out=dst[:], in_=src.rearrange("(c p t) -> p c t", p=P, t=PACK))
 
         def VE():
-            nc.vector.tensor_copy(out=e32[:].rearrange("p (c u e) -> p c u e", u=2, e=2), in_=vec_cols(2, 6))
+            nc.vector.tensor_copy(out=e32[:], in_=flat(e_sb[:]))
 
         def VL():
-            nc.vector.tensor_copy(out=lam32[:].rearrange("p (c u e) -> p c u e", u=2, e=2), in_=vec_cols(6, 8))
+            nc.vector.tensor_copy(out=lam32[:], in_=flat(lam_sb[:]))
 
         def RHO():
-            nc.vector.tensor_scalar(out=rho_neg[:].rearrange("p (c u e) -> p c u e", u=2, e=2), in0=vec_cols(8, 12), scalar1=-float(A), scalar2=None, op0=ALU.mult)
+            nc.vector.tensor_scalar(out=rho_neg[:], in0=flat(rho_sb[:]), scalar1=-float(A), scalar2=None, op0=ALU.mult)
 
         def T(i):
             bank = t_bank(i)
@@ -370,12 +363,11 @@ def tile_dampedsoftmaxfisherproduct_kernel(tc, h, g, w_words, w_scales, v, e, rh
 
         ctx.enter_context(tc.manual_schedule())
 
-        nc.vector.memset(vec_rows[:].bitcast(U32), 0)
         nc.vector.memset(w_plane[:].rearrange("p g a -> p (g a)").bitcast(U32), 0)
         make_identity(nc, ident[:])
         load_h(0, 1)
-        nc.scalar.dma_start(out=g_sb[:], in_=g.rearrange("(c p t) -> p c t", p=P, t=PACK))
-        load_vec(2, e)
+        load_vec(nc.scalar, g_sb, g)
+        load_vec(nc.scalar, e_sb, e)
         load_h(1, 2)
         load_h(2, 4)
         nc.sync.dma_start(out=w_codes[:].bitcast(I32), in_=w_words.rearrange("g p n -> p g n").bitcast(I32))
@@ -389,26 +381,26 @@ def tile_dampedsoftmaxfisherproduct_kernel(tc, h, g, w_words, w_scales, v, e, rh
         load_h(4, 6)
         load_h(6, 8)
 
-        T(0)
-        VT()
-        load_vec(6, lam)
-        load_vec(8, rho)
+        load_vec(nc.sync, lam_sb, lam)
+        load_vec(nc.sync, rho_sb, rho)
         for j in range(4, PAIRS):
             load_h(2 * j, 2 * j + 2)
-        T(1)
+
+        both(T, 0)
         F(0)
         VE()
         F(1)
-        for i in range(2 * PACK, TILES):
-            DIAG(i, True)
+        for G in (0, GROUPS - 1):
+            for t in range(PACK):
+                DIAG(PACK * G + t, True)
         both(T, 1)
-        for i in range(PACK):
+        for i in range(PACK, 2 * PACK):
             DIAG(i, False)
         QF(0)
         DG(0, 0)
         both(Z, 0)
         both(F, 1)
-        for i in range(PACK, 2 * PACK):
+        for i in range(2 * PACK, 3 * PACK):
             DIAG(i, False)
         QF(1)
         both(Z, 1)
@@ -420,7 +412,6 @@ def tile_dampedsoftmaxfisherproduct_kernel(tc, h, g, w_words, w_scales, v, e, rh
         for j in range(2):
             both(MAX, j)
             both(EXP, j)
-        VT()
         both(F, 2)
         fill(T, 3)
         QV(1)
@@ -452,8 +443,8 @@ def tile_dampedsoftmaxfisherproduct_kernel(tc, h, g, w_words, w_scales, v, e, rh
         HE(1, 1, 2, PACK)
         Q(0, 0, 2)
         YP(0)
-        fill(T, 4)
         DG(2, 0)
+        fill(T, 4)
         DG(2, 1)
 
         for j in range(2, PAIRS - 2):
@@ -477,9 +468,9 @@ def tile_dampedsoftmaxfisherproduct_kernel(tc, h, g, w_words, w_scales, v, e, rh
                 QY(G, half * HALF_A, (half + 1) * HALF_A if j < PAIRS - 3 else A)
             Q(j - 1, 0, 2)
             YP(j - 1)
+            DG(j + 1, 0)
             if j + 3 < PAIRS:
                 fill(T, j + 3)
-            DG(j + 1, 0)
             if j < PAIRS - 3:
                 DG(j + 1, 1)
 

@@ -54,7 +54,6 @@ def tile_dampedsoftmaxfisherproduct_kernel(tc, h, g, w_words, w_scales, v, e, rh
         lam_sb = tile("lam_sb", [P, HALVES, PACK], BF16)
         lam32 = tile("lam32", [P, HALVES * PACK], F32)
         e32 = tile("e32", [P, TILES], F32)
-        rho_neg = tile("rho_neg", [P, TILES], F32)
         diag = [tile("diag%d" % G, [P, PACK, P], BF16) for G in range(GROUPS)]
         h_sb = [tile("h%d" % j, [P, 2, D], BF16) for j in range(PAIRS)]
         v_sb = [tile("v%d" % gh, [P, PACK, A], BF16) for gh in range(HALVES)]
@@ -77,9 +76,8 @@ def tile_dampedsoftmaxfisherproduct_kernel(tc, h, g, w_words, w_scales, v, e, rh
         neg_max = tile("neg_max", [P, TILES], F32)
         total = tile("total", [P, TILES], F32)
         inv = tile("inv", [P, TILES], F32)
-        coef = tile("coef", [P, TILES], F32)
-        acc = tile("acc", [P, TILES], F32)
-        shift = tile("shift", [P, TILES], F32)
+        acc_rho = tile("acc_rho", [P, PAIRS + 1, 2, 2], F32)
+        shift_coef = tile("shift_coef", [P, PAIRS + 1, 2, 2], F32)
 
         def f_unit(j):
             return (j - F_LEAD) % PAIRS
@@ -98,6 +96,12 @@ def tile_dampedsoftmaxfisherproduct_kernel(tc, h, g, w_words, w_scales, v, e, rh
 
         def col(t, i):
             return t[:, i : i + 1]
+
+        def behind(t, i):
+            return t[:, i // 2 + 1, 0, i % 2 : i % 2 + 1]
+
+        def ahead(t, i):
+            return t[:, i // 2, 1, i % 2 : i % 2 + 1]
 
         def flat(ap):
             return ap.rearrange("p a t -> p (a t)")
@@ -136,7 +140,7 @@ def tile_dampedsoftmaxfisherproduct_kernel(tc, h, g, w_words, w_scales, v, e, rh
             nc.vector.tensor_copy(out=lam32[:], in_=flat(lam_sb[:]))
 
         def RHO():
-            nc.vector.tensor_scalar(out=rho_neg[:], in0=flat(rho_sb[:]), scalar1=-float(A), scalar2=None, op0=ALU.mult)
+            nc.vector.tensor_scalar(out=acc_rho[:, :PAIRS, 1, :], in0=flat(rho_sb[:]).rearrange("p (j e) -> p j e", e=2), scalar1=-float(A), scalar2=None, op0=ALU.mult)
 
         def T(i):
             bank = t_bank(i)
@@ -228,25 +232,28 @@ def tile_dampedsoftmaxfisherproduct_kernel(tc, h, g, w_words, w_scales, v, e, rh
             nc.vector.reciprocal(out=inv[:, i : i + n], in_=total[:, i : i + n])
 
         def C(i):
-            nc.scalar.activation(out=col(coef, i), in_=col(inv, i), func=ACT.Copy, scale=col(rho_neg, i))
+            nc.scalar.activation(out=ahead(shift_coef, i), in_=col(inv, i), func=ACT.Copy, scale=ahead(acc_rho, i))
 
         def W(i):
             nc.vector.scalar_tensor_tensor(
-                out=row(eu, i), in0=u_bank(i)[:], scalar=col(coef, i), in1=row(ex, i),
-                op0=ALU.mult, op1=ALU.mult, accum_out=col(acc, i),
+                out=row(eu, i), in0=u_bank(i)[:], scalar=ahead(shift_coef, i), in1=row(ex, i),
+                op0=ALU.mult, op1=ALU.mult, accum_out=behind(acc_rho, i),
             )
 
         def B(i):
-            nc.scalar.activation(out=col(shift, i), in_=col(acc, i), func=ACT.Copy, scale=col(inv, i))
+            nc.scalar.activation(out=behind(shift_coef, i), in_=behind(acc_rho, i), func=ACT.Copy, scale=col(inv, i))
+
+        def BC(j):
+            nc.gpsimd.tensor_tensor(out=flat(shift_coef[:, j, :, :]), in0=flat(acc_rho[:, j, :, :]), in1=inv[:, 2 * j - 2 : 2 * j + 2], op=ALU.mult)
 
         def E2P(i):
-            nc.gpsimd.tensor_scalar(out=row(ex, i), in0=row(ex, i), scalar1=col(acc, i), scalar2=col(inv, i), op0=ALU.mult, op1=ALU.mult)
+            nc.gpsimd.tensor_scalar(out=row(ex, i), in0=row(ex, i), scalar1=behind(acc_rho, i), scalar2=col(inv, i), op0=ALU.mult, op1=ALU.mult)
 
         def E2V(i):
-            nc.vector.tensor_scalar(out=row(ex, i), in0=row(ex, i), scalar1=col(acc, i), scalar2=col(inv, i), op0=ALU.mult, op1=ALU.mult)
+            nc.vector.tensor_scalar(out=row(ex, i), in0=row(ex, i), scalar1=behind(acc_rho, i), scalar2=col(inv, i), op0=ALU.mult, op1=ALU.mult)
 
         def E2(i):
-            nc.scalar.activation(out=row(ex, i), in_=row(ex, i), func=ACT.Copy, scale=col(shift, i))
+            nc.scalar.activation(out=row(ex, i), in_=row(ex, i), func=ACT.Copy, scale=behind(shift_coef, i))
 
         def YP(j):
             G, u = divmod(j, 2)
@@ -434,7 +441,6 @@ def tile_dampedsoftmaxfisherproduct_kernel(tc, h, g, w_words, w_scales, v, e, rh
         both(W, 0)
         fill(U, 1)
         HE(1, 0)
-        LV(PACK - 1, False)
         B(0)
         HE(1, 1, 0, 2)
         B(1)
@@ -453,15 +459,12 @@ def tile_dampedsoftmaxfisherproduct_kernel(tc, h, g, w_words, w_scales, v, e, rh
             fill(Z, j + 1)
             use(W, j - 1)
             fill(U, j)
-            use(F, j + 2)
             R(2 * j, 2)
-            B(first(j - 1))
+            use(F, j + 2)
+            BC(j)
             HE(j, 0)
-            B(second(j - 1))
-            E2(first(j - 1))
             HE(j, 1, 0, 2)
-            fill(C, j)
-            E2(second(j - 1))
+            use(E2, j - 1)
             HE(j, 1, 2, PACK)
             if j >= 3:
                 G, half = divmod(j - 3, 2)
@@ -524,7 +527,7 @@ def tile_dampedsoftmaxfisherproduct_kernel(tc, h, g, w_words, w_scales, v, e, rh
         QH(HE_ITEMS - 2)
         for b in range(2):
             HE(HE_ITEMS - 1, b)
-        for c in range(PACK, 2 * PACK):
+        for c in range(PACK - 1, 2 * PACK):
             LV(c, False)
         for b in range(4):
             K(b, GROUPS - 1)

@@ -48,6 +48,7 @@ def tile_dampedsoftmaxfisherproduct_kernel(tc, h, g, w_words, w_scales, v, e, rh
         d_banks = banks[6:8]
 
         ident = tile("ident", [P, P], F32)
+        zeros = tile("zeros", [P, K_PASS], BF16)
         g_sb = tile("g_sb", [P, HALVES, PACK], BF16)
         e_sb = tile("e_sb", [P, GROUPS, PACK], BF16)
         rho_sb = tile("rho_sb", [P, GROUPS, PACK], BF16)
@@ -132,6 +133,10 @@ def tile_dampedsoftmaxfisherproduct_kernel(tc, h, g, w_words, w_scales, v, e, rh
 
         def load_vec(eng, dst, src):
             eng.dma_start(out=dst[:], in_=src.rearrange("(c p t) -> p c t", p=P, t=PACK))
+
+        def warm_up(count):
+            for n in range(count):
+                nc.tensor.matmul(out=d_banks[1][:], lhsT=zeros[:, :P], rhs=zeros[:], start=True, stop=True)
 
         def VE():
             nc.vector.tensor_copy(out=e32[:], in_=flat(e_sb[:]))
@@ -370,6 +375,7 @@ def tile_dampedsoftmaxfisherproduct_kernel(tc, h, g, w_words, w_scales, v, e, rh
 
         ctx.enter_context(tc.manual_schedule())
 
+        nc.vector.memset(zeros[:].bitcast(U32), 0)
         nc.vector.memset(w_plane[:].rearrange("p g a -> p (g a)").bitcast(U32), 0)
         make_identity(nc, ident[:])
         load_h(0, 1)
@@ -393,7 +399,9 @@ def tile_dampedsoftmaxfisherproduct_kernel(tc, h, g, w_words, w_scales, v, e, rh
         for j in range(4, PAIRS):
             load_h(2 * j, 2 * j + 2)
 
+        warm_up(3)
         both(T, 0)
+        warm_up(2)
         F(0)
         VE()
         F(1)

@@ -264,9 +264,9 @@ def tile_dampedsoftmaxfisherproduct_kernel(tc, h, g, w_words, w_scales, v, e, rh
             G, u = divmod(j, 2)
             slots = slice(2 * u, 2 * u + 2)
             nc.gpsimd.tensor_tensor(
-                out=y_bf[G % 2][:, :, slots],
-                in0=ex[G % 2][:, slots, :].rearrange("p t a -> p a t"),
-                in1=eu[G % 2][:, slots, :].rearrange("p t a -> p a t"),
+                out=y_bf[G % 2][:, :, slots].rearrange("p (c i) t -> p c t i", i=2),
+                in0=ex[G % 2][:, slots, :].rearrange("p t (c i) -> p c t i", i=2),
+                in1=eu[G % 2][:, slots, :].rearrange("p t (c i) -> p c t i", i=2),
                 op=ALU.subtract,
             )
 

@@ -264,9 +264,9 @@ def tile_dampedsoftmaxfisherproduct_kernel(tc, h, g, w_words, w_scales, v, e, rh
             G, u = divmod(j, 2)
             slots = slice(2 * u, 2 * u + 2)
             nc.gpsimd.tensor_tensor(
-                out=y_bf[G % 2][:, :, slots].rearrange("p (c i) t -> p c t i", i=2),
-                in0=ex[G % 2][:, slots, :].rearrange("p t (c i) -> p c t i", i=2),
-                in1=eu[G % 2][:, slots, :].rearrange("p t (c i) -> p c t i", i=2),
+                out=y_bf[G % 2][:, :, slots].rearrange("p (c i) t -> p c t i", i=4),
+                in0=ex[G % 2][:, slots, :].rearrange("p t (c i) -> p c t i", i=4),
+                in1=eu[G % 2][:, slots, :].rearrange("p t (c i) -> p c t i", i=4),
                 op=ALU.subtract,
             )
 
@@ -296,7 +296,8 @@ def tile_dampedsoftmaxfisherproduct_kernel(tc, h, g, w_words, w_scales, v, e, rh
                 nc.scalar.copy(out=out, in_=in_)
 
         def OP(gh, half):
-            nc.gpsimd.tensor_scalar(out=wide_bf[gh][:, half * HALF_A : (half + 1) * HALF_A, :], in0=res[gh][:, half, :, :].rearrange("p t a -> p a t"), scalar1=1.0, scalar2=0.0, op0=ALU.mult, op1=ALU.add)
+            out, in_ = runs(wide_bf[gh][:, half * HALF_A : (half + 1) * HALF_A, :], res[gh][:, half, :, :], 0, HALF_A, 2)
+            nc.gpsimd.tensor_scalar(out=out, in0=in_, scalar1=1.0, scalar2=0.0, op0=ALU.mult, op1=ALU.add)
 
         def DIAG(i, scalar):
             out = diag[i // PACK][:, i % PACK, :]

@@ -142,10 +142,10 @@ def tile_dampedsoftmaxfisherproduct_kernel(tc, h, g, w_words, w_scales, v, e, rh
             nc.vector.tensor_copy(out=e32[:], in_=flat(e_sb[:]))
 
         def VL():
-            nc.vector.tensor_copy(out=lam32[:], in_=flat(lam_sb[:]))
+            nc.scalar.activation(out=lam32[:], in_=flat(lam_sb[:]), func=ACT.Copy)
 
         def RHO():
-            nc.vector.tensor_scalar(out=acc_rho[:, :PAIRS, 1, :], in0=flat(rho_sb[:]).rearrange("p (j e) -> p j e", e=2), scalar1=-float(A), scalar2=None, op0=ALU.mult)
+            nc.scalar.activation(out=acc_rho[:, :PAIRS, 1, :], in_=flat(rho_sb[:]).rearrange("p (j e) -> p j e", e=2), func=ACT.Copy, scale=-float(A))
 
         def T(i):
             bank = t_bank(i)
@@ -247,6 +247,9 @@ def tile_dampedsoftmaxfisherproduct_kernel(tc, h, g, w_words, w_scales, v, e, rh
 
         def B(i):
             nc.scalar.activation(out=behind(shift_coef, i), in_=behind(acc_rho, i), func=ACT.Copy, scale=col(inv, i))
+
+        def CP(j, n):
+            nc.gpsimd.tensor_tensor(out=shift_coef[:, j : j + n, 1, :], in0=acc_rho[:, j : j + n, 1, :], in1=inv[:, 2 * j : 2 * (j + n)].rearrange("p (j e) -> p j e", e=2), op=ALU.mult)
 
         def BC(j):
             nc.gpsimd.tensor_tensor(out=flat(shift_coef[:, j, :, :]), in0=flat(acc_rho[:, j, :, :]), in1=inv[:, 2 * j - 2 : 2 * j + 2], op=ALU.mult)
@@ -401,8 +404,10 @@ def tile_dampedsoftmaxfisherproduct_kernel(tc, h, g, w_words, w_scales, v, e, rh
             load_h(2 * j, 2 * j + 2)
 
         warm_up(3)
-        both(T, 0)
-        warm_up(2)
+        T(0)
+        warm_up(1)
+        T(1)
+        warm_up(1)
         F(0)
         VE()
         F(1)
@@ -420,6 +425,7 @@ def tile_dampedsoftmaxfisherproduct_kernel(tc, h, g, w_words, w_scales, v, e, rh
             DIAG(i, False)
         QF(1)
         both(Z, 1)
+        HE(0, 0)
         VI(0, False, 0, A)
         VI(1, True, 0, A)
         both(T, 2)
@@ -429,6 +435,7 @@ def tile_dampedsoftmaxfisherproduct_kernel(tc, h, g, w_words, w_scales, v, e, rh
             both(MAX, j)
             both(EXP, j)
         both(F, 2)
+        DG(1, 0)
         fill(T, 3)
         QV(1)
         QV(0)
@@ -436,27 +443,23 @@ def tile_dampedsoftmaxfisherproduct_kernel(tc, h, g, w_words, w_scales, v, e, rh
         RHO()
         VL()
         R(0, 4)
-        HE(0, 0)
-        DG(1, 0)
+        CP(0, 2)
         both(U, 0)
-        for c in range(PACK - 1):
+        for c in range(2):
             LV(c, True)
         HE(0, 1)
-        both(C, 0)
-        fill(C, 1)
+        HE(1, 0)
         DG(1, 1)
         fill(Z, 2)
         use(F, 3)
         both(W, 0)
         fill(U, 1)
-        HE(1, 0)
-        B(0)
         HE(1, 1, 0, 2)
-        B(1)
-        E2(0)
-        E2(1)
+        B(0)
         HE(1, 1, 2, PACK)
+        E2(0)
         Q(0, 0, 2)
+        E2P(1)
         YP(0)
         DG(2, 0)
         fill(T, 4)
@@ -470,15 +473,22 @@ def tile_dampedsoftmaxfisherproduct_kernel(tc, h, g, w_words, w_scales, v, e, rh
             fill(U, j)
             R(2 * j, 2)
             use(F, j + 2)
-            BC(j)
+            if j > 2:
+                BC(j)
             HE(j, 0)
+            if j == 2:
+                use(B, j - 1)
             HE(j, 1, 0, 2)
             use(E2, j - 1)
             HE(j, 1, 2, PACK)
             if j >= 3:
                 G, half = divmod(j - 3, 2)
                 QY(G, half * HALF_A, (half + 1) * HALF_A if j < PAIRS - 3 else A)
-            Q(j - 1, 0, 2)
+                Q(j - 1, 0, 2)
+            else:
+                QH(j - 1)
+                QF(j + 2)
+                CP(j, 1)
             YP(j - 1)
             DG(j + 1, 0)
             if j + 3 < PAIRS:
@@ -536,7 +546,7 @@ def tile_dampedsoftmaxfisherproduct_kernel(tc, h, g, w_words, w_scales, v, e, rh
         QH(HE_ITEMS - 2)
         for b in range(2):
             HE(HE_ITEMS - 1, b)
-        for c in range(PACK - 1, 2 * PACK):
+        for c in range(2, 2 * PACK):
             LV(c, False)
         for b in range(4):
             K(b, GROUPS - 1)
@@ -559,8 +569,8 @@ def tile_dampedsoftmaxfisherproduct_kernel(tc, h, g, w_words, w_scales, v, e, rh
         EP(5)
         OI(1, 0, False, 0, HALF_A)
         EP(6)
-        QO(0, 0)
         EP(7)
+        QO(0, 0)
         QO(0, 1)
         store_words(0, 0, A)
         OI(1, 1, False, 160, HALF_A)

@@ -30,6 +30,7 @@ HE_ITEMS = GROUPS * HALVES
 STAGE_BUFS = 3
 F_LEAD = 3
 HALF_A = A // 2
+RUN = 4
 
 
 def tile_dampedsoftmaxfisherproduct_kernel(tc, h, g, w_words, w_scales, v, e, rho, lam, out_0, out_1, out_2):
@@ -227,11 +228,20 @@ def tile_dampedsoftmaxfisherproduct_kernel(tc, h, g, w_words, w_scales, v, e, rh
         def MAX(i):
             nc.vector.tensor_reduce(out=col(neg_max, i), in_=z_bank(i)[:], axis=mybir.AxisListType.X, op=ALU.max, negate=True)
 
+        def pair_of(tiles, j):
+            G, u = divmod(j, 2)
+            return tiles[G % 2][:, 2 * u : 2 * u + 2, :].rearrange("p e a -> p (e a)").rearrange("p (c e i) -> p c e i", e=2, i=RUN)
+
+        def in_runs(ap):
+            return ap.rearrange("p (c i) -> p c i", i=RUN)
+
         def row(tiles, i):
-            return tiles[(i // PACK) % 2][:, i % PACK, :]
+            if i // PACK == GROUPS - 1:
+                return in_runs(tiles[(i // PACK) % 2][:, i % PACK, :])
+            return pair_of(tiles, i // 2)[:, :, i % 2, :]
 
         def EXP(i):
-            nc.scalar.activation(out=row(ex, i), in_=z_bank(i)[:], func=ACT.Exp, bias=col(neg_max, i), accum_out=col(total, i))
+            nc.scalar.activation(out=row(ex, i), in_=in_runs(z_bank(i)[:]), func=ACT.Exp, bias=col(neg_max, i), accum_out=col(total, i))
 
         def R(i, n):
             nc.vector.reciprocal(out=inv[:, i : i + n], in_=total[:, i : i + n])
@@ -241,7 +251,7 @@ def tile_dampedsoftmaxfisherproduct_kernel(tc, h, g, w_words, w_scales, v, e, rh
 
         def W(i):
             nc.vector.scalar_tensor_tensor(
-                out=row(eu, i), in0=u_bank(i)[:], scalar=ahead(shift_coef, i), in1=row(ex, i),
+                out=row(eu, i), in0=in_runs(u_bank(i)[:]), scalar=ahead(shift_coef, i), in1=row(ex, i),
                 op0=ALU.mult, op1=ALU.mult, accum_out=behind(acc_rho, i),
             )
 
@@ -267,9 +277,9 @@ def tile_dampedsoftmaxfisherproduct_kernel(tc, h, g, w_words, w_scales, v, e, rh
             G, u = divmod(j, 2)
             slots = slice(2 * u, 2 * u + 2)
             nc.gpsimd.tensor_tensor(
-                out=y_bf[G % 2][:, :, slots].rearrange("p (c i) t -> p c t i", i=4),
-                in0=ex[G % 2][:, slots, :].rearrange("p t (c i) -> p c t i", i=4),
-                in1=eu[G % 2][:, slots, :].rearrange("p t (c i) -> p c t i", i=4),
+                out=y_bf[G % 2][:, :, slots].rearrange("p (c i) t -> p c t i", i=RUN),
+                in0=pair_of(ex, j),
+                in1=pair_of(eu, j),
                 op=ALU.subtract,
             )
 

@@ -232,12 +232,15 @@ def tile_dampedsoftmaxfisherproduct_kernel(tc, h, g, w_words, w_scales, v, e, rh
             G, u = divmod(j, 2)
             return tiles[G % 2][:, 2 * u : 2 * u + 2, :].rearrange("p e a -> p (e a)").rearrange("p (c e i) -> p c e i", e=2, i=RUN)
 
+        def group_of(tiles, G):
+            return tiles[G % 2][:].rearrange("p t a -> p (t a)").rearrange("p (c t i) -> p c t i", t=PACK, i=RUN)
+
         def in_runs(ap):
             return ap.rearrange("p (c i) -> p c i", i=RUN)
 
         def row(tiles, i):
             if i // PACK == GROUPS - 1:
-                return in_runs(tiles[(i // PACK) % 2][:, i % PACK, :])
+                return group_of(tiles, i // PACK)[:, :, i % PACK, :]
             return pair_of(tiles, i // 2)[:, :, i % 2, :]
 
         def EXP(i):
@@ -285,9 +288,9 @@ def tile_dampedsoftmaxfisherproduct_kernel(tc, h, g, w_words, w_scales, v, e, rh
 
         def YV(G, a0, a1):
             nc.vector.tensor_tensor(
-                out=y_bf[G % 2][:, a0:a1, :].rearrange("p (c i) t -> p c t i", i=2),
-                in0=ex[G % 2][:, :, a0:a1].rearrange("p t (c i) -> p c t i", i=2),
-                in1=eu[G % 2][:, :, a0:a1].rearrange("p t (c i) -> p c t i", i=2),
+                out=y_bf[G % 2][:, a0:a1, :].rearrange("p (c i) t -> p c t i", i=RUN),
+                in0=group_of(ex, G)[:, a0 // RUN : a1 // RUN, :, :],
+                in1=group_of(eu, G)[:, a0 // RUN : a1 // RUN, :, :],
                 op=ALU.subtract,
             )
 
@@ -468,6 +471,7 @@ def tile_dampedsoftmaxfisherproduct_kernel(tc, h, g, w_words, w_scales, v, e, rh
         B(0)
         HE(1, 1, 2, PACK)
         E2(0)
+        LV(2, False)
         Q(0, 0, 2)
         E2P(1)
         YP(0)
@@ -556,15 +560,15 @@ def tile_dampedsoftmaxfisherproduct_kernel(tc, h, g, w_words, w_scales, v, e, rh
         QH(HE_ITEMS - 2)
         for b in range(2):
             HE(HE_ITEMS - 1, b)
-        for c in range(2, 2 * PACK):
+        for c in range(3, 2 * PACK):
             LV(c, False)
         for b in range(4):
             K(b, GROUPS - 1)
         K(4, 2)
         K(5, 2)
         EP(0)
-        QH(HE_ITEMS - 1)
         EP(1)
+        QH(HE_ITEMS - 1)
         OI(0, 0, False, 0, HALF_A)
         for G in range(GROUPS - 1):
             K(6, G)
@@ -586,7 +590,6 @@ def tile_dampedsoftmaxfisherproduct_kernel(tc, h, g, w_words, w_scales, v, e, rh
         OI(1, 1, False, 160, HALF_A)
         OI(1, 1, True, 0, 160)
         QO(1, 0)
-        store_words(1, 0, HALF_A)
         QO(1, 1)
-        store_words(1, HALF_A, A)
+        store_words(1, 0, A)
         store_scales()

@@ -218,6 +218,9 @@ def tile_dampedsoftmaxfisherproduct_kernel(tc, h, g, w_words, w_scales, v, e, rh
         def QV(gh):
             nc.vector.quantize_mx(out=v_codes[:, gh, :].bitcast(FP8X4), scales=v_plane[:, gh, :], in_=flat(v_bf[gh]))
 
+        def DV(i):
+            DIAG(i, False)
+
         def LV(c, pool):
             gh, s = divmod(c, PACK)
             if pool:
@@ -364,11 +367,11 @@ def tile_dampedsoftmaxfisherproduct_kernel(tc, h, g, w_words, w_scales, v, e, rh
             nc.sync.dma_start(out=words[:, a0:a1], in_=o_codes[:, gh, a0:a1].bitcast(I32))
 
         def store_scales():
-            for q in range(4):
-                eng = nc.scalar if q < 2 else nc.sync
+            for r in range(4):
+                eng = nc.scalar if r < 2 else nc.sync
                 eng.dma_start(
-                    out=out_2[:, 4 * q : 4 * q + 4, :].rearrange("g q a -> q g a").bitcast(I32),
-                    in_=o_plane[32 * q : 32 * q + 4, :, :].bitcast(I32),
+                    out=out_2.rearrange("g (q r) a -> r q g a", r=4)[r].bitcast(I32),
+                    in_=o_plane[r:P:32, :, :].bitcast(I32),
                 )
 
         def first(j):
@@ -393,7 +396,6 @@ def tile_dampedsoftmaxfisherproduct_kernel(tc, h, g, w_words, w_scales, v, e, rh
         ctx.enter_context(tc.manual_schedule())
 
         nc.vector.memset(zeros[:].bitcast(U32), 0)
-        nc.vector.memset(w_plane[:].rearrange("p g a -> p (g a)").bitcast(U32), 0)
         make_identity(nc, ident[:])
         load_h(0, 1)
         load_vec(nc.scalar, g_sb, g)
@@ -401,16 +403,15 @@ def tile_dampedsoftmaxfisherproduct_kernel(tc, h, g, w_words, w_scales, v, e, rh
         load_h(1, 2)
         load_h(2, 4)
         nc.sync.dma_start(out=w_codes[:].bitcast(I32), in_=w_words.rearrange("g p n -> p g n").bitcast(I32))
-        for q in range(4):
-            nc.sync.dma_start(
-                out=w_plane[32 * q : 32 * q + 4, :, :].bitcast(I32),
-                in_=w_scales[:, 4 * q : 4 * q + 4, :].rearrange("g q a -> q g a").bitcast(I32),
-            )
         load_v(0)
+        for r in range(0, 4):
+            nc.sync.dma_start(
+                out=w_plane[r:P:32, :, :].bitcast(I32),
+                in_=w_scales.rearrange("g (q r) a -> r q g a", r=4)[r].bitcast(I32),
+            )
         load_v(1)
         load_h(4, 6)
         load_h(6, 8)
-
         load_vec(nc.sync, lam_sb, lam)
         load_vec(nc.sync, rho_sb, rho)
         for j in range(4, PAIRS):
@@ -424,18 +425,15 @@ def tile_dampedsoftmaxfisherproduct_kernel(tc, h, g, w_words, w_scales, v, e, rh
         F(0)
         VE()
         F(1)
-        for G in (0, GROUPS - 1):
-            for t in range(PACK):
-                DIAG(PACK * G + t, True)
+        for i in range(TILES - PACK):
+            DIAG(i, True)
         both(T, 1)
-        for i in range(PACK, 2 * PACK):
-            DIAG(i, False)
+        both(DV, 6)
         QF(0)
         DG(0, 0)
         both(Z, 0)
         both(F, 1)
-        for i in range(2 * PACK, 3 * PACK):
-            DIAG(i, False)
+        both(DV, 7)
         QF(1)
         both(Z, 1)
         HE(0, 0)

@@ -120,6 +120,9 @@ def tile_dampedsoftmaxfisherproduct_kernel(tc, h, g, w_words, w_scales, v, e, rh
         def u_bank(i):
             return (z_banks if i // 2 == LAST else u_banks)[i % 2]
 
+        def d_bank(k, b):
+            return z_banks[0] if (k, b) == (1, 1) else d_banks[b]
+
         def k_bank(c):
             return (t_banks + u_banks + z_banks + d_banks)[c]
 
@@ -198,7 +201,7 @@ def tile_dampedsoftmaxfisherproduct_kernel(tc, h, g, w_words, w_scales, v, e, rh
         def DG(k, b):
             gh, G = divmod(k, GROUPS)
             d0 = gh * K_PASS + b * HE_COLS
-            bank = d_banks[b][:].bitcast(BF16)
+            bank = d_bank(k, b)[:].bitcast(BF16)
             for t in range(PACK):
                 nc.tensor.matmul(
                     out=bank[:, t * HE_COLS : (t + 1) * HE_COLS],
@@ -212,7 +215,7 @@ def tile_dampedsoftmaxfisherproduct_kernel(tc, h, g, w_words, w_scales, v, e, rh
             m = HE_COLS // PACK
             nc.scalar.copy(
                 out=stage[k % STAGE_BUFS][:, 0, :].rearrange("p (s m t) -> p s m t", s=PACK, t=PACK)[:, s0:s1, m * b : m * (b + 1), :],
-                in_=d_banks[b][:].bitcast(BF16).rearrange("p (t m s) -> p s m t", t=PACK, s=PACK)[:, s0:s1, :, :],
+                in_=d_bank(k, b)[:].bitcast(BF16).rearrange("p (t m s) -> p s m t", t=PACK, s=PACK)[:, s0:s1, :, :],
             )
 
         def QV(gh):
@@ -399,16 +402,21 @@ def tile_dampedsoftmaxfisherproduct_kernel(tc, h, g, w_words, w_scales, v, e, rh
         make_identity(nc, ident[:])
         load_h(0, 1)
         load_vec(nc.scalar, g_sb, g)
-        load_vec(nc.scalar, e_sb, e)
         load_h(1, 2)
         load_h(2, 4)
         nc.sync.dma_start(out=w_codes[:].bitcast(I32), in_=w_words.rearrange("g p n -> p g n").bitcast(I32))
-        load_v(0)
-        for r in range(0, 4):
+        for r in range(0, 2):
             nc.sync.dma_start(
                 out=w_plane[r:P:32, :, :].bitcast(I32),
                 in_=w_scales.rearrange("g (q r) a -> r q g a", r=4)[r].bitcast(I32),
             )
+        load_vec(nc.scalar, e_sb, e)
+        for r in range(2, 4):
+            nc.sync.dma_start(
+                out=w_plane[r:P:32, :, :].bitcast(I32),
+                in_=w_scales.rearrange("g (q r) a -> r q g a", r=4)[r].bitcast(I32),
+            )
+        load_v(0)
         load_v(1)
         load_h(4, 6)
         load_h(6, 8)
@@ -432,6 +440,7 @@ def tile_dampedsoftmaxfisherproduct_kernel(tc, h, g, w_words, w_scales, v, e, rh
         QF(0)
         DG(0, 0)
         both(Z, 0)
+        DG(0, 1)
         both(F, 1)
         both(DV, 7)
         QF(1)
@@ -440,7 +449,6 @@ def tile_dampedsoftmaxfisherproduct_kernel(tc, h, g, w_words, w_scales, v, e, rh
         VI(0, False, 0, A)
         VI(1, True, 0, A)
         both(T, 2)
-        DG(0, 1)
 
         for j in range(2):
             both(MAX, j)
@@ -448,6 +456,7 @@ def tile_dampedsoftmaxfisherproduct_kernel(tc, h, g, w_words, w_scales, v, e, rh
         both(F, 2)
         DG(1, 0)
         fill(T, 3)
+        DG(1, 1)
         QV(1)
         QV(0)
         QF(2)
@@ -459,15 +468,14 @@ def tile_dampedsoftmaxfisherproduct_kernel(tc, h, g, w_words, w_scales, v, e, rh
         for c in range(2):
             LV(c, True)
         HE(0, 1)
-        HE(1, 0)
-        DG(1, 1)
+        HE(1, 1)
         fill(Z, 2)
         use(F, 3)
         both(W, 0)
         fill(U, 1)
-        HE(1, 1, 0, 2)
+        HE(1, 0, 0, 2)
         B(0)
-        HE(1, 1, 2, PACK)
+        HE(1, 0, 2, PACK)
         E2(0)
         LV(2, False)
         Q(0, 0, 2)
@@ -496,7 +504,11 @@ def tile_dampedsoftmaxfisherproduct_kernel(tc, h, g, w_words, w_scales, v, e, rh
             if j >= 3:
                 G, half = divmod(j - 3, 2)
                 QY(G, half * HALF_A, (half + 1) * HALF_A if j < PAIRS - 3 else A)
-                Q(j - 1, 0, 2)
+                if j < PAIRS - 3:
+                    Q(j - 1, 0, 2)
+                else:
+                    QF(j + 2)
+                    QH(j - 1)
             else:
                 QH(j - 1)
                 QF(j + 2)

import math
from contextlib import ExitStack

import concourse.mybir as mybir
from concourse.masks import make_identity

N, D, A = 2048, 1024, 512
FLOPS = 3 * 2 * N * D * A

F32 = mybir.dt.float32
BF16 = mybir.dt.bfloat16
I32 = mybir.dt.int32
U32 = mybir.dt.uint32
U8 = mybir.dt.uint8
FP8X4 = mybir.dt.float8_e4m3fn_x4
FP4X4 = mybir.dt.float4_e2m1fn_x4
ALU = mybir.AluOpType
ACT = mybir.ActivationFunctionType

P = 128
PACK = 4
K_PASS = P * PACK
GROUPS = N // K_PASS
HALVES = D // K_PASS
TILES = GROUPS * PACK
PAIRS = TILES // 2
LAST = PAIRS - 1
HE_COLS = 256
HE_ITEMS = GROUPS * HALVES
STAGE_BUFS = 3
F_LEAD = 3
HALF_A = A // 2
RUN = 4


def tile_dampedsoftmaxfisherproduct_kernel(tc, h, g, w_words, w_scales, v, e, rho, lam, out_0, out_1, out_2):
    nc = tc.nc
    with ExitStack() as ctx:
        sb = ctx.enter_context(tc.tile_pool(name="sb", bufs=1))
        ps = ctx.enter_context(tc.psum_pool(name="ps", bufs=1))

        def tile(name, shape, dtype):
            return sb.tile(shape, dtype, name=name, align_bytes=64)

        banks = [ps.tile([P, 512], F32, name="bank%d" % b) for b in range(8)]
        t_banks = banks[0:2]
        z_banks = banks[2:4]
        u_banks = banks[4:6]
        d_banks = banks[6:8]

        ident = tile("ident", [P, P], F32)
        zeros = tile("zeros", [P, K_PASS], BF16)
        g_sb = tile("g_sb", [P, HALVES, PACK], BF16)
        e_sb = tile("e_sb", [P, GROUPS, PACK], BF16)
        rho_sb = tile("rho_sb", [P, GROUPS, PACK], BF16)
        lam_sb = tile("lam_sb", [P, HALVES, PACK], BF16)
        lam32 = tile("lam32", [P, HALVES * PACK], F32)
        e32 = tile("e32", [P, TILES], F32)
        diag = [tile("diag%d" % G, [P, PACK, P], BF16) for G in range(GROUPS)]
        h_sb = [tile("h%d" % j, [P, 2, D], BF16) for j in range(PAIRS)]
        v_sb = [tile("v%d" % gh, [P, PACK, A], BF16) for gh in range(HALVES)]
        w_codes = tile("w_codes", [P, HALVES, 2 * A], U8)
        w_plane = tile("w_plane", [P, HALVES, A], U8)
        v_codes = tile("v_codes", [P, HALVES, A], U32)
        v_plane = tile("v_plane", [P, HALVES, A], U8)
        stage = [tile("stage%d" % b, [P, 2, K_PASS * PACK], BF16) for b in range(STAGE_BUFS)]
        codes = tile("codes", [P, PAIRS, 2, K_PASS], U32)
        plane = tile("plane", [P, PAIRS, 2, K_PASS], U8)
        ex = [tile("ex%d" % b, [P, PACK, A], F32) for b in range(2)]
        eu = [tile("eu%d" % b, [P, PACK, A], F32) for b in range(2)]
        y_bf = [tile("y_bf%d" % b, [P, A, PACK], BF16) for b in range(2)]
        y_codes = tile("y_codes", [P, GROUPS, A], U32)
        y_plane = tile("y_plane", [P, GROUPS, A], U8)
        res = [tile("res%d" % gh, [P, 2, PACK, HALF_A], F32) for gh in range(HALVES)]
        wide_bf = [tile("wide_bf%d" % b, [P, A, PACK], BF16) for b in range(2)]
        o_codes = tile("o_codes", [P, HALVES, A], U32)
        o_plane = tile("o_plane", [P, HALVES, A], U8)
        neg_max = tile("neg_max", [P, TILES], F32)
        total = tile("total", [P, TILES], F32)
        inv = tile("inv", [P, TILES], F32)
        acc_rho = tile("acc_rho", [P, PAIRS + 1, 2, 2], F32)
        shift_coef = tile("shift_coef", [P, PAIRS + 1, 2, 2], F32)

        def f_unit(j):
            return (j - F_LEAD) % PAIRS

        def f_cols(t, i, gh):
            c0 = (i % 2 * HALVES + gh) * P
            return t[:, f_unit(i // 2), 1, c0 : c0 + P]

        def as_words(t):
            return t.rearrange("p s a -> p (s a)").bitcast(BF16).rearrange("p (a t) -> p a t", t=PACK)

        v_bf = [as_words(res[0][:, 0, :, :]), stage[f_unit(1) % STAGE_BUFS][:, 1, :].rearrange("p (a t) -> p a t", t=PACK)]

        def res_row(c):
            return res[c // PACK][:, :, c % PACK, :]

        def col(t, i):
            return t[:, i : i + 1]

        def behind(t, i):
            return t[:, i // 2 + 1, 0, i % 2 : i % 2 + 1]

        def ahead(t, i):
            return t[:, i // 2, 1, i % 2 : i % 2 + 1]

        def flat(ap):
            return ap.rearrange("p a t -> p (a t)")

        def h_row(i):
            return h_sb[i // 2][:, i % 2, :]

        def t_bank(i):
            return (u_banks if i // 2 == 1 else t_banks)[i % 2]

        def z_bank(i):
            return {1: u_banks, LAST: t_banks}.get(i // 2, z_banks)[i % 2]

        def u_bank(i):
            return (z_banks if i // 2 == LAST else u_banks)[i % 2]

        def d_bank(k, b):
            return z_banks[0] if (k, b) == (1, 1) else d_banks[b]

        def k_bank(c):
            return (t_banks + u_banks + z_banks + d_banks)[c]

        def load_h(i0, i1):
            G, t0 = divmod(i0, PACK)
            rows = h[G * K_PASS : (G + 1) * K_PASS, :].rearrange("(p t) d -> p t d", t=PACK)
            nc.sync.dma_start(out=h_sb[i0 // 2][:, i0 % 2 : i0 % 2 + i1 - i0, :], in_=rows[:, t0 : t0 + i1 - i0, :])

        def load_v(gh):
            rows = v[gh * K_PASS : (gh + 1) * K_PASS, :].rearrange("(p t) a -> p t a", t=PACK)
            nc.sync.dma_start(out=v_sb[gh][:], in_=rows)

        def load_vec(eng, dst, src):
            eng.dma_start(out=dst[:], in_=src.rearrange("(c p t) -> p c t", p=P, t=PACK))

        def warm_up(count):
            for n in range(count):
                nc.tensor.matmul(out=d_banks[1][:], lhsT=zeros[:, :P], rhs=zeros[:], start=True, stop=True)

        def VE():
            nc.vector.tensor_copy(out=e32[:], in_=flat(e_sb[:]))

        def VL():
            nc.scalar.activation(out=lam32[:], in_=flat(lam_sb[:]), func=ACT.Copy)

        def RHO():
            nc.scalar.activation(out=acc_rho[:, :PAIRS, 1, :], in_=flat(rho_sb[:]).rearrange("p (j e) -> p j e", e=2), func=ACT.Copy, scale=-float(A))

        def T(i):
            bank = t_bank(i)
            words = h_row(i).bitcast(F32)
            for u in range(2):
                for gh in range(HALVES):
                    c0 = (2 * u + gh) * P
                    nc.tensor.transpose(bank[:, c0 : c0 + P], words[:, 256 * gh + u : 256 * (gh + 1) : 2], ident[:])

        def F(i):
            nc.vector.tensor_tensor(
                out=stage[f_unit(i // 2) % STAGE_BUFS][:, 1, i % 2 * D : (i % 2 + 1) * D].rearrange("p (g r u e) -> p g r u e", g=HALVES, u=2, e=2),
                in0=t_bank(i)[:].bitcast(BF16).rearrange("p (u g r e) -> p g r u e", u=2, g=HALVES, e=2),
                in1=g_sb[:].rearrange("p g (o u e) -> p g o u e", o=1, u=2).to_broadcast([P, HALVES, P, 2, 2]),
                op=ALU.mult,
            )

        def Q(unit, part0, part1):
            nc.vector.quantize_mx(
                out=codes[:, unit, part0:part1, :].rearrange("p h c -> p (h c)").bitcast(FP8X4),
                scales=plane[:, unit, part0:part1, :].rearrange("p h c -> p (h c)"),
                in_=stage[unit % STAGE_BUFS][:, part0:part1, :].rearrange("p h c -> p (h c)"),
            )

        def QF(j):
            Q(f_unit(j), 1, 2)

        def QH(k):
            Q(k, 0, 1)

        def stage1(i, bank, rhs_codes, rhs_plane):
            for gh in range(HALVES):
                nc.tensor.matmul_mx(
                    out=bank[:],
                    lhsT=f_cols(codes, i, gh).bitcast(FP8X4),
                    lhsT_scale=f_cols(plane, i, gh),
                    rhs=rhs_codes(gh),
                    rhs_scale=rhs_plane[:, gh, :],
                    start=(gh == 0),
                    stop=(gh == HALVES - 1),
                )

        def Z(i):
            stage1(i, z_bank(i), lambda gh: w_codes[:, gh, :].bitcast(FP4X4), w_plane)

        def U(i):
            stage1(i, u_bank(i), lambda gh: v_codes[:, gh, :].bitcast(FP8X4), v_plane)

        def DG(k, b):
            gh, G = divmod(k, GROUPS)
            d0 = gh * K_PASS + b * HE_COLS
            bank = d_bank(k, b)[:].bitcast(BF16)
            for t in range(PACK):
                nc.tensor.matmul(
                    out=bank[:, t * HE_COLS : (t + 1) * HE_COLS],
                    lhsT=diag[G][:, t, :],
                    rhs=h_row(PACK * G + t)[:, d0 : d0 + HE_COLS],
                    start=True,
                    stop=True,
                )

        def HE(k, b, s0=0, s1=PACK):
            m = HE_COLS // PACK
            nc.scalar.copy(
                out=stage[k % STAGE_BUFS][:, 0, :].rearrange("p (s m t) -> p s m t", s=PACK, t=PACK)[:, s0:s1, m * b : m * (b + 1), :],
                in_=d_bank(k, b)[:].bitcast(BF16).rearrange("p (t m s) -> p s m t", t=PACK, s=PACK)[:, s0:s1, :, :],
            )

        def QV(gh):
            nc.vector.quantize_mx(out=v_codes[:, gh, :].bitcast(FP8X4), scales=v_plane[:, gh, :], in_=flat(v_bf[gh]))

        def DV(i):
            DIAG(i, False)

        def LV(c, pool):
            gh, s = divmod(c, PACK)
            if pool:
                nc.gpsimd.tensor_scalar(out=res_row(c), in0=v_sb[gh][:, s, :].rearrange("p (h a) -> p h a", h=2), scalar1=col(lam32, c), scalar2=0.0, op0=ALU.mult, op1=ALU.add)
            else:
                nc.scalar.activation(out=res_row(c), in_=v_sb[gh][:, s, :].rearrange("p (h a) -> p h a", h=2), func=ACT.Copy, scale=col(lam32, c))

        def MAX(i):
            nc.vector.tensor_reduce(out=col(neg_max, i), in_=z_bank(i)[:], axis=mybir.AxisListType.X, op=ALU.max, negate=True)

        def pair_of(tiles, j):
            G, u = divmod(j, 2)
            return tiles[G % 2][:, 2 * u : 2 * u + 2, :].rearrange("p e a -> p (e a)").rearrange("p (c e i) -> p c e i", e=2, i=RUN)

        def group_of(tiles, G):
            return tiles[G % 2][:].rearrange("p t a -> p (t a)").rearrange("p (c t i) -> p c t i", t=PACK, i=RUN)

        def in_runs(ap):
            return ap.rearrange("p (c i) -> p c i", i=RUN)

        def row(tiles, i):
            if i // PACK == GROUPS - 1:
                return group_of(tiles, i // PACK)[:, :, i % PACK, :]
            return pair_of(tiles, i // 2)[:, :, i % 2, :]

        def EXP(i):
            nc.scalar.activation(out=row(ex, i), in_=in_runs(z_bank(i)[:]), func=ACT.Exp, bias=col(neg_max, i), accum_out=col(total, i))

        def R(i, n):
            nc.vector.reciprocal(out=inv[:, i : i + n], in_=total[:, i : i + n])

        def C(i):
            nc.scalar.activation(out=ahead(shift_coef, i), in_=col(inv, i), func=ACT.Copy, scale=ahead(acc_rho, i))

        def W(i):
            nc.vector.scalar_tensor_tensor(
                out=row(eu, i), in0=in_runs(u_bank(i)[:]), scalar=ahead(shift_coef, i), in1=row(ex, i),
                op0=ALU.mult, op1=ALU.mult, accum_out=behind(acc_rho, i),
            )

        def B(i):
            nc.scalar.activation(out=behind(shift_coef, i), in_=behind(acc_rho, i), func=ACT.Copy, scale=col(inv, i))

        def CP(j, n):
            nc.gpsimd.tensor_tensor(out=shift_coef[:, j : j + n, 1, :], in0=acc_rho[:, j : j + n, 1, :], in1=inv[:, 2 * j : 2 * (j + n)].rearrange("p (j e) -> p j e", e=2), op=ALU.mult)

        def BC(j):
            nc.gpsimd.tensor_tensor(out=flat(shift_coef[:, j, :, :]), in0=flat(acc_rho[:, j, :, :]), in1=inv[:, 2 * j - 2 : 2 * j + 2], op=ALU.mult)

        def E2P(i):
            nc.gpsimd.tensor_scalar(out=row(ex, i), in0=row(ex, i), scalar1=behind(acc_rho, i), scalar2=col(inv, i), op0=ALU.mult, op1=ALU.mult)

        def E2V(i):
            nc.vector.tensor_scalar(out=row(ex, i), in0=row(ex, i), scalar1=behind(acc_rho, i), scalar2=col(inv, i), op0=ALU.mult, op1=ALU.mult)

        def E2(i):
            nc.scalar.activation(out=row(ex, i), in_=row(ex, i), func=ACT.Copy, scale=behind(shift_coef, i))

        def YP(j):
            G, u = divmod(j, 2)
            slots = slice(2 * u, 2 * u + 2)
            nc.gpsimd.tensor_tensor(
                out=y_bf[G % 2][:, :, slots].rearrange("p (c i) t -> p c t i", i=RUN),
                in0=pair_of(ex, j),
                in1=pair_of(eu, j),
                op=ALU.subtract,
            )

        def YV(G, a0, a1):
            nc.vector.tensor_tensor(
                out=y_bf[G % 2][:, a0:a1, :].rearrange("p (c i) t -> p c t i", i=RUN),
                in0=group_of(ex, G)[:, a0 // RUN : a1 // RUN, :, :],
                in1=group_of(eu, G)[:, a0 // RUN : a1 // RUN, :, :],
                op=ALU.subtract,
            )

        def runs(dst, src, a0, a1, run):
            return (dst[:, a0:a1, :].rearrange("p (c i) t -> p c t i", i=run), src[:, :, a0:a1].rearrange("p t (c i) -> p c t i", i=run))

        def VI(gh, pool, a0, a1):
            if pool:
                nc.gpsimd.tensor_scalar(out=v_bf[gh][:, a0:a1, :], in0=v_sb[gh][:, :, a0:a1].rearrange("p t a -> p a t"), scalar1=1.0, scalar2=0.0, op0=ALU.mult, op1=ALU.add)
            else:
                out, in_ = runs(v_bf[gh], v_sb[gh], a0, a1, 4)
                nc.scalar.copy(out=out, in_=in_)

        def OI(gh, half, vec, a0, a1):
            out, in_ = runs(wide_bf[gh][:, half * HALF_A : (half + 1) * HALF_A, :], res[gh][:, half, :, :], a0, a1, 2)
            if vec:
                nc.vector.tensor_copy(out=out, in_=in_)
            else:
                nc.scalar.copy(out=out, in_=in_)

        def OP(gh, half):
            out, in_ = runs(wide_bf[gh][:, half * HALF_A : (half + 1) * HALF_A, :], res[gh][:, half, :, :], 0, HALF_A, 2)
            nc.gpsimd.tensor_scalar(out=out, in0=in_, scalar1=1.0, scalar2=0.0, op0=ALU.mult, op1=ALU.add)

        def DIAG(i, scalar):
            out = diag[i // PACK][:, i % PACK, :]
            if scalar:
                nc.scalar.activation(out=out, in_=ident[:], func=ACT.Copy, scale=col(e32, i))
            else:
                nc.vector.tensor_scalar(out=out, in0=ident[:], scalar1=col(e32, i), scalar2=None, op0=ALU.mult)

        def QY(G, a0, a1):
            nc.vector.quantize_mx(out=y_codes[:, G, a0:a1].bitcast(FP8X4), scales=y_plane[:, G, a0:a1], in_=flat(y_bf[G % 2][:, a0:a1, :]))

        def K(b, G):
            gh, half, pair = b // 4, b // 2 % 2, b % 2
            k = gh * GROUPS + G
            cols = slice(half * HALF_A, (half + 1) * HALF_A)
            for e in range(2):
                s = 2 * pair + e
                nc.tensor.matmul_mx(
                    out=k_bank(b)[:, e * HALF_A : (e + 1) * HALF_A],
                    lhsT=codes[:, k, 0, s * P : (s + 1) * P].bitcast(FP8X4),
                    lhsT_scale=plane[:, k, 0, s * P : (s + 1) * P],
                    rhs=y_codes[:, G, cols].bitcast(FP8X4),
                    rhs_scale=y_plane[:, G, cols],
                    start=(G == 0 and e == 0),
                    stop=(G == GROUPS - 1 and e == 1),
                )

        def EP(b):
            gh, half, pair = b // 4, b // 2 % 2, b % 2
            part = res[gh][:, half, 2 * pair : 2 * pair + 2, :].rearrange("p e a -> p (e a)")
            nc.vector.scalar_tensor_tensor(
                out=part, in0=k_bank(b)[:], scalar=1.0 / math.sqrt(N), in1=part,
                op0=ALU.mult, op1=ALU.add,
            )
            ST(b)

        def ST(b):
            gh, half, pair = b // 4, b // 2 % 2, b % 2
            rows = out_0[gh * K_PASS : (gh + 1) * K_PASS, :].rearrange("(p t) a -> p t a", t=PACK)
            nc.sync.dma_start(out=rows[:, 2 * pair : 2 * pair + 2, half * HALF_A : (half + 1) * HALF_A], in_=res[gh][:, half, 2 * pair : 2 * pair + 2, :])

        def QO(gh, half):
            cols = slice(half * HALF_A, (half + 1) * HALF_A)
            nc.vector.quantize_mx(out=o_codes[:, gh, cols].bitcast(FP8X4), scales=o_plane[:, gh, cols], in_=flat(wide_bf[gh][:, cols, :]))

        def store_words(gh, a0, a1):
            words = out_1[gh].rearrange("p m t -> p (m t)").bitcast(I32)
            nc.sync.dma_start(out=words[:, a0:a1], in_=o_codes[:, gh, a0:a1].bitcast(I32))

        def store_scales():
            for r in range(4):
                eng = nc.scalar if r < 2 else nc.sync
                eng.dma_start(
                    out=out_2.rearrange("g (q r) a -> r q g a", r=4)[r].bitcast(I32),
                    in_=o_plane[r:P:32, :, :].bitcast(I32),
                )

        def first(j):
            return 2 * j + j % 2

        def second(j):
            return 2 * j + 1 - j % 2

        def use(step, j):
            step(first(j))
            step(second(j))

        def fill(step, j):
            step(second(j))
            step(first(j))

        def both(step, j):
            if 0 <= j < PAIRS:
                step(2 * j)
                step(2 * j + 1)

        ctx.enter_context(tc.manual_schedule())

        nc.vector.memset(zeros[:].bitcast(U32), 0)
        make_identity(nc, ident[:])
        load_h(0, 1)
        load_vec(nc.scalar, g_sb, g)
        load_h(1, 2)
        load_h(2, 4)
        nc.sync.dma_start(out=w_codes[:].bitcast(I32), in_=w_words.rearrange("g p n -> p g n").bitcast(I32))
        for r in range(0, 2):
            nc.sync.dma_start(
                out=w_plane[r:P:32, :, :].bitcast(I32),
                in_=w_scales.rearrange("g (q r) a -> r q g a", r=4)[r].bitcast(I32),
            )
        load_vec(nc.scalar, e_sb, e)
        for r in range(2, 4):
            nc.sync.dma_start(
                out=w_plane[r:P:32, :, :].bitcast(I32),
                in_=w_scales.rearrange("g (q r) a -> r q g a", r=4)[r].bitcast(I32),
            )
        load_v(0)
        load_v(1)
        load_h(4, 6)
        load_h(6, 8)
        load_vec(nc.sync, lam_sb, lam)
        load_vec(nc.sync, rho_sb, rho)
        for j in range(4, PAIRS):
            load_h(2 * j, 2 * j + 2)

        warm_up(3)
        T(0)
        warm_up(1)
        T(1)
        warm_up(1)
        F(0)
        VE()
        F(1)
        for i in range(TILES - PACK):
            DIAG(i, True)
        both(T, 1)
        both(DV, 6)
        QF(0)
        DG(0, 0)
        both(Z, 0)
        DG(0, 1)
        both(F, 1)
        both(DV, 7)
        QF(1)
        both(Z, 1)
        HE(0, 0)
        VI(0, False, 0, A)
        VI(1, True, 0, A)
        both(T, 2)

        for j in range(2):
            both(MAX, j)
            both(EXP, j)
        both(F, 2)
        DG(1, 0)
        fill(T, 3)
        DG(1, 1)
        QV(1)
        QV(0)
        QF(2)
        RHO()
        VL()
        R(0, 4)
        CP(0, 2)
        both(U, 0)
        for c in range(2):
            LV(c, True)
        HE(0, 1)
        HE(1, 1)
        fill(Z, 2)
        use(F, 3)
        both(W, 0)
        fill(U, 1)
        HE(1, 0, 0, 2)
        B(0)
        HE(1, 0, 2, PACK)
        E2(0)
        LV(2, False)
        Q(0, 0, 2)
        E2P(1)
        YP(0)
        DG(2, 0)
        fill(T, 4)
        DG(2, 1)

        for j in range(2, PAIRS - 2):
            use(MAX, j)
            use(EXP, j)
            fill(Z, j + 1)
            use(W, j - 1)
            fill(U, j)
            R(2 * j, 2)
            use(F, j + 2)
            if j > 2:
                BC(j)
            HE(j, 0)
            if j == 2:
                use(B, j - 1)
            HE(j, 1, 0, 2)
            use(E2, j - 1)
            HE(j, 1, 2, PACK)
            if j >= 3:
                G, half = divmod(j - 3, 2)
                QY(G, half * HALF_A, (half + 1) * HALF_A if j < PAIRS - 3 else A)
                if j < PAIRS - 3:
                    Q(j - 1, 0, 2)
                else:
                    QF(j + 2)
                    QH(j - 1)
            else:
                QH(j - 1)
                QF(j + 2)
                CP(j, 1)
            YP(j - 1)
            DG(j + 1, 0)
            if j + 3 < PAIRS:
                fill(T, j + 3)
            if j < PAIRS - 3:
                DG(j + 1, 1)

        j = LAST - 1
        HE(HE_ITEMS - 2, 0, 0, 2)
        use(MAX, j)
        use(EXP, j)
        both(Z, LAST)
        DG(HE_ITEMS - 2, 1)
        use(W, j - 1)
        fill(U, j)
        both(U, LAST)
        R(2 * j, 2)
        both(MAX, LAST)
        B(first(j - 1))
        E2P(second(j - 1))
        E2(first(j - 1))
        fill(C, j)
        YP(j - 1)
        both(EXP, LAST)
        for i in range(2 * j, TILES):
            W(i)
            if i + 2 < TILES:
                R(i + 2, 1)
                C(i + 2)
            if i < TILES - 1:
                B(i)
            if i > 2 * j:
                E2(i - 1)
            else:
                HE(HE_ITEMS - 2, 0, 2, PACK)
        for b in range(0, 4, 2):
            for G in range(2):
                K(b, G)
                K(b + 1, G)
        DG(HE_ITEMS - 1, 0)
        QH(HE_ITEMS - 3)
        E2V(TILES - 1)
        QY(GROUPS - 2, 0, A)
        for G in range(2):
            K(4, G)
            K(5, G)
        HE(HE_ITEMS - 2, 1)
        DG(HE_ITEMS - 1, 1)
        for b in range(4):
            K(b, GROUPS - 2)
        YV(GROUPS - 1, 0, HALF_A)
        YV(GROUPS - 1, HALF_A, A)
        QY(GROUPS - 1, 0, HALF_A)
        QY(GROUPS - 1, HALF_A, A)
        QH(HE_ITEMS - 2)
        for b in range(2):
            HE(HE_ITEMS - 1, b)
        for c in range(3, 2 * PACK):
            LV(c, False)
        for b in range(4):
            K(b, GROUPS - 1)
        K(4, 2)
        K(5, 2)
        EP(0)
        EP(1)
        QH(HE_ITEMS - 1)
        OI(0, 0, False, 0, HALF_A)
        for G in range(GROUPS - 1):
            K(6, G)
        for b in range(4, 7):
            K(b, GROUPS - 1)
        for G in range(GROUPS):
            K(7, G)
        EP(2)
        EP(3)
        OP(0, 1)
        EP(4)
        EP(5)
        OI(1, 0, False, 0, HALF_A)
        EP(6)
        EP(7)
        QO(0, 0)
        QO(0, 1)
        store_words(0, 0, A)
        OI(1, 1, False, 160, HALF_A)
        OI(1, 1, True, 0, 160)
        QO(1, 0)
        QO(1, 1)
        store_words(1, 0, A)
        store_scales()
